import numpy as np
import ml_dtypes


def mxq(x, axis, fmt="e4m3"):
    dtype, down = {"e4m3": (ml_dtypes.float8_e4m3fn, 7), "e5m2": (ml_dtypes.float8_e5m2, 14)}[fmt]
    v = np.moveaxis(np.asarray(x, np.float32).astype(ml_dtypes.bfloat16).astype(np.float64), axis, -1)
    blocks = v.reshape(v.shape[:-1] + (-1, 32))
    amax = np.abs(blocks).max(-1, keepdims=True)
    byte = np.maximum(np.where(amax > 0, np.frexp(amax)[1] - 1 + 127, 0) - down, 1)
    scale = np.exp2(byte - 127.0)
    codes = (blocks / scale).astype(np.float32).astype(dtype).astype(np.float64)
    return np.moveaxis((codes * scale).reshape(v.shape), -1, axis)


WIDE = False


def mx_kscale(k):
    if not WIDE:
        return np.ones(k)
    levels = np.array([18, -18])
    if k % 512:
        return np.exp2(np.random.permutation(np.resize(levels, k // 32))).repeat(32)
    a = np.empty((k // 512, 16))
    for p in range(k // 512):
        a[p, :8] = np.random.permutation(np.resize(levels, 8))
        for g in range(8):
            far = levels[np.abs(levels - a[p, g]) >= 10]
            a[p, g + 8] = far[np.random.randint(len(far))]
    return np.exp2(a.ravel()).repeat(32)


def f64(x):
    return np.asarray(x).astype(np.float64)


def striped(idx):
    return np.tile(np.asarray(idx).reshape(-1, 16).T, (8, 1)).astype(np.uint16)


def unstriped(offs):
    return offs[:16].T.reshape(-1).astype(np.int64)


N, T, D, V = 512, 2048, 512, 1024


def setup_inputs():
    n = np.random.standard_normal
    idx = np.random.permutation(T)[:N]
    s = mx_kscale(D)[:, None]
    z = mx_kscale(V)[:, None]
    w = n((D, V)) / np.sqrt(D)
    return {
        "xT": (n((D, T)) / s).astype(np.float32),
        "wd": (w * s).astype(np.float32),
        "wv": (w.T / z).astype(np.float32),
        "y": np.random.randint(0, 2, (V, N)).astype(np.float32),
        "cw": (np.random.uniform(0.5, 1.5, (V, 1)) / np.sqrt(V) * z).astype(np.float32),
        "rw": np.tile(np.random.uniform(0.5, 1.5, N), (128, 1)).astype(np.float32),
        "offs": striped(idx),
    }


def reference(xT, wd, wv, y, cw, rw, offs):
    idx = unstriped(offs)
    a = mxq(f64(wd), 0, "e4m3").T @ mxq(f64(xT)[:, idx], 0, "e4m3")
    g = f64(cw) * f64(rw)[:1] * (1.0 / (1.0 + np.exp(-a)) - f64(y))
    dx = mxq(f64(wv), 0, "e4m3").T @ mxq(g, 0, "e5m2")
    gx = np.zeros((D, T))
    gx[:, idx] = dx
    return gx

@@ -1,0 +1,147 @@
+from contextlib import ExitStack
+
+import concourse.mybir as mybir
+from concourse.masks import make_identity
+
+N, T, D, V = 512, 2048, 512, 1024
+FLOPS = 2 * 2 * N * D * V
+
+F32 = mybir.dt.float32
+BF16 = mybir.dt.bfloat16
+U32 = mybir.dt.uint32
+U16 = mybir.dt.uint16
+U8 = mybir.dt.uint8
+E4M3 = mybir.dt.float8_e4m3fn_x4
+E5M2 = mybir.dt.float8_e5m2_x4
+ACT = mybir.ActivationFunctionType
+ALU = mybir.AluOpType
+
+P = 128
+PACK = 4
+PASS = P * PACK
+V_PASSES = V // PASS
+D_TILES = D // P
+LINE = 4
+WD_VECTOR_COLUMNS = 80
+
+
+def tile_attend_gml_nce_kernel(tc, xT, wd, wv, y, cw, rw, offs, out):
+    nc = tc.nc
+    with ExitStack() as ctx:
+        sb = ctx.enter_context(tc.tile_pool(name="sb", bufs=1))
+        psum = ctx.enter_context(tc.psum_pool(name="psum", bufs=8))
+
+        def bank(name):
+            return psum.tile([P, N], F32, name=name, tag="bank")
+
+        offsets = sb.tile([P, N // 16], U16, name="offsets")
+        x_planes = [sb.tile([P, T], F32, name="x_plane%d" % j) for j in range(PACK)]
+        wd_raw = [sb.tile([P, PACK, PASS], F32, name="wd_raw%d" % h) for h in range(V_PASSES)]
+        wv_raw = [sb.tile([P, PACK, D], F32, name="wv_raw%d" % h) for h in range(V_PASSES)]
+        y_sb = [sb.tile([P, PACK, N], F32, name="y_sb%d" % h) for h in range(V_PASSES)]
+        cw_sb = sb.tile([P, V_PASSES, PACK], F32, name="cw_sb")
+        rw_sb = sb.tile([P, LINE], F32, name="rw_sb")
+
+        x_rows = xT.rearrange("(p j) n -> j p n", j=PACK)
+        wd_rows = wd.rearrange("(p j) v -> p j v", j=PACK)
+        wv_rows = wv.rearrange("(h p j) d -> h p j d", p=P, j=PACK)
+        y_rows = y.rearrange("(h p j) n -> h p j n", p=P, j=PACK)
+
+        nc.sync.dma_start(x_planes[0][:], x_rows[0])
+        nc.sync.dma_start(offsets[:], offs)
+        nc.scalar.dma_start(rw_sb[:], rw[0:1, :].rearrange("o (c i) -> (o c) i", i=LINE))
+        nc.scalar.dma_start(cw_sb[:], cw.rearrange("(h p j) o -> p h (j o)", p=P, j=PACK))
+        for j in range(1, PACK):
+            nc.sync.dma_start(x_planes[j][:], x_rows[j])
+        nc.sync.dma_start(wd_raw[0][:], wd_rows[:, :, 0:PASS])
+        nc.sync.dma_start(y_sb[0][:, 0:2, :], y_rows[0][:, 0:2, :])
+        nc.sync.dma_start(y_sb[0][:, 2:4, :], y_rows[0][:, 2:4, :])
+        nc.sync.dma_start(wd_raw[1][:], wd_rows[:, :, PASS:V])
+        nc.sync.dma_start(y_sb[1][:], y_rows[1])
+        for h in range(V_PASSES):
+            nc.sync.dma_start(wv_raw[h][:], wv_rows[h])
+
+        warm = sb.tile([P, 1], F32, name="warm")
+        warm_out = sb.tile([P, 1], F32, name="warm_out")
+        nc.vector.memset(warm[:], 0.0)
+        nc.scalar.activation(warm_out[:], warm[:], ACT.Sigmoid)
+
+        ident = sb.tile([P, P], F32, name="ident")
+        make_identity(nc, ident[:])
+        rw_bank = bank("rw_bank")
+        for i in range(LINE):
+            nc.tensor.transpose(rw_bank[:, i * P:(i + 1) * P], rw_sb[:, i:i + 1].to_broadcast([P, P]), ident[:])
+        weight = [sb.tile([P, N // LINE, PACK, LINE], F32, name="weight%d" % h) for h in range(V_PASSES)]
+        for h in range(V_PASSES):
+            for j in range(PACK):
+                nc.scalar.activation(weight[h][:, :, j, :], rw_bank[:].rearrange("p (i c) -> p c i", i=LINE),
+                                     ACT.Copy, scale=cw_sb[:, h, j:j + 1])
+
+        windows = [sb.tile([P, T], F32, name="window%d" % b) for b in range(D_TILES)]
+        for b in range(D_TILES):
+            nc.vector.memset(windows[b][:], 0.0)
+
+        x_bf = sb.tile([P, N, PACK], BF16, name="x_bf", align_bytes=64)
+        x_codes = sb.tile([P, N], U32, name="x_codes", align_bytes=64)
+        x_scales = sb.tile([P, N], U8, name="x_scales", align_bytes=64)
+        for j in range(PACK):
+            nc.vector.tensor_copy(x_bf[:, :, j], x_planes[j][:].indirect(offsets[:]))
+        nc.vector.quantize_mx(out=x_codes[:].bitcast(E4M3), scales=x_scales[:],
+                              in_=x_bf[:].rearrange("p n j -> p (n j)"))
+
+        g_codes = sb.tile([P, V_PASSES, N], U32, name="g_codes", align_bytes=64)
+        g_scales = sb.tile([P, V_PASSES, N], U8, name="g_scales", align_bytes=64)
+        for h in range(V_PASSES):
+            wd_bf = sb.tile([P, PACK, P, PACK], BF16, name="wd_bf%d" % h, align_bytes=64)
+            wd_codes = sb.tile([P, PACK, P], U32, name="wd_codes%d" % h, align_bytes=64)
+            wd_scales = sb.tile([P, PACK, P], U8, name="wd_scales%d" % h, align_bytes=64)
+            src = wd_raw[h][:].rearrange("p j (m t) -> p m j t", t=PACK)
+            dst = wd_bf[:].rearrange("p t m j -> p m j t")
+            split = WD_VECTOR_COLUMNS if h == 0 else 0
+            if split:
+                nc.vector.tensor_copy(dst[:, 0:split], src[:, 0:split])
+            nc.scalar.copy(dst[:, split:P], src[:, split:P])
+
+            sig = sb.tile([P, PACK, N], F32, name="sig%d" % h)
+            diff = sb.tile([P, PACK, N], F32, name="diff%d" % h)
+            for t in range(PACK):
+                nc.vector.quantize_mx(out=wd_codes[:, t, :].bitcast(E4M3), scales=wd_scales[:, t, :],
+                                      in_=wd_bf[:, t].rearrange("p m j -> p (m j)"))
+            for t in range(PACK):
+                a_bank = bank("a_bank")
+                nc.tensor.matmul_mx(out=a_bank[:], lhsT=wd_codes[:, t, :].bitcast(E4M3), lhsT_scale=wd_scales[:, t, :],
+                                    rhs=x_codes[:].bitcast(E4M3), rhs_scale=x_scales[:], start=True, stop=True)
+                nc.scalar.activation(sig[:, t, :], a_bank[:], ACT.Sigmoid)
+                nc.vector.tensor_tensor(diff[:, t, :], sig[:, t, :], y_sb[h][:, t, :], ALU.subtract)
+
+            g_bf = sb.tile([P, N, PACK], BF16, name="g_bf%d" % h, align_bytes=64)
+            g_dst = g_bf[:].rearrange("p (c i) t -> p c t i", i=LINE)
+            g_src = diff[:].rearrange("p t (c i) -> p c t i", i=LINE)
+            half = N // 2
+            for u in range(2):
+                cs = slice(u * half // LINE, (u + 1) * half // LINE)
+                nc.vector.tensor_tensor(g_dst[:, cs], g_src[:, cs], weight[h][:, cs], ALU.mult)
+            for u in range(2):
+                ns = slice(u * half, (u + 1) * half)
+                nc.vector.quantize_mx(out=g_codes[:, h, ns].bitcast(E5M2), scales=g_scales[:, h, ns],
+                                      in_=g_bf[:, ns].rearrange("p n t -> p (n t)"))
+
+        wv_bf = sb.tile([P, D_TILES, V_PASSES, P, PACK], BF16, name="wv_bf", align_bytes=64)
+        wv_codes = sb.tile([P, D_TILES, V_PASSES, P], U32, name="wv_codes", align_bytes=64)
+        wv_scales = sb.tile([P, D_TILES, V_PASSES, P], U8, name="wv_scales", align_bytes=64)
+        for b in range(D_TILES):
+            for h in range(V_PASSES):
+                nc.scalar.copy(wv_bf[:, b, h].rearrange("p (c i) j -> p c j i", i=LINE),
+                               wv_raw[h][:, :, b * P:(b + 1) * P].rearrange("p j (c i) -> p c j i", i=LINE))
+            nc.vector.quantize_mx(out=wv_codes[:, b].rearrange("p h m -> p (h m)").bitcast(E4M3),
+                                  scales=wv_scales[:, b].rearrange("p h m -> p (h m)"),
+                                  in_=wv_bf[:, b].rearrange("p h m j -> p (h m j)"))
+            dx_bank = bank("dx_bank")
+            for h in range(V_PASSES):
+                nc.tensor.matmul_mx(out=dx_bank[:], lhsT=wv_codes[:, b, h, :].bitcast(E4M3), lhsT_scale=wv_scales[:, b, h, :],
+                                    rhs=g_codes[:, h, :].bitcast(E5M2), rhs_scale=g_scales[:, h, :],
+                                    start=(h == 0), stop=(h == V_PASSES - 1))
+            dx = sb.tile([P, N], F32, name="dx%d" % b)
+            nc.scalar.copy(dx[:], dx_bank[:])
+            nc.vector.tensor_copy(windows[b][:].indirect(offsets[:]), dx[:])
+            nc.sync.dma_start(out[b * P:(b + 1) * P, :], windows[b][:])

@@ -54,9 +54,10 @@ def tile_attend_gml_nce_kernel(tc, xT, wd, wv, y, cw, rw, offs, out):
         for j in range(1, PACK):
             nc.sync.dma_start(x_planes[j][:], x_rows[j])
         nc.sync.dma_start(wd_raw[0][:], wd_rows[:, :, 0:PASS])
+        nc.sync.dma_start(wd_raw[1][:, :, 0:PASS // 2], wd_rows[:, :, PASS:PASS + PASS // 2])
         nc.sync.dma_start(y_sb[0][:, 0:2, :], y_rows[0][:, 0:2, :])
         nc.sync.dma_start(y_sb[0][:, 2:4, :], y_rows[0][:, 2:4, :])
-        nc.sync.dma_start(wd_raw[1][:], wd_rows[:, :, PASS:V])
+        nc.sync.dma_start(wd_raw[1][:, :, PASS // 2:PASS], wd_rows[:, :, PASS + PASS // 2:V])
         nc.sync.dma_start(y_sb[1][:], y_rows[1])
         for h in range(V_PASSES):
             nc.sync.dma_start(wv_raw[h][:], wv_rows[h])
@@ -77,9 +78,10 @@ def tile_attend_gml_nce_kernel(tc, xT, wd, wv, y, cw, rw, offs, out):
                 nc.scalar.activation(weight[h][:, :, j, :], rw_bank[:].rearrange("p (i c) -> p c i", i=LINE),
                                      ACT.Copy, scale=cw_sb[:, h, j:j + 1])
 
-        windows = [sb.tile([P, T], F32, name="window%d" % b) for b in range(D_TILES)]
-        for b in range(D_TILES):
-            nc.vector.memset(windows[b][:], 0.0)
+        windows = [sb.tile([P, T], F32, name="window%d" % b) for b in range(3)]
+        nc.vector.memset(windows[0][:], 0.0)
+        nc.vector.memset(windows[1][:], 0.0)
+        nc.gpsimd.memset(windows[2][:], 0.0)
 
         x_bf = sb.tile([P, N, PACK], BF16, name="x_bf", align_bytes=64)
         x_codes = sb.tile([P, N], U32, name="x_codes", align_bytes=64)
@@ -91,33 +93,35 @@ def tile_attend_gml_nce_kernel(tc, xT, wd, wv, y, cw, rw, offs, out):
 
         g_codes = sb.tile([P, V_PASSES, N], U32, name="g_codes", align_bytes=64)
         g_scales = sb.tile([P, V_PASSES, N], U8, name="g_scales", align_bytes=64)
-        for h in range(V_PASSES):
-            wd_bf = sb.tile([P, PACK, P, PACK], BF16, name="wd_bf%d" % h, align_bytes=64)
+        wd_bf = [sb.tile([P, PACK, P, PACK], BF16, name="wd_bf%d" % h, align_bytes=64) for h in range(V_PASSES)]
+        sig = [sb.tile([P, PACK, N], F32, name="sig%d" % h) for h in range(V_PASSES)]
+        diff = [sb.tile([P, PACK, N], F32, name="diff%d" % h) for h in range(V_PASSES)]
+        half = N // 2
+
+        def cast_wd(copy, h, m0, m1):
+            src = wd_raw[h][:].rearrange("p j (m t) -> p m j t", t=PACK)
+            dst = wd_bf[h][:].rearrange("p t m j -> p m j t")
+            copy(dst[:, m0:m1], src[:, m0:m1])
+
+        def logits(h):
             wd_codes = sb.tile([P, PACK, P], U32, name="wd_codes%d" % h, align_bytes=64)
             wd_scales = sb.tile([P, PACK, P], U8, name="wd_scales%d" % h, align_bytes=64)
-            src = wd_raw[h][:].rearrange("p j (m t) -> p m j t", t=PACK)
-            dst = wd_bf[:].rearrange("p t m j -> p m j t")
-            split = WD_VECTOR_COLUMNS if h == 0 else 0
-            if split:
-                nc.vector.tensor_copy(dst[:, 0:split], src[:, 0:split])
-            nc.scalar.copy(dst[:, split:P], src[:, split:P])
-
-            sig = sb.tile([P, PACK, N], F32, name="sig%d" % h)
-            diff = sb.tile([P, PACK, N], F32, name="diff%d" % h)
             for t in range(PACK):
                 nc.vector.quantize_mx(out=wd_codes[:, t, :].bitcast(E4M3), scales=wd_scales[:, t, :],
-                                      in_=wd_bf[:, t].rearrange("p m j -> p (m j)"))
-            for t in range(PACK):
+                                      in_=wd_bf[h][:, t].rearrange("p m j -> p (m j)"))
                 a_bank = bank("a_bank")
                 nc.tensor.matmul_mx(out=a_bank[:], lhsT=wd_codes[:, t, :].bitcast(E4M3), lhsT_scale=wd_scales[:, t, :],
                                     rhs=x_codes[:].bitcast(E4M3), rhs_scale=x_scales[:], start=True, stop=True)
-                nc.scalar.activation(sig[:, t, :], a_bank[:], ACT.Sigmoid)
-                nc.vector.tensor_tensor(diff[:, t, :], sig[:, t, :], y_sb[h][:, t, :], ALU.subtract)
+                nc.scalar.activation(sig[h][:, t, :], a_bank[:], ACT.Sigmoid)
 
+        def subtract_labels(h):
+            for t in range(PACK):
+                nc.vector.tensor_tensor(diff[h][:, t, :], sig[h][:, t, :], y_sb[h][:, t, :], ALU.subtract)
+
+        def weigh_and_quantise(h):
             g_bf = sb.tile([P, N, PACK], BF16, name="g_bf%d" % h, align_bytes=64)
             g_dst = g_bf[:].rearrange("p (c i) t -> p c t i", i=LINE)
-            g_src = diff[:].rearrange("p t (c i) -> p c t i", i=LINE)
-            half = N // 2
+            g_src = diff[h][:].rearrange("p t (c i) -> p c t i", i=LINE)
             for u in range(2):
                 cs = slice(u * half // LINE, (u + 1) * half // LINE)
                 nc.vector.tensor_tensor(g_dst[:, cs], g_src[:, cs], weight[h][:, cs], ALU.mult)
@@ -129,19 +133,50 @@ def tile_attend_gml_nce_kernel(tc, xT, wd, wv, y, cw, rw, offs, out):
         wv_bf = sb.tile([P, D_TILES, V_PASSES, P, PACK], BF16, name="wv_bf", align_bytes=64)
         wv_codes = sb.tile([P, D_TILES, V_PASSES, P], U32, name="wv_codes", align_bytes=64)
         wv_scales = sb.tile([P, D_TILES, V_PASSES, P], U8, name="wv_scales", align_bytes=64)
-        for b in range(D_TILES):
+        dx_banks = {}
+
+        def quantise_wv(b):
             for h in range(V_PASSES):
                 nc.scalar.copy(wv_bf[:, b, h].rearrange("p (c i) j -> p c j i", i=LINE),
                                wv_raw[h][:, :, b * P:(b + 1) * P].rearrange("p j (c i) -> p c j i", i=LINE))
             nc.vector.quantize_mx(out=wv_codes[:, b].rearrange("p h m -> p (h m)").bitcast(E4M3),
                                   scales=wv_scales[:, b].rearrange("p h m -> p (h m)"),
                                   in_=wv_bf[:, b].rearrange("p h m j -> p (h m j)"))
-            dx_bank = bank("dx_bank")
-            for h in range(V_PASSES):
-                nc.tensor.matmul_mx(out=dx_bank[:], lhsT=wv_codes[:, b, h, :].bitcast(E4M3), lhsT_scale=wv_scales[:, b, h, :],
-                                    rhs=g_codes[:, h, :].bitcast(E5M2), rhs_scale=g_scales[:, h, :],
-                                    start=(h == 0), stop=(h == V_PASSES - 1))
+
+        def dx_pass(b, h):
+            if h == 0:
+                dx_banks[b] = bank("dx_bank")
+            nc.tensor.matmul_mx(out=dx_banks[b][:], lhsT=wv_codes[:, b, h, :].bitcast(E4M3),
+                                lhsT_scale=wv_scales[:, b, h, :],
+                                rhs=g_codes[:, h, :].bitcast(E5M2), rhs_scale=g_scales[:, h, :],
+                                start=(h == 0), stop=(h == V_PASSES - 1))
+
+        def scatter_and_store(b, pieces):
             dx = sb.tile([P, N], F32, name="dx%d" % b)
-            nc.scalar.copy(dx[:], dx_bank[:])
-            nc.vector.tensor_copy(windows[b][:].indirect(offsets[:]), dx[:])
-            nc.sync.dma_start(out[b * P:(b + 1) * P, :], windows[b][:])
+            window = windows[b % len(windows)]
+            width = N // pieces
+            for u in range(pieces):
+                ns = slice(u * width, (u + 1) * width)
+                nc.scalar.copy(dx[:, ns], dx_banks[b][:, ns])
+                nc.vector.tensor_copy(window[:].indirect(offsets[:, u * width // 16:(u + 1) * width // 16]), dx[:, ns])
+            nc.sync.dma_start(out[b * P:(b + 1) * P, :], window[:])
+
+        cast_wd(nc.vector.tensor_copy, 0, 0, WD_VECTOR_COLUMNS)
+        cast_wd(nc.scalar.copy, 0, WD_VECTOR_COLUMNS, P)
+        logits(0)
+        subtract_labels(0)
+        cast_wd(nc.scalar.copy, 1, 0, P // 2)
+        cast_wd(nc.scalar.copy, 1, P // 2, P)
+        logits(1)
+        weigh_and_quantise(0)
+        subtract_labels(1)
+        quantise_wv(0)
+        dx_pass(0, 0)
+        weigh_and_quantise(1)
+        dx_pass(0, 1)
+        scatter_and_store(0, 2)
+        for b in range(1, D_TILES):
+            quantise_wv(b)
+            for h in range(V_PASSES):
+                dx_pass(b, h)
+            scatter_and_store(b, 1)

@@ -22,7 +22,6 @@ PASS = P * PACK
 V_PASSES = V // PASS
 D_TILES = D // P
 LINE = 4
-WD_VECTOR_COLUMNS = 80
 
 
 def tile_attend_gml_nce_kernel(tc, xT, wd, wv, y, cw, rw, offs, out):
@@ -54,13 +53,14 @@ def tile_attend_gml_nce_kernel(tc, xT, wd, wv, y, cw, rw, offs, out):
         for j in range(1, PACK):
             nc.sync.dma_start(x_planes[j][:], x_rows[j])
         nc.sync.dma_start(wd_raw[0][:], wd_rows[:, :, 0:PASS])
-        nc.sync.dma_start(wd_raw[1][:, :, 0:PASS // 2], wd_rows[:, :, PASS:PASS + PASS // 2])
         nc.sync.dma_start(y_sb[0][:, 0:2, :], y_rows[0][:, 0:2, :])
         nc.sync.dma_start(y_sb[0][:, 2:4, :], y_rows[0][:, 2:4, :])
-        nc.sync.dma_start(wd_raw[1][:, :, PASS // 2:PASS], wd_rows[:, :, PASS + PASS // 2:V])
+        nc.sync.dma_start(wd_raw[1][:], wd_rows[:, :, PASS:V])
         nc.sync.dma_start(y_sb[1][:], y_rows[1])
-        for h in range(V_PASSES):
-            nc.sync.dma_start(wv_raw[h][:], wv_rows[h])
+        for u in range(2):
+            ds = slice(u * D // 2, (u + 1) * D // 2)
+            for h in range(V_PASSES):
+                nc.sync.dma_start(wv_raw[h][:, :, ds], wv_rows[h][:, :, ds])
 
         warm = sb.tile([P, 1], F32, name="warm")
         warm_out = sb.tile([P, 1], F32, name="warm_out")
@@ -86,22 +86,27 @@ def tile_attend_gml_nce_kernel(tc, xT, wd, wv, y, cw, rw, offs, out):
         x_bf = sb.tile([P, N, PACK], BF16, name="x_bf", align_bytes=64)
         x_codes = sb.tile([P, N], U32, name="x_codes", align_bytes=64)
         x_scales = sb.tile([P, N], U8, name="x_scales", align_bytes=64)
-        for j in range(PACK):
+        half = N // 2
+        halves = [slice(0, half), slice(half, N)]
+        offset_halves = [offsets[:, 0:half // 16], offsets[:, half // 16:N // 16]]
+        for j in range(PACK - 1):
             nc.vector.tensor_copy(x_bf[:, :, j], x_planes[j][:].indirect(offsets[:]))
-        nc.vector.quantize_mx(out=x_codes[:].bitcast(E4M3), scales=x_scales[:],
-                              in_=x_bf[:].rearrange("p n j -> p (n j)"))
+        for u in range(2):
+            nc.vector.tensor_copy(x_bf[:, halves[u], PACK - 1], x_planes[PACK - 1][:].indirect(offset_halves[u]))
+        for u in range(2):
+            nc.vector.quantize_mx(out=x_codes[:, halves[u]].bitcast(E4M3), scales=x_scales[:, halves[u]],
+                                  in_=x_bf[:, halves[u]].rearrange("p n j -> p (n j)"))
 
         g_codes = sb.tile([P, V_PASSES, N], U32, name="g_codes", align_bytes=64)
         g_scales = sb.tile([P, V_PASSES, N], U8, name="g_scales", align_bytes=64)
         wd_bf = [sb.tile([P, PACK, P, PACK], BF16, name="wd_bf%d" % h, align_bytes=64) for h in range(V_PASSES)]
         sig = [sb.tile([P, PACK, N], F32, name="sig%d" % h) for h in range(V_PASSES)]
         diff = [sb.tile([P, PACK, N], F32, name="diff%d" % h) for h in range(V_PASSES)]
-        half = N // 2
 
-        def cast_wd(copy, h, m0, m1):
+        def cast_wd(copy, h, t0):
             src = wd_raw[h][:].rearrange("p j (m t) -> p m j t", t=PACK)
             dst = wd_bf[h][:].rearrange("p t m j -> p m j t")
-            copy(dst[:, m0:m1], src[:, m0:m1])
+            copy(dst[:, :, :, t0:t0 + 2], src[:, :, :, t0:t0 + 2])
 
         def logits(h):
             wd_codes = sb.tile([P, PACK, P], U32, name="wd_codes%d" % h, align_bytes=64)
@@ -116,32 +121,34 @@ def tile_attend_gml_nce_kernel(tc, xT, wd, wv, y, cw, rw, offs, out):
 
         def subtract_labels(h):
             for t in range(PACK):
-                nc.vector.tensor_tensor(diff[h][:, t, :], sig[h][:, t, :], y_sb[h][:, t, :], ALU.subtract)
+                for ns in (halves if t == PACK - 1 else [slice(0, N)]):
+                    nc.vector.tensor_tensor(diff[h][:, t, ns], sig[h][:, t, ns], y_sb[h][:, t, ns], ALU.subtract)
 
-        def weigh_and_quantise(h):
+        def weigh_and_quantise(h, pieces):
             g_bf = sb.tile([P, N, PACK], BF16, name="g_bf%d" % h, align_bytes=64)
             g_dst = g_bf[:].rearrange("p (c i) t -> p c t i", i=LINE)
             g_src = diff[h][:].rearrange("p t (c i) -> p c t i", i=LINE)
-            for u in range(2):
-                cs = slice(u * half // LINE, (u + 1) * half // LINE)
+            for u in range(pieces):
+                cs = slice(u * N // pieces // LINE, (u + 1) * N // pieces // LINE)
                 nc.vector.tensor_tensor(g_dst[:, cs], g_src[:, cs], weight[h][:, cs], ALU.mult)
             for u in range(2):
                 ns = slice(u * half, (u + 1) * half)
                 nc.vector.quantize_mx(out=g_codes[:, h, ns].bitcast(E5M2), scales=g_scales[:, h, ns],
                                       in_=g_bf[:, ns].rearrange("p n t -> p (n t)"))
 
-        wv_bf = sb.tile([P, D_TILES, V_PASSES, P, PACK], BF16, name="wv_bf", align_bytes=64)
         wv_codes = sb.tile([P, D_TILES, V_PASSES, P], U32, name="wv_codes", align_bytes=64)
         wv_scales = sb.tile([P, D_TILES, V_PASSES, P], U8, name="wv_scales", align_bytes=64)
         dx_banks = {}
 
         def quantise_wv(b):
+            wv_bf = sb.tile([P, V_PASSES, P, PACK], BF16, name="wv_bf%d" % b, align_bytes=64)
+            copy = nc.vector.tensor_copy if b == D_TILES - 1 else nc.scalar.copy
             for h in range(V_PASSES):
-                nc.scalar.copy(wv_bf[:, b, h].rearrange("p (c i) j -> p c j i", i=LINE),
+                copy(wv_bf[:, h].rearrange("p (c i) j -> p c j i", i=LINE),
                                wv_raw[h][:, :, b * P:(b + 1) * P].rearrange("p j (c i) -> p c j i", i=LINE))
             nc.vector.quantize_mx(out=wv_codes[:, b].rearrange("p h m -> p (h m)").bitcast(E4M3),
                                   scales=wv_scales[:, b].rearrange("p h m -> p (h m)"),
-                                  in_=wv_bf[:, b].rearrange("p h m j -> p (h m j)"))
+                                  in_=wv_bf[:].rearrange("p h m j -> p (h m j)"))
 
         def dx_pass(b, h):
             if h == 0:
@@ -152,31 +159,33 @@ def tile_attend_gml_nce_kernel(tc, xT, wd, wv, y, cw, rw, offs, out):
                                 start=(h == 0), stop=(h == V_PASSES - 1))
 
         def scatter_and_store(b, pieces):
-            dx = sb.tile([P, N], F32, name="dx%d" % b)
             window = windows[b % len(windows)]
             width = N // pieces
             for u in range(pieces):
                 ns = slice(u * width, (u + 1) * width)
-                nc.scalar.copy(dx[:, ns], dx_banks[b][:, ns])
-                nc.vector.tensor_copy(window[:].indirect(offsets[:, u * width // 16:(u + 1) * width // 16]), dx[:, ns])
+                dx = sb.tile([P, width], F32, name="dx%d_%d" % (b, u), tag="dx%d_%d" % (b, u), align_bytes=64)
+                nc.scalar.copy(dx[:], dx_banks[b][:, ns])
+                nc.vector.tensor_copy(window[:].indirect(offsets[:, u * width // 16:(u + 1) * width // 16]), dx[:])
             nc.sync.dma_start(out[b * P:(b + 1) * P, :], window[:])
 
-        cast_wd(nc.vector.tensor_copy, 0, 0, WD_VECTOR_COLUMNS)
-        cast_wd(nc.scalar.copy, 0, WD_VECTOR_COLUMNS, P)
+        cast_wd(nc.vector.tensor_copy, 0, 0)
+        cast_wd(nc.scalar.copy, 0, 2)
         logits(0)
         subtract_labels(0)
-        cast_wd(nc.scalar.copy, 1, 0, P // 2)
-        cast_wd(nc.scalar.copy, 1, P // 2, P)
+        cast_wd(nc.scalar.copy, 1, 0)
+        cast_wd(nc.scalar.copy, 1, 2)
         logits(1)
-        weigh_and_quantise(0)
+        weigh_and_quantise(0, 4)
         subtract_labels(1)
         quantise_wv(0)
         dx_pass(0, 0)
-        weigh_and_quantise(1)
+        weigh_and_quantise(1, 2)
         dx_pass(0, 1)
         scatter_and_store(0, 2)
         for b in range(1, D_TILES):
             quantise_wv(b)
             for h in range(V_PASSES):
                 dx_pass(b, h)
-            scatter_and_store(b, 1)
+            if b > 1:
+                scatter_and_store(b - 1, 1)
+        scatter_and_store(D_TILES - 1, 1)

@@ -72,10 +72,10 @@ def tile_attend_gml_nce_kernel(tc, xT, wd, wv, y, cw, rw, offs, out):
         rw_bank = bank("rw_bank")
         for i in range(LINE):
             nc.tensor.transpose(rw_bank[:, i * P:(i + 1) * P], rw_sb[:, i:i + 1].to_broadcast([P, P]), ident[:])
-        weight = [sb.tile([P, N // LINE, PACK, LINE], F32, name="weight%d" % h) for h in range(V_PASSES)]
+        weight = [sb.tile([P, PACK, N], F32, name="weight%d" % h) for h in range(V_PASSES)]
         for h in range(V_PASSES):
             for j in range(PACK):
-                nc.scalar.activation(weight[h][:, :, j, :], rw_bank[:].rearrange("p (i c) -> p c i", i=LINE),
+                nc.scalar.activation(weight[h][:, j, :].rearrange("p (c i) -> p c i", i=LINE), rw_bank[:].rearrange("p (i c) -> p c i", i=LINE),
                                      ACT.Copy, scale=cw_sb[:, h, j:j + 1])
 
         windows = [sb.tile([P, T], F32, name="window%d" % b) for b in range(3)]
@@ -103,10 +103,10 @@ def tile_attend_gml_nce_kernel(tc, xT, wd, wv, y, cw, rw, offs, out):
         sig = [sb.tile([P, PACK, N], F32, name="sig%d" % h) for h in range(V_PASSES)]
         diff = [sb.tile([P, PACK, N], F32, name="diff%d" % h) for h in range(V_PASSES)]
 
-        def cast_wd(copy, h, t0):
+        def cast_wd(copy, h, t0, ms):
             src = wd_raw[h][:].rearrange("p j (m t) -> p m j t", t=PACK)
             dst = wd_bf[h][:].rearrange("p t m j -> p m j t")
-            copy(dst[:, :, :, t0:t0 + 2], src[:, :, :, t0:t0 + 2])
+            copy(dst[:, ms, :, t0:t0 + 2], src[:, ms, :, t0:t0 + 2])
 
         def logits(h):
             wd_codes = sb.tile([P, PACK, P], U32, name="wd_codes%d" % h, align_bytes=64)
@@ -126,11 +126,12 @@ def tile_attend_gml_nce_kernel(tc, xT, wd, wv, y, cw, rw, offs, out):
 
         def weigh_and_quantise(h, pieces):
             g_bf = sb.tile([P, N, PACK], BF16, name="g_bf%d" % h, align_bytes=64)
-            g_dst = g_bf[:].rearrange("p (c i) t -> p c t i", i=LINE)
-            g_src = diff[h][:].rearrange("p t (c i) -> p c t i", i=LINE)
+            g_dst = g_bf[:].rearrange("p (c i) t -> p c t i", i=2)
+            g_src = diff[h][:].rearrange("p t (c i) -> p c t i", i=2)
+            g_weight = weight[h][:].rearrange("p t (c i) -> p c t i", i=2)
             for u in range(pieces):
-                cs = slice(u * N // pieces // LINE, (u + 1) * N // pieces // LINE)
-                nc.vector.tensor_tensor(g_dst[:, cs], g_src[:, cs], weight[h][:, cs], ALU.mult)
+                cs = slice(u * N // pieces // 2, (u + 1) * N // pieces // 2)
+                nc.vector.tensor_tensor(g_dst[:, cs], g_src[:, cs], g_weight[:, cs], ALU.mult)
             for u in range(2):
                 ns = slice(u * half, (u + 1) * half)
                 nc.vector.quantize_mx(out=g_codes[:, h, ns].bitcast(E5M2), scales=g_scales[:, h, ns],
@@ -168,12 +169,13 @@ def tile_attend_gml_nce_kernel(tc, xT, wd, wv, y, cw, rw, offs, out):
                 nc.vector.tensor_copy(window[:].indirect(offsets[:, u * width // 16:(u + 1) * width // 16]), dx[:])
             nc.sync.dma_start(out[b * P:(b + 1) * P, :], window[:])
 
-        cast_wd(nc.vector.tensor_copy, 0, 0)
-        cast_wd(nc.scalar.copy, 0, 2)
+        for t0 in (0, 2):
+            cast_wd(nc.vector.tensor_copy, 0, t0, slice(0, 80))
+            cast_wd(nc.scalar.copy, 0, t0, slice(80, P))
         logits(0)
         subtract_labels(0)
-        cast_wd(nc.scalar.copy, 1, 0)
-        cast_wd(nc.scalar.copy, 1, 2)
+        for t0 in (0, 2):
+            cast_wd(nc.scalar.copy, 1, t0, slice(0, P))
         logits(1)
         weigh_and_quantise(0, 4)
         subtract_labels(1)

@@ -36,7 +36,7 @@ def tile_attend_gml_nce_kernel(tc, xT, wd, wv, y, cw, rw, offs, out):
         offsets = sb.tile([P, N // 16], U16, name="offsets")
         x_planes = [sb.tile([P, T], F32, name="x_plane%d" % j) for j in range(PACK)]
         wd_raw = [sb.tile([P, PACK, PASS], F32, name="wd_raw%d" % h) for h in range(V_PASSES)]
-        wv_raw = [sb.tile([P, PACK, D], F32, name="wv_raw%d" % h) for h in range(V_PASSES)]
+        wv_raw = [[sb.tile([P, PACK, D // 2], F32, name="wv_raw%d_%d" % (h, u)) for u in range(2)] for h in range(V_PASSES)]
         y_sb = [sb.tile([P, PACK, N], F32, name="y_sb%d" % h) for h in range(V_PASSES)]
         cw_sb = sb.tile([P, V_PASSES, PACK], F32, name="cw_sb")
         rw_sb = sb.tile([P, LINE], F32, name="rw_sb")
@@ -60,7 +60,7 @@ def tile_attend_gml_nce_kernel(tc, xT, wd, wv, y, cw, rw, offs, out):
         for u in range(2):
             ds = slice(u * D // 2, (u + 1) * D // 2)
             for h in range(V_PASSES):
-                nc.sync.dma_start(wv_raw[h][:, :, ds], wv_rows[h][:, :, ds])
+                nc.sync.dma_start(wv_raw[h][u][:], wv_rows[h][:, :, ds])
 
         warm = sb.tile([P, 1], F32, name="warm")
         warm_out = sb.tile([P, 1], F32, name="warm_out")
@@ -146,7 +146,7 @@ def tile_attend_gml_nce_kernel(tc, xT, wd, wv, y, cw, rw, offs, out):
             copy = nc.vector.tensor_copy if b == D_TILES - 1 else nc.scalar.copy
             for h in range(V_PASSES):
                 copy(wv_bf[:, h].rearrange("p (c i) j -> p c j i", i=LINE),
-                               wv_raw[h][:, :, b * P:(b + 1) * P].rearrange("p j (c i) -> p c j i", i=LINE))
+                               wv_raw[h][b // 2][:, :, b % 2 * P:(b % 2 + 1) * P].rearrange("p j (c i) -> p c j i", i=LINE))
             nc.vector.quantize_mx(out=wv_codes[:, b].rearrange("p h m -> p (h m)").bitcast(E4M3),
                                   scales=wv_scales[:, b].rearrange("p h m -> p (h m)"),
                                   in_=wv_bf[:].rearrange("p h m j -> p (h m j)"))

@@ -119,45 +119,49 @@ def tile_attend_gml_nce_kernel(tc, xT, wd, wv, y, cw, rw, offs, out):
                                     rhs=x_codes[:].bitcast(E4M3), rhs_scale=x_scales[:], start=True, stop=True)
                 nc.scalar.activation(sig[h][:, t, :], a_bank[:], ACT.Sigmoid)
 
-        def subtract_labels(h):
-            for t in range(PACK):
-                for ns in (halves if t == PACK - 1 else [slice(0, N)]):
+        def subtract_labels(h, ts):
+            for t in ts:
+                for ns in ([slice(0, P), slice(P, N)] if t == PACK - 1 else [slice(0, N)]):
                     nc.vector.tensor_tensor(diff[h][:, t, ns], sig[h][:, t, ns], y_sb[h][:, t, ns], ALU.subtract)
 
-        def weigh_and_quantise(h, pieces):
-            g_bf = sb.tile([P, N, PACK], BF16, name="g_bf%d" % h, align_bytes=64)
-            g_dst = g_bf[:].rearrange("p (c i) t -> p c t i", i=2)
+        g_bf = [sb.tile([P, N, PACK], BF16, name="g_bf%d" % h, align_bytes=64) for h in range(V_PASSES)]
+
+        def weigh(h, cuts):
+            g_dst = g_bf[h][:].rearrange("p (c i) t -> p c t i", i=2)
             g_src = diff[h][:].rearrange("p t (c i) -> p c t i", i=2)
             g_weight = weight[h][:].rearrange("p t (c i) -> p c t i", i=2)
-            for u in range(pieces):
-                cs = slice(u * N // pieces // 2, (u + 1) * N // pieces // 2)
+            for n0, n1 in zip(cuts, cuts[1:]):
+                cs = slice(n0 // 2, n1 // 2)
                 nc.vector.tensor_tensor(g_dst[:, cs], g_src[:, cs], g_weight[:, cs], ALU.mult)
-            for u in range(2):
-                ns = slice(u * half, (u + 1) * half)
-                nc.vector.quantize_mx(out=g_codes[:, h, ns].bitcast(E5M2), scales=g_scales[:, h, ns],
-                                      in_=g_bf[:, ns].rearrange("p n t -> p (n t)"))
+
+        def quantise_g(h, n0, n1):
+            nc.vector.quantize_mx(out=g_codes[:, h, n0:n1].bitcast(E5M2), scales=g_scales[:, h, n0:n1],
+                                  in_=g_bf[h][:, n0:n1].rearrange("p n t -> p (n t)"))
 
         wv_codes = sb.tile([P, D_TILES, V_PASSES, P], U32, name="wv_codes", align_bytes=64)
         wv_scales = sb.tile([P, D_TILES, V_PASSES, P], U8, name="wv_scales", align_bytes=64)
         dx_banks = {}
 
-        def quantise_wv(b):
-            wv_bf = sb.tile([P, V_PASSES, P, PACK], BF16, name="wv_bf%d" % b, align_bytes=64)
-            copy = nc.vector.tensor_copy if b == D_TILES - 1 else nc.scalar.copy
+        wv_bf = [sb.tile([P, V_PASSES, P, PACK], BF16, name="wv_bf%d" % b, align_bytes=64) for b in range(D_TILES)]
+
+        def cast_wv(copy, b):
             for h in range(V_PASSES):
-                copy(wv_bf[:, h].rearrange("p (c i) j -> p c j i", i=LINE),
-                               wv_raw[h][b // 2][:, :, b % 2 * P:(b % 2 + 1) * P].rearrange("p j (c i) -> p c j i", i=LINE))
+                copy(wv_bf[b][:, h].rearrange("p (c i) j -> p c j i", i=LINE),
+                     wv_raw[h][b // 2][:, :, b % 2 * P:(b % 2 + 1) * P].rearrange("p j (c i) -> p c j i", i=LINE))
+
+        def quantise_wv(b):
             nc.vector.quantize_mx(out=wv_codes[:, b].rearrange("p h m -> p (h m)").bitcast(E4M3),
                                   scales=wv_scales[:, b].rearrange("p h m -> p (h m)"),
-                                  in_=wv_bf[:].rearrange("p h m j -> p (h m j)"))
+                                  in_=wv_bf[b][:].rearrange("p h m j -> p (h m j)"))
 
         def dx_pass(b, h):
-            if h == 0:
+            first = h == (0 if b == 0 else V_PASSES - 1)
+            if first:
                 dx_banks[b] = bank("dx_bank")
             nc.tensor.matmul_mx(out=dx_banks[b][:], lhsT=wv_codes[:, b, h, :].bitcast(E4M3),
                                 lhsT_scale=wv_scales[:, b, h, :],
                                 rhs=g_codes[:, h, :].bitcast(E5M2), rhs_scale=g_scales[:, h, :],
-                                start=(h == 0), stop=(h == V_PASSES - 1))
+                                start=first, stop=not first)
 
         def scatter_and_store(b, pieces):
             window = windows[b % len(windows)]
@@ -173,21 +177,30 @@ def tile_attend_gml_nce_kernel(tc, xT, wd, wv, y, cw, rw, offs, out):
             cast_wd(nc.vector.tensor_copy, 0, t0, slice(0, 80))
             cast_wd(nc.scalar.copy, 0, t0, slice(80, P))
         logits(0)
-        subtract_labels(0)
+        subtract_labels(0, range(PACK))
         for t0 in (0, 2):
             cast_wd(nc.scalar.copy, 1, t0, slice(0, P))
         logits(1)
-        weigh_and_quantise(0, 4)
-        subtract_labels(1)
+        weigh(0, (0, 128, 256, 384, 512))
+        quantise_g(0, 0, half)
+        subtract_labels(1, [0])
+        quantise_g(0, half, N)
+        subtract_labels(1, range(1, PACK))
+        weigh(1, (0, 128, 384))
+        cast_wv(nc.scalar.copy, 0)
         quantise_wv(0)
         dx_pass(0, 0)
-        weigh_and_quantise(1, 2)
+        weigh(1, (384, 512))
+        for n0, n1 in ((0, 256), (256, 384), (384, 512)):
+            quantise_g(1, n0, n1)
         dx_pass(0, 1)
-        scatter_and_store(0, 2)
+        for b in range(1, D_TILES - 1):
+            cast_wv(nc.scalar.copy, b)
+        cast_wv(nc.vector.tensor_copy, D_TILES - 1)
         for b in range(1, D_TILES):
             quantise_wv(b)
-            for h in range(V_PASSES):
+        scatter_and_store(0, 1)
+        for b in range(1, D_TILES):
+            for h in reversed(range(V_PASSES)):
                 dx_pass(b, h)
-            if b > 1:
-                scatter_and_store(b - 1, 1)
-        scatter_and_store(D_TILES - 1, 1)
+            scatter_and_store(b, 1)

@@ -22,12 +22,16 @@ PASS = P * PACK
 V_PASSES = V // PASS
 D_TILES = D // P
 LINE = 4
+DIRECT = 384
+TURNED = range(DIRECT // P, N // P)
 
 
 def tile_attend_gml_nce_kernel(tc, xT, wd, wv, y, cw, rw, offs, out):
     nc = tc.nc
     with ExitStack() as ctx:
         sb = ctx.enter_context(tc.tile_pool(name="sb", bufs=1))
+        line = ctx.enter_context(tc.tile_pool(name="line", bufs=PACK + 1))
+        late = ctx.enter_context(tc.tile_pool(name="late", bufs=D_TILES + 2))
         psum = ctx.enter_context(tc.psum_pool(name="psum", bufs=8))
 
         def bank(name):
@@ -35,7 +39,12 @@ def tile_attend_gml_nce_kernel(tc, xT, wd, wv, y, cw, rw, offs, out):
 
         offsets = sb.tile([P, N // 16], U16, name="offsets")
         x_planes = [sb.tile([P, T], F32, name="x_plane%d" % j) for j in range(PACK)]
-        wd_raw = [sb.tile([P, PACK, PASS], F32, name="wd_raw%d" % h) for h in range(V_PASSES)]
+        wd_parts = ((0, 0, P), (1, 0, 48), (1, 48, P))
+        wd_raw = {(h, m0): sb.tile([P, PACK, (m1 - m0) * PACK], F32, name="wd_raw%d_%d" % (h, m0)) for h, m0, m1 in wd_parts}
+
+        def load_wd(h, m0, m1):
+            nc.sync.dma_start(wd_raw[h, m0][:], wd_rows[:, :, h * PASS + m0 * PACK:h * PASS + m1 * PACK])
+
         wv_raw = [[sb.tile([P, PACK, D // 2], F32, name="wv_raw%d_%d" % (h, u)) for u in range(2)] for h in range(V_PASSES)]
         y_sb = [sb.tile([P, PACK, N], F32, name="y_sb%d" % h) for h in range(V_PASSES)]
         cw_sb = sb.tile([P, V_PASSES, PACK], F32, name="cw_sb")
@@ -52,10 +61,11 @@ def tile_attend_gml_nce_kernel(tc, xT, wd, wv, y, cw, rw, offs, out):
         nc.scalar.dma_start(cw_sb[:], cw.rearrange("(h p j) o -> p h (j o)", p=P, j=PACK))
         for j in range(1, PACK):
             nc.sync.dma_start(x_planes[j][:], x_rows[j])
-        nc.sync.dma_start(wd_raw[0][:], wd_rows[:, :, 0:PASS])
+        load_wd(*wd_parts[0])
+        load_wd(*wd_parts[1])
         nc.sync.dma_start(y_sb[0][:, 0:2, :], y_rows[0][:, 0:2, :])
         nc.sync.dma_start(y_sb[0][:, 2:4, :], y_rows[0][:, 2:4, :])
-        nc.sync.dma_start(wd_raw[1][:], wd_rows[:, :, PASS:V])
+        load_wd(*wd_parts[2])
         nc.sync.dma_start(y_sb[1][:], y_rows[1])
         for u in range(2):
             ds = slice(u * D // 2, (u + 1) * D // 2)
@@ -72,16 +82,39 @@ def tile_attend_gml_nce_kernel(tc, xT, wd, wv, y, cw, rw, offs, out):
         rw_bank = bank("rw_bank")
         for i in range(LINE):
             nc.tensor.transpose(rw_bank[:, i * P:(i + 1) * P], rw_sb[:, i:i + 1].to_broadcast([P, P]), ident[:])
-        weight = [sb.tile([P, PACK, N], F32, name="weight%d" % h) for h in range(V_PASSES)]
-        for h in range(V_PASSES):
-            for j in range(PACK):
-                nc.scalar.activation(weight[h][:, j, :].rearrange("p (c i) -> p c i", i=LINE), rw_bank[:].rearrange("p (i c) -> p c i", i=LINE),
-                                     ACT.Copy, scale=cw_sb[:, h, j:j + 1])
+        minus_rw = sb.tile([P, N], F32, name="minus_rw")
+        nc.scalar.activation(minus_rw[:].rearrange("p (c i) -> p c i", i=LINE), rw_bank[:].rearrange("p (i c) -> p c i", i=LINE), ACT.Copy, scale=-1.0)
+        weight = [sb.tile([P, PACK, N], F32, name="weight0"), sb.tile([P, PACK, DIRECT], F32, name="weight1")]
+        for j in range(PACK):
+            nc.scalar.activation(weight[0][:, j, :].rearrange("p (c i) -> p c i", i=LINE), rw_bank[:].rearrange("p (i c) -> p c i", i=LINE),
+                                 ACT.Copy, scale=cw_sb[:, 0, j:j + 1])
+        for j in range(PACK):
+            nc.scalar.activation(weight[1][:, j, :], minus_rw[:, 0:DIRECT], ACT.Copy, scale=cw_sb[:, 1, j:j + 1])
+        column_bank = bank("column_bank")
+        for q in TURNED:
+            nc.tensor.transpose(column_bank[:, q * P:(q + 1) * P], minus_rw[:, q * P:(q + 1) * P], ident[:])
+        minus_rw_column = sb.tile([P, len(TURNED)], F32, name="minus_rw_column")
+        nc.scalar.copy(minus_rw_column[:], column_bank[:, DIRECT:N:P])
 
-        windows = [sb.tile([P, T], F32, name="window%d" % b) for b in range(3)]
+        def place(t):
+            return slice((t % 2 * 2 + t // 2) * P, (t % 2 * 2 + t // 2 + 1) * P)
+
+        def by_words(full_bank):
+            return full_bank[:].rearrange("p (e k) -> p k e", e=2)
+
+        cw_bank = bank("cw_bank")
+        for t in range(PACK):
+            nc.tensor.transpose(cw_bank[:, place(t)], cw_sb[:, 1, t:t + 1].to_broadcast([P, P]), ident[:])
+        weight_turned = {}
+        for q in TURNED:
+            weight_turned[q] = sb.tile([P, 2 * P, 2], F32, name="weight_turned%d" % q)
+            nc.scalar.activation(weight_turned[q][:], by_words(cw_bank), ACT.Copy, scale=minus_rw_column[:, q - TURNED[0]:q - TURNED[0] + 1])
+
+        windows = [sb.tile([P, T], F32, name="window%d" % b) for b in range(D_TILES)]
         nc.vector.memset(windows[0][:], 0.0)
         nc.vector.memset(windows[1][:], 0.0)
-        nc.gpsimd.memset(windows[2][:], 0.0)
+        nc.vector.memset(windows[2][:], 0.0)
+        nc.gpsimd.memset(windows[3][:], 0.0)
 
         x_bf = sb.tile([P, N, PACK], BF16, name="x_bf", align_bytes=64)
         x_codes = sb.tile([P, N], U32, name="x_codes", align_bytes=64)
@@ -99,32 +132,68 @@ def tile_attend_gml_nce_kernel(tc, xT, wd, wv, y, cw, rw, offs, out):
 
         g_codes = sb.tile([P, V_PASSES, N], U32, name="g_codes", align_bytes=64)
         g_scales = sb.tile([P, V_PASSES, N], U8, name="g_scales", align_bytes=64)
-        wd_bf = [sb.tile([P, PACK, P, PACK], BF16, name="wd_bf%d" % h, align_bytes=64) for h in range(V_PASSES)]
+        wd_codes = {}
+        wd_bf = {0: sb.tile([P, PACK, P, PACK], BF16, name="wd_bf0", align_bytes=64)}
+        for t in range(PACK):
+            wd_codes[0, t] = line.tile([P, P], U32, name="wd_codes0_%d" % t, tag="wd_line", align_bytes=64)
+        wd_bf[1] = line.tile([P, PACK, P, PACK], BF16, name="wd_bf1", tag="wd_line", align_bytes=64)
+        for t in range(PACK):
+            wd_codes[1, t] = sb.tile([P, P], U32, name="wd_codes1_%d" % t, align_bytes=64)
         sig = [sb.tile([P, PACK, N], F32, name="sig%d" % h) for h in range(V_PASSES)]
-        diff = [sb.tile([P, PACK, N], F32, name="diff%d" % h) for h in range(V_PASSES)]
+        diff = [sb.tile([P, PACK, (N, DIRECT)[h]], F32, name="diff%d" % h) for h in range(V_PASSES)]
 
-        def cast_wd(copy, h, t0, ms):
-            src = wd_raw[h][:].rearrange("p j (m t) -> p m j t", t=PACK)
+        def cast_wd(copy, h, t0, ms, m0=0):
+            src = wd_raw[h, m0][:].rearrange("p j (m t) -> p m j t", t=PACK)
             dst = wd_bf[h][:].rearrange("p t m j -> p m j t")
-            copy(dst[:, ms, :, t0:t0 + 2], src[:, ms, :, t0:t0 + 2])
+            copy(dst[:, ms, :, t0:t0 + 2], src[:, ms.start - m0:ms.stop - m0, :, t0:t0 + 2])
 
         def logits(h):
-            wd_codes = sb.tile([P, PACK, P], U32, name="wd_codes%d" % h, align_bytes=64)
             wd_scales = sb.tile([P, PACK, P], U8, name="wd_scales%d" % h, align_bytes=64)
             for t in range(PACK):
-                nc.vector.quantize_mx(out=wd_codes[:, t, :].bitcast(E4M3), scales=wd_scales[:, t, :],
+                nc.vector.quantize_mx(out=wd_codes[h, t][:].bitcast(E4M3), scales=wd_scales[:, t, :],
                                       in_=wd_bf[h][:, t].rearrange("p m j -> p (m j)"))
                 a_bank = bank("a_bank")
-                nc.tensor.matmul_mx(out=a_bank[:], lhsT=wd_codes[:, t, :].bitcast(E4M3), lhsT_scale=wd_scales[:, t, :],
+                nc.tensor.matmul_mx(out=a_bank[:], lhsT=wd_codes[h, t][:].bitcast(E4M3), lhsT_scale=wd_scales[:, t, :],
                                     rhs=x_codes[:].bitcast(E4M3), rhs_scale=x_scales[:], start=True, stop=True)
-                nc.scalar.activation(sig[h][:, t, :], a_bank[:], ACT.Sigmoid)
+                nc.scalar.activation(sig[h][:, t, :], a_bank[:], ACT.Sigmoid, scale=(1.0, -1.0)[h])
 
         def subtract_labels(h, ts):
             for t in ts:
                 for ns in ([slice(0, P), slice(P, N)] if t == PACK - 1 else [slice(0, N)]):
                     nc.vector.tensor_tensor(diff[h][:, t, ns], sig[h][:, t, ns], y_sb[h][:, t, ns], ALU.subtract)
 
-        g_bf = [sb.tile([P, N, PACK], BF16, name="g_bf%d" % h, align_bytes=64) for h in range(V_PASSES)]
+        g_bf = [sb.tile([P, (N, DIRECT)[h], PACK], BF16, name="g_bf%d" % h, align_bytes=64) for h in range(V_PASSES)]
+
+        def add_labels(t, ns):
+            nc.vector.scalar_tensor_tensor(diff[1][:, t, ns], y_sb[1][:, t, ns], -1.0, sig[1][:, t, ns], ALU.add, ALU.add)
+
+        def turn_and_add():
+            sums = {q: bank("sum_bank") for q in TURNED}
+            for q in TURNED:
+                for t in range(PACK):
+                    nc.tensor.matmul(sums[q][:, place(t)], lhsT=y_sb[1][:, t, q * P:(q + 1) * P], rhs=ident[:], is_transpose=True,
+                                     start=t == 0, stop=False)
+            for t in range(PACK):
+                for q in TURNED:
+                    nc.tensor.matmul(sums[q][:, place(t)], lhsT=sig[1][:, t, q * P:(q + 1) * P], rhs=ident[:], is_transpose=True,
+                                     start=False, stop=t == PACK - 1)
+            return sums
+
+        g_words = {}
+
+        def weigh_turned(sums, q):
+            g_turned = sb.tile([P, 2 * P, 2], BF16, name="g_turned%d" % q, align_bytes=64)
+            nc.vector.scalar_tensor_tensor(g_turned[:], by_words(sums[q]), -1.0, weight_turned[q][:], ALU.add, ALU.mult)
+            words = g_turned[:].rearrange("p k e -> p (k e)").bitcast(F32)
+            word_bank = bank("word_bank")
+            for u in range(2):
+                nc.tensor.transpose(word_bank[:, u * P:(u + 1) * P], words[:, u * P:(u + 1) * P], ident[:])
+            g_words[q] = sb.tile([P, P, 2], F32, name="g_words%d" % q, align_bytes=64)
+            nc.scalar.copy(g_words[q][:], word_bank[:, 0:2 * P].rearrange("p (u i) -> p i u", u=2))
+
+        def quantise_turned(q):
+            nc.vector.quantize_mx(out=g_codes[:, 1, q * P:(q + 1) * P].bitcast(E5M2), scales=g_scales[:, 1, q * P:(q + 1) * P],
+                                  in_=g_words[q][:].rearrange("p i u -> p (i u)").bitcast(BF16))
 
         def weigh(h, cuts):
             g_dst = g_bf[h][:].rearrange("p (c i) t -> p c t i", i=2)
@@ -163,44 +232,54 @@ def tile_attend_gml_nce_kernel(tc, xT, wd, wv, y, cw, rw, offs, out):
                                 rhs=g_codes[:, h, :].bitcast(E5M2), rhs_scale=g_scales[:, h, :],
                                 start=first, stop=not first)
 
-        def scatter_and_store(b, pieces):
-            window = windows[b % len(windows)]
-            width = N // pieces
-            for u in range(pieces):
-                ns = slice(u * width, (u + 1) * width)
-                dx = sb.tile([P, width], F32, name="dx%d_%d" % (b, u), tag="dx%d_%d" % (b, u), align_bytes=64)
-                nc.scalar.copy(dx[:], dx_banks[b][:, ns])
-                nc.vector.tensor_copy(window[:].indirect(offsets[:, u * width // 16:(u + 1) * width // 16]), dx[:])
-            nc.sync.dma_start(out[b * P:(b + 1) * P, :], window[:])
+        def scatter(b, ns):
+            dx = late.tile([P, ns.stop - ns.start], F32, name="dx%d_%d" % (b, ns.start), tag="dx", align_bytes=64)
+            nc.scalar.copy(dx[:], dx_banks[b][:, ns])
+            nc.vector.tensor_copy(windows[b % len(windows)][:].indirect(offsets[:, ns.start // 16:ns.stop // 16]), dx[:])
+            if ns.stop == N:
+                nc.sync.dma_start(out[b * P:(b + 1) * P, :], windows[b % len(windows)][:])
 
         for t0 in (0, 2):
             cast_wd(nc.vector.tensor_copy, 0, t0, slice(0, 80))
             cast_wd(nc.scalar.copy, 0, t0, slice(80, P))
         logits(0)
+        for t0 in (0, 2):
+            cast_wd(nc.vector.tensor_copy, 1, t0, slice(0, 48))
         subtract_labels(0, range(PACK))
         for t0 in (0, 2):
-            cast_wd(nc.scalar.copy, 1, t0, slice(0, P))
+            cast_wd(nc.scalar.copy, 1, t0, slice(48, P), 48)
         logits(1)
         weigh(0, (0, 128, 256, 384, 512))
         quantise_g(0, 0, half)
-        subtract_labels(1, [0])
+        add_labels(0, slice(0, DIRECT))
         quantise_g(0, half, N)
-        subtract_labels(1, range(1, PACK))
-        weigh(1, (0, 128, 384))
+        for t in (1, 2):
+            add_labels(t, slice(0, DIRECT))
+        add_labels(3, slice(0, P))
+        add_labels(3, slice(P, DIRECT))
+        sums = turn_and_add()
+        for q in TURNED:
+            weigh_turned(sums, q)
+        weigh(1, (0, 128, 256))
         cast_wv(nc.scalar.copy, 0)
         quantise_wv(0)
         dx_pass(0, 0)
-        weigh(1, (384, 512))
-        for n0, n1 in ((0, 256), (256, 384), (384, 512)):
-            quantise_g(1, n0, n1)
+        weigh(1, (DIRECT - P, DIRECT))
+        quantise_g(1, 0, 256)
+        quantise_turned(3)
+        quantise_g(1, 256, 384)
         dx_pass(0, 1)
         for b in range(1, D_TILES - 1):
             cast_wv(nc.scalar.copy, b)
+        quantise_wv(1)
         cast_wv(nc.vector.tensor_copy, D_TILES - 1)
-        for b in range(1, D_TILES):
+        for b in range(2, D_TILES):
             quantise_wv(b)
-        scatter_and_store(0, 1)
         for b in range(1, D_TILES):
             for h in reversed(range(V_PASSES)):
                 dx_pass(b, h)
-            scatter_and_store(b, 1)
+        for ns in halves:
+            for b in range(2):
+                scatter(b, ns)
+        for b in range(2, D_TILES):
+            scatter(b, slice(0, N))

@@ -22,7 +22,16 @@ PASS = P * PACK
 V_PASSES = V // PASS
 D_TILES = D // P
 LINE = 4
-DIRECT = 384
+DIRECT = 256
+EARLY_TILES = 2
+WD0_VECTOR = 80
+WD1_EARLY = 48
+WD1_VECTOR = 48
+LOADS = ("wd0", "wd1a", "y0_02", "y0_24", "wd1b", "y1", "wv0", "wv1")
+Y_FIRST = True
+S_ORDER = "wBw"
+V_ORDER = "aqbqcd"
+SPLIT_WV0 = True
 TURNED = range(DIRECT // P, N // P)
 
 
@@ -31,7 +40,9 @@ def tile_attend_gml_nce_kernel(tc, xT, wd, wv, y, cw, rw, offs, out):
     with ExitStack() as ctx:
         sb = ctx.enter_context(tc.tile_pool(name="sb", bufs=1))
         line = ctx.enter_context(tc.tile_pool(name="line", bufs=PACK + 1))
-        late = ctx.enter_context(tc.tile_pool(name="late", bufs=D_TILES + 2))
+        late = ctx.enter_context(tc.tile_pool(name="late", bufs=15))
+        vline = ctx.enter_context(tc.tile_pool(name="vline", bufs=6))
+        ahead = ctx.enter_context(tc.tile_pool(name="ahead", bufs=4))
         psum = ctx.enter_context(tc.psum_pool(name="psum", bufs=8))
 
         def bank(name):
@@ -39,14 +50,19 @@ def tile_attend_gml_nce_kernel(tc, xT, wd, wv, y, cw, rw, offs, out):
 
         offsets = sb.tile([P, N // 16], U16, name="offsets")
         x_planes = [sb.tile([P, T], F32, name="x_plane%d" % j) for j in range(PACK)]
-        wd_parts = ((0, 0, P), (1, 0, 48), (1, 48, P))
+        wd_parts = [part for part in ((0, 0, P), (1, 0, WD1_EARLY), (1, WD1_EARLY, P)) if part[1] < part[2]]
         wd_raw = {(h, m0): sb.tile([P, PACK, (m1 - m0) * PACK], F32, name="wd_raw%d_%d" % (h, m0)) for h, m0, m1 in wd_parts}
 
         def load_wd(h, m0, m1):
             nc.sync.dma_start(wd_raw[h, m0][:], wd_rows[:, :, h * PASS + m0 * PACK:h * PASS + m1 * PACK])
 
         wv_raw = [[sb.tile([P, PACK, D // 2], F32, name="wv_raw%d_%d" % (h, u)) for u in range(2)] for h in range(V_PASSES)]
-        y_sb = [sb.tile([P, PACK, N], F32, name="y_sb%d" % h) for h in range(V_PASSES)]
+        y_sb = [sb.tile([P, PACK, N], F32, name="y_sb0")]
+        if "y1" in LOADS:
+            y_whole = sb.tile([P, PACK, N], F32, name="y_sb1")
+            y1 = [y_whole[:, :, 0:DIRECT], y_whole[:, :, DIRECT:N]]
+        else:
+            y1 = [sb.tile([P, PACK, DIRECT], F32, name="y1_%d" % u)[:] for u in range(2)]
         cw_sb = sb.tile([P, V_PASSES, PACK], F32, name="cw_sb")
         rw_sb = sb.tile([P, LINE], F32, name="rw_sb")
 
@@ -61,16 +77,25 @@ def tile_attend_gml_nce_kernel(tc, xT, wd, wv, y, cw, rw, offs, out):
         nc.scalar.dma_start(cw_sb[:], cw.rearrange("(h p j) o -> p h (j o)", p=P, j=PACK))
         for j in range(1, PACK):
             nc.sync.dma_start(x_planes[j][:], x_rows[j])
-        load_wd(*wd_parts[0])
-        load_wd(*wd_parts[1])
-        nc.sync.dma_start(y_sb[0][:, 0:2, :], y_rows[0][:, 0:2, :])
-        nc.sync.dma_start(y_sb[0][:, 2:4, :], y_rows[0][:, 2:4, :])
-        load_wd(*wd_parts[2])
-        nc.sync.dma_start(y_sb[1][:], y_rows[1])
-        for u in range(2):
-            ds = slice(u * D // 2, (u + 1) * D // 2)
-            for h in range(V_PASSES):
-                nc.sync.dma_start(wv_raw[h][u][:], wv_rows[h][:, :, ds])
+        for what in LOADS:
+            if what == "wd0":
+                load_wd(0, 0, P)
+            elif what == "wd1a":
+                load_wd(1, 0, WD1_EARLY)
+            elif what == "wd1b":
+                load_wd(1, WD1_EARLY, P)
+            elif what.startswith("y0"):
+                ts = slice(int(what[3]), int(what[4]))
+                nc.sync.dma_start(y_sb[0][:, ts, :], y_rows[0][:, ts, :])
+            elif what == "y1":
+                nc.sync.dma_start(y_whole[:], y_rows[1])
+            elif what.startswith("y1"):
+                u = "ab".index(what[2])
+                nc.sync.dma_start(y1[u], y_rows[1][:, :, u * DIRECT:(u + 1) * DIRECT])
+            else:
+                u = int(what[2])
+                for h in range(V_PASSES):
+                    nc.sync.dma_start(wv_raw[h][u][:], wv_rows[h][:, :, u * D // 2:(u + 1) * D // 2])
 
         warm = sb.tile([P, 1], F32, name="warm")
         warm_out = sb.tile([P, 1], F32, name="warm_out")
@@ -132,14 +157,17 @@ def tile_attend_gml_nce_kernel(tc, xT, wd, wv, y, cw, rw, offs, out):
 
         g_codes = sb.tile([P, V_PASSES, N], U32, name="g_codes", align_bytes=64)
         g_scales = sb.tile([P, V_PASSES, N], U8, name="g_scales", align_bytes=64)
+        nc.gpsimd.memset(g_codes[:, 1, DIRECT:N], 0)
+        nc.gpsimd.memset(g_scales[:, 1, DIRECT:N], 0)
         wd_codes = {}
         wd_bf = {0: sb.tile([P, PACK, P, PACK], BF16, name="wd_bf0", align_bytes=64)}
         for t in range(PACK):
             wd_codes[0, t] = line.tile([P, P], U32, name="wd_codes0_%d" % t, tag="wd_line", align_bytes=64)
         wd_bf[1] = line.tile([P, PACK, P, PACK], BF16, name="wd_bf1", tag="wd_line", align_bytes=64)
-        for t in range(PACK):
-            wd_codes[1, t] = sb.tile([P, P], U32, name="wd_codes1_%d" % t, align_bytes=64)
-        sig = [sb.tile([P, PACK, N], F32, name="sig%d" % h) for h in range(V_PASSES)]
+        sig = [sb.tile([P, PACK, N], F32, name="sig0")]
+        sig1 = {}
+        codes1 = {}
+        scales1 = [sb.tile([P, 2, P], U8, name="wd_scales1_%d" % k, align_bytes=64) for k in range(2)]
         diff = [sb.tile([P, PACK, (N, DIRECT)[h]], F32, name="diff%d" % h) for h in range(V_PASSES)]
 
         def cast_wd(copy, h, t0, ms, m0=0):
@@ -157,129 +185,191 @@ def tile_attend_gml_nce_kernel(tc, xT, wd, wv, y, cw, rw, offs, out):
                                     rhs=x_codes[:].bitcast(E4M3), rhs_scale=x_scales[:], start=True, stop=True)
                 nc.scalar.activation(sig[h][:, t, :], a_bank[:], ACT.Sigmoid, scale=(1.0, -1.0)[h])
 
+        def quantise_wd1(k):
+            codes1[k] = vline.tile([P, 2, P], U32, name="wd_codes1_%d" % k, tag="vline", align_bytes=64)
+            nc.vector.quantize_mx(out=codes1[k][:].rearrange("p t m -> p (t m)").bitcast(E4M3),
+                                  scales=scales1[k][:].rearrange("p t m -> p (t m)"),
+                                  in_=wd_bf[1][:, 2 * k:2 * k + 2].rearrange("p t m j -> p (t m j)"))
+
+        def logits_second(u, k):
+            a_bank = bank("a_bank")
+            for e in range(2):
+                nc.tensor.matmul_mx(out=a_bank[:, halves[e]], lhsT=codes1[k][:, e, :].bitcast(E4M3), lhsT_scale=scales1[k][:, e, :],
+                                    rhs=x_codes[:, halves[u]].bitcast(E4M3), rhs_scale=x_scales[:, halves[u]], start=True, stop=True)
+            sig1[u, k] = late.tile([P, 2, half], F32, name="sig1_%d_%d" % (u, k), tag="late", align_bytes=64)
+            nc.scalar.activation(sig1[u, k][:].rearrange("p t n -> p (t n)"), a_bank[:], ACT.Sigmoid, scale=-1.0)
+
         def subtract_labels(h, ts):
             for t in ts:
                 for ns in ([slice(0, P), slice(P, N)] if t == PACK - 1 else [slice(0, N)]):
                     nc.vector.tensor_tensor(diff[h][:, t, ns], sig[h][:, t, ns], y_sb[h][:, t, ns], ALU.subtract)
 
-        g_bf = [sb.tile([P, (N, DIRECT)[h], PACK], BF16, name="g_bf%d" % h, align_bytes=64) for h in range(V_PASSES)]
+        g_bf = {}
 
-        def add_labels(t, ns):
-            nc.vector.scalar_tensor_tensor(diff[1][:, t, ns], y_sb[1][:, t, ns], -1.0, sig[1][:, t, ns], ALU.add, ALU.add)
+        def add_labels(k):
+            ts = slice(2 * k, 2 * k + 2)
+            nc.vector.scalar_tensor_tensor(diff[1][:, ts, :], y1[0][:, ts, :], -1.0, sig1[0, k][:], ALU.add, ALU.add)
 
         def turn_and_add():
             sums = {q: bank("sum_bank") for q in TURNED}
-            for q in TURNED:
-                for t in range(PACK):
-                    nc.tensor.matmul(sums[q][:, place(t)], lhsT=y_sb[1][:, t, q * P:(q + 1) * P], rhs=ident[:], is_transpose=True,
-                                     start=t == 0, stop=False)
-            for t in range(PACK):
-                for q in TURNED:
-                    nc.tensor.matmul(sums[q][:, place(t)], lhsT=sig[1][:, t, q * P:(q + 1) * P], rhs=ident[:], is_transpose=True,
-                                     start=False, stop=t == PACK - 1)
+            blocks = {q: slice(q * P - DIRECT, (q + 1) * P - DIRECT) for q in TURNED}
+            labels = [(q, t, y1[1][:, t, blocks[q]]) for q in TURNED for t in range(PACK)]
+            sigmoids = [(q, t, sig1[1, t // 2][:, t % 2, blocks[q]]) for t in range(PACK) for q in TURNED]
+            first, second = (labels, sigmoids) if Y_FIRST else (sigmoids, labels)
+            for q, t, part in first:
+                nc.tensor.matmul(sums[q][:, place(t)], lhsT=part, rhs=ident[:], is_transpose=True, start=t == 0, stop=False)
+            for q, t, part in second:
+                nc.tensor.matmul(sums[q][:, place(t)], lhsT=part, rhs=ident[:], is_transpose=True, start=False, stop=t == PACK - 1)
             return sums
 
-        g_words = {}
+        g_turned = {}
 
         def weigh_turned(sums, q):
-            g_turned = sb.tile([P, 2 * P, 2], BF16, name="g_turned%d" % q, align_bytes=64)
-            nc.vector.scalar_tensor_tensor(g_turned[:], by_words(sums[q]), -1.0, weight_turned[q][:], ALU.add, ALU.mult)
-            words = g_turned[:].rearrange("p k e -> p (k e)").bitcast(F32)
+            g_turned[q] = ahead.tile([P, 2 * P, 2], BF16, name="g_turned%d" % q, tag="ahead", align_bytes=64)
+            nc.vector.scalar_tensor_tensor(g_turned[q][:], by_words(sums[q]), -1.0, weight_turned[q][:], ALU.add, ALU.mult)
+
+        def turn_back():
             word_bank = bank("word_bank")
-            for u in range(2):
-                nc.tensor.transpose(word_bank[:, u * P:(u + 1) * P], words[:, u * P:(u + 1) * P], ident[:])
-            g_words[q] = sb.tile([P, P, 2], F32, name="g_words%d" % q, align_bytes=64)
-            nc.scalar.copy(g_words[q][:], word_bank[:, 0:2 * P].rearrange("p (u i) -> p i u", u=2))
+            for a, q in enumerate(TURNED):
+                words = g_turned[q][:].rearrange("p k e -> p (k e)").bitcast(F32)
+                for u in range(2):
+                    nc.tensor.transpose(word_bank[:, (2 * a + u) * P:(2 * a + u + 1) * P], words[:, u * P:(u + 1) * P], ident[:])
+            g_words = late.tile([P, len(TURNED), P, 2], F32, name="g_words", tag="late", align_bytes=64)
+            nc.scalar.copy(g_words[:], word_bank[:].rearrange("p (a u i) -> p a i u", a=len(TURNED), u=2))
+            return g_words
 
-        def quantise_turned(q):
-            nc.vector.quantize_mx(out=g_codes[:, 1, q * P:(q + 1) * P].bitcast(E5M2), scales=g_scales[:, 1, q * P:(q + 1) * P],
-                                  in_=g_words[q][:].rearrange("p i u -> p (i u)").bitcast(BF16))
+        def quantise_turned(g_words):
+            nc.vector.quantize_mx(out=g_codes[:, 1, DIRECT:N].bitcast(E5M2), scales=g_scales[:, 1, DIRECT:N],
+                                  in_=g_words[:].rearrange("p a i u -> p (a i u)").bitcast(BF16))
 
-        def weigh(h, cuts):
-            g_dst = g_bf[h][:].rearrange("p (c i) t -> p c t i", i=2)
+        def weigh(h, q):
+            if h == 0:
+                g_bf[h, q] = vline.tile([P, P, PACK], BF16, name="g_bf%d_%d" % (h, q), tag="vline", align_bytes=64)[:]
+            else:
+                if q == 0:
+                    g_bf[h] = sb.tile([P, DIRECT, PACK], BF16, name="g_bf1", align_bytes=64)
+                g_bf[h, q] = g_bf[h][:, q * P:(q + 1) * P]
+            cs = slice(q * P // 2, (q + 1) * P // 2)
+            g_dst = g_bf[h, q].rearrange("p (c i) t -> p c t i", i=2)
             g_src = diff[h][:].rearrange("p t (c i) -> p c t i", i=2)
             g_weight = weight[h][:].rearrange("p t (c i) -> p c t i", i=2)
-            for n0, n1 in zip(cuts, cuts[1:]):
-                cs = slice(n0 // 2, n1 // 2)
-                nc.vector.tensor_tensor(g_dst[:, cs], g_src[:, cs], g_weight[:, cs], ALU.mult)
+            nc.vector.tensor_tensor(g_dst, g_src[:, cs], g_weight[:, cs], ALU.mult)
 
-        def quantise_g(h, n0, n1):
+        def quantise_g(h, n0, n1, values):
             nc.vector.quantize_mx(out=g_codes[:, h, n0:n1].bitcast(E5M2), scales=g_scales[:, h, n0:n1],
-                                  in_=g_bf[h][:, n0:n1].rearrange("p n t -> p (n t)"))
+                                  in_=values.rearrange("p n t -> p (n t)"))
 
-        wv_codes = sb.tile([P, D_TILES, V_PASSES, P], U32, name="wv_codes", align_bytes=64)
+        wv_codes = {}
         wv_scales = sb.tile([P, D_TILES, V_PASSES, P], U8, name="wv_scales", align_bytes=64)
-        dx_banks = {}
+        wv_bf = {}
 
-        wv_bf = [sb.tile([P, V_PASSES, P, PACK], BF16, name="wv_bf%d" % b, align_bytes=64) for b in range(D_TILES)]
+        def cast_wv(b, hs=range(V_PASSES)):
+            for h in hs:
+                if h == 0:
+                    wv_bf[b] = late.tile([P, V_PASSES, P, PACK], BF16, name="wv_bf%d" % b, tag="late", align_bytes=64)
+                nc.scalar.copy(wv_bf[b][:, h].rearrange("p (c i) j -> p c j i", i=LINE),
+                               wv_raw[h][b // 2][:, :, b % 2 * P:(b % 2 + 1) * P].rearrange("p j (c i) -> p c j i", i=LINE))
 
-        def cast_wv(copy, b):
-            for h in range(V_PASSES):
-                copy(wv_bf[b][:, h].rearrange("p (c i) j -> p c j i", i=LINE),
-                     wv_raw[h][b // 2][:, :, b % 2 * P:(b % 2 + 1) * P].rearrange("p j (c i) -> p c j i", i=LINE))
+        def quantise_wv(b, h0=0, h1=V_PASSES):
+            if b == 0:
+                wv_tile = ahead.tile([P, h1 - h0, P], U32, name="wv_codes%d_%d" % (b, h0), tag="ahead", align_bytes=64)
+            else:
+                wv_tile = sb.tile([P, h1 - h0, P], U32, name="wv_codes%d" % b, align_bytes=64)
+            for h in range(h0, h1):
+                wv_codes[b, h] = wv_tile[:, h - h0, :]
+            nc.vector.quantize_mx(out=wv_tile[:].rearrange("p h m -> p (h m)").bitcast(E4M3),
+                                  scales=wv_scales[:, b, h0:h1].rearrange("p h m -> p (h m)"),
+                                  in_=wv_bf[b][:, h0:h1].rearrange("p h m j -> p (h m j)"))
 
-        def quantise_wv(b):
-            nc.vector.quantize_mx(out=wv_codes[:, b].rearrange("p h m -> p (h m)").bitcast(E4M3),
-                                  scales=wv_scales[:, b].rearrange("p h m -> p (h m)"),
-                                  in_=wv_bf[b][:].rearrange("p h m j -> p (h m j)"))
+        def dx_product(b, dx_bank=None, hs=range(V_PASSES)):
+            if dx_bank is None:
+                dx_bank = bank("dx_bank")
+            for h in hs:
+                nc.tensor.matmul_mx(out=dx_bank[:], lhsT=wv_codes[b, h].bitcast(E4M3),
+                                    lhsT_scale=wv_scales[:, b, h, :],
+                                    rhs=g_codes[:, h, :].bitcast(E5M2), rhs_scale=g_scales[:, h, :],
+                                    start=h == 0, stop=h == V_PASSES - 1)
+            return dx_bank
 
-        def dx_pass(b, h):
-            first = h == (0 if b == 0 else V_PASSES - 1)
-            if first:
-                dx_banks[b] = bank("dx_bank")
-            nc.tensor.matmul_mx(out=dx_banks[b][:], lhsT=wv_codes[:, b, h, :].bitcast(E4M3),
-                                lhsT_scale=wv_scales[:, b, h, :],
-                                rhs=g_codes[:, h, :].bitcast(E5M2), rhs_scale=g_scales[:, h, :],
-                                start=first, stop=not first)
+        def copy_dx(dx_bank, b, ns):
+            dx = late.tile([P, ns.stop - ns.start], F32, name="dx%d_%d" % (b, ns.start), tag="late", align_bytes=64)
+            nc.scalar.copy(dx[:], dx_bank[:, ns])
+            return dx
 
-        def scatter(b, ns):
-            dx = late.tile([P, ns.stop - ns.start], F32, name="dx%d_%d" % (b, ns.start), tag="dx", align_bytes=64)
-            nc.scalar.copy(dx[:], dx_banks[b][:, ns])
-            nc.vector.tensor_copy(windows[b % len(windows)][:].indirect(offsets[:, ns.start // 16:ns.stop // 16]), dx[:])
+        def scatter(dx, b, ns):
+            nc.vector.tensor_copy(windows[b][:].indirect(offsets[:, ns.start // 16:ns.stop // 16]), dx[:])
             if ns.stop == N:
-                nc.sync.dma_start(out[b * P:(b + 1) * P, :], windows[b % len(windows)][:])
+                nc.sync.dma_start(out[b * P:(b + 1) * P, :], windows[b][:])
 
         for t0 in (0, 2):
-            cast_wd(nc.vector.tensor_copy, 0, t0, slice(0, 80))
-            cast_wd(nc.scalar.copy, 0, t0, slice(80, P))
+            cast_wd(nc.vector.tensor_copy, 0, t0, slice(0, WD0_VECTOR))
+            cast_wd(nc.scalar.copy, 0, t0, slice(WD0_VECTOR, P))
         logits(0)
-        for t0 in (0, 2):
-            cast_wd(nc.vector.tensor_copy, 1, t0, slice(0, 48))
-        subtract_labels(0, range(PACK))
-        for t0 in (0, 2):
-            cast_wd(nc.scalar.copy, 1, t0, slice(48, P), 48)
-        logits(1)
-        weigh(0, (0, 128, 256, 384, 512))
-        quantise_g(0, 0, half)
-        add_labels(0, slice(0, DIRECT))
-        quantise_g(0, half, N)
-        for t in (1, 2):
-            add_labels(t, slice(0, DIRECT))
-        add_labels(3, slice(0, P))
-        add_labels(3, slice(P, DIRECT))
+        if WD1_EARLY:
+            for t0 in (0, 2):
+                cast_wd(nc.vector.tensor_copy, 1, t0, slice(0, WD1_EARLY))
+        late_cut = max(WD1_EARLY, WD1_VECTOR)
+        subtract_labels(0, range(PACK - 1))
+        if WD1_VECTOR > WD1_EARLY:
+            for t0 in (0, 2):
+                cast_wd(nc.vector.tensor_copy, 1, t0, slice(WD1_EARLY, WD1_VECTOR), WD1_EARLY)
+        subtract_labels(0, [PACK - 1])
+        if late_cut < P:
+            for t0 in (0, 2):
+                cast_wd(nc.scalar.copy, 1, t0, slice(late_cut, P), WD1_EARLY)
+        for step in V_ORDER:
+            if step == "q":
+                quantise_wd1(len(codes1))
+                logits_second(0, len(codes1) - 1)
+            else:
+                weigh(0, "abcd".index(step))
+        if S_ORDER == "BW":
+            logits_second(1, 0)
+            logits_second(1, 1)
+            cast_wv(0)
+        elif S_ORDER == "WB":
+            cast_wv(0)
+            logits_second(1, 0)
+            logits_second(1, 1)
+        elif S_ORDER == "wBw":
+            cast_wv(0, [0])
+            logits_second(1, 0)
+            logits_second(1, 1)
+            cast_wv(0, [1])
+        for q in range(2):
+            quantise_g(0, q * P, (q + 1) * P, g_bf[0, q])
+        add_labels(0)
+        quantise_g(0, 2 * P, 3 * P, g_bf[0, 2])
+        add_labels(1)
+        quantise_g(0, 3 * P, 4 * P, g_bf[0, 3])
         sums = turn_and_add()
+        weigh(1, 0)
+        if SPLIT_WV0:
+            quantise_wv(0, 0, 1)
+            early0 = dx_product(0, None, [0])
+            weigh(1, 1)
+            quantise_wv(0, 1, 2)
+            quantise_g(1, 0, DIRECT, g_bf[1][:])
+            dx_product(0, early0, [1])
+        else:
+            weigh(1, 1)
+            quantise_wv(0)
+            quantise_g(1, 0, DIRECT, g_bf[1][:])
+            early0 = dx_product(0)
         for q in TURNED:
             weigh_turned(sums, q)
-        weigh(1, (0, 128, 256))
-        cast_wv(nc.scalar.copy, 0)
-        quantise_wv(0)
-        dx_pass(0, 0)
-        weigh(1, (DIRECT - P, DIRECT))
-        quantise_g(1, 0, 256)
-        quantise_turned(3)
-        quantise_g(1, 256, 384)
-        dx_pass(0, 1)
-        for b in range(1, D_TILES - 1):
-            cast_wv(nc.scalar.copy, b)
+        cast_wv(1)
         quantise_wv(1)
-        cast_wv(nc.vector.tensor_copy, D_TILES - 1)
-        for b in range(2, D_TILES):
-            quantise_wv(b)
-        for b in range(1, D_TILES):
-            for h in reversed(range(V_PASSES)):
-                dx_pass(b, h)
-        for ns in halves:
-            for b in range(2):
-                scatter(b, ns)
-        for b in range(2, D_TILES):
-            scatter(b, slice(0, N))
+        dx_early0 = copy_dx(early0, 0, halves[0])
+        g_words = turn_back()
+        early1 = dx_product(1)
+        scatter(dx_early0, 0, halves[0])
+        quantise_turned(g_words)
+        scatter(copy_dx(early1, 1, halves[0]), 1, halves[0])
+        final = [dx_product(b) for b in range(EARLY_TILES)]
+        for b in range(EARLY_TILES):
+            cast_wv(EARLY_TILES + b)
+            quantise_wv(EARLY_TILES + b)
+            scatter(copy_dx(final[b], b, halves[1]), b, halves[1])
+        for b in range(EARLY_TILES, D_TILES):
+            scatter(copy_dx(dx_product(b), b, slice(0, N)), b, slice(0, N))

@@ -22,31 +22,39 @@ PASS = P * PACK
 V_PASSES = V // PASS
 D_TILES = D // P
 LINE = 4
-DIRECT = 256
+HALF = N // 2
+BLOCKS = HALF // P
 EARLY_TILES = 2
-WD0_VECTOR = 80
-WD1_EARLY = 48
-WD1_VECTOR = 48
-LOADS = ("wd0", "wd1a", "y0_02", "y0_24", "wd1b", "y1", "wv0", "wv1")
-Y_FIRST = True
-S_ORDER = "wBw"
-V_ORDER = "aqbqcd"
-SPLIT_WV0 = True
-TURNED = range(DIRECT // P, N // P)
+WD0_VECTOR = 128
+WD1_EARLY = 64
+S_BUFS = 23
+V_BUFS = 16
+LOADS = ("wd0", "wd1a", "y0_02", "y0_23", "wd1b", "y0_34", "y1", "wv0", "wv1")
+Y_FIRST = (True, True)
+TURN0 = False
+FULL = (True, True)
+TAIL = "s0 s1 w1 v1 x0 b p1 A0 g x1 A1 f0 f1 w2 v2 B0 w3 v3 B1"
+ORDER = "A0 A1 Va0 Va1 Sb0 Sb1 d0 d1 q0 a0 q1 a1 a2 a3 g C0 C1 U w0 w1 e0 e1 G m0 m1 v0 h v1"
 
 
 def tile_attend_gml_nce_kernel(tc, xT, wd, wv, y, cw, rw, offs, out):
     nc = tc.nc
     with ExitStack() as ctx:
         sb = ctx.enter_context(tc.tile_pool(name="sb", bufs=1))
-        line = ctx.enter_context(tc.tile_pool(name="line", bufs=PACK + 1))
-        late = ctx.enter_context(tc.tile_pool(name="late", bufs=15))
-        vline = ctx.enter_context(tc.tile_pool(name="vline", bufs=6))
-        ahead = ctx.enter_context(tc.tile_pool(name="ahead", bufs=4))
+        sline = ctx.enter_context(tc.tile_pool(name="sline", bufs=S_BUFS))
+        vline = ctx.enter_context(tc.tile_pool(name="vline", bufs=V_BUFS))
         psum = ctx.enter_context(tc.psum_pool(name="psum", bufs=8))
 
         def bank(name):
             return psum.tile([P, N], F32, name=name, tag="bank")
+
+        def scalar_tile(shape, dtype, name):
+            return sline.tile(shape, dtype, name=name, tag="sline", align_bytes=64)
+
+        def vector_tile(shape, dtype, name):
+            return vline.tile(shape, dtype, name=name, tag="vline", align_bytes=64)
+
+        halves = [slice(0, HALF), slice(HALF, N)]
 
         offsets = sb.tile([P, N // 16], U16, name="offsets")
         x_planes = [sb.tile([P, T], F32, name="x_plane%d" % j) for j in range(PACK)]
@@ -57,12 +65,16 @@ def tile_attend_gml_nce_kernel(tc, xT, wd, wv, y, cw, rw, offs, out):
             nc.sync.dma_start(wd_raw[h, m0][:], wd_rows[:, :, h * PASS + m0 * PACK:h * PASS + m1 * PACK])
 
         wv_raw = [[sb.tile([P, PACK, D // 2], F32, name="wv_raw%d_%d" % (h, u)) for u in range(2)] for h in range(V_PASSES)]
-        y_sb = [sb.tile([P, PACK, N], F32, name="y_sb0")]
-        if "y1" in LOADS:
-            y_whole = sb.tile([P, PACK, N], F32, name="y_sb1")
-            y1 = [y_whole[:, :, 0:DIRECT], y_whole[:, :, DIRECT:N]]
-        else:
-            y1 = [sb.tile([P, PACK, DIRECT], F32, name="y1_%d" % u)[:] for u in range(2)]
+        y_whole = {}
+        y_sb = {}
+        for h in range(V_PASSES):
+            if "y%da" % h in LOADS:
+                for u in range(2):
+                    y_sb[h, u] = sb.tile([P, PACK, HALF], F32, name="y%d_%d" % (h, u))[:]
+            else:
+                y_whole[h] = sb.tile([P, PACK, N], F32, name="y_sb%d" % h)
+                for u in range(2):
+                    y_sb[h, u] = y_whole[h][:, :, halves[u]]
         cw_sb = sb.tile([P, V_PASSES, PACK], F32, name="cw_sb")
         rw_sb = sb.tile([P, LINE], F32, name="rw_sb")
 
@@ -84,18 +96,18 @@ def tile_attend_gml_nce_kernel(tc, xT, wd, wv, y, cw, rw, offs, out):
                 load_wd(1, 0, WD1_EARLY)
             elif what == "wd1b":
                 load_wd(1, WD1_EARLY, P)
-            elif what.startswith("y0"):
-                ts = slice(int(what[3]), int(what[4]))
-                nc.sync.dma_start(y_sb[0][:, ts, :], y_rows[0][:, ts, :])
-            elif what == "y1":
-                nc.sync.dma_start(y_whole[:], y_rows[1])
-            elif what.startswith("y1"):
-                u = "ab".index(what[2])
-                nc.sync.dma_start(y1[u], y_rows[1][:, :, u * DIRECT:(u + 1) * DIRECT])
-            else:
+            elif what.startswith("wv"):
                 u = int(what[2])
                 for h in range(V_PASSES):
                     nc.sync.dma_start(wv_raw[h][u][:], wv_rows[h][:, :, u * D // 2:(u + 1) * D // 2])
+            elif len(what) == 5:
+                h, ts = int(what[1]), slice(int(what[3]), int(what[4]))
+                nc.sync.dma_start(y_whole[h][:, ts, :], y_rows[h][:, ts, :])
+            elif len(what) == 2:
+                nc.sync.dma_start(y_whole[int(what[1])][:], y_rows[int(what[1])])
+            else:
+                h, u = int(what[1]), "ab".index(what[2])
+                nc.sync.dma_start(y_sb[h, u], y_rows[h][:, :, halves[u]])
 
         warm = sb.tile([P, 1], F32, name="warm")
         warm_out = sb.tile([P, 1], F32, name="warm_out")
@@ -107,19 +119,26 @@ def tile_attend_gml_nce_kernel(tc, xT, wd, wv, y, cw, rw, offs, out):
         rw_bank = bank("rw_bank")
         for i in range(LINE):
             nc.tensor.transpose(rw_bank[:, i * P:(i + 1) * P], rw_sb[:, i:i + 1].to_broadcast([P, P]), ident[:])
-        minus_rw = sb.tile([P, N], F32, name="minus_rw")
-        nc.scalar.activation(minus_rw[:].rearrange("p (c i) -> p c i", i=LINE), rw_bank[:].rearrange("p (i c) -> p c i", i=LINE), ACT.Copy, scale=-1.0)
-        weight = [sb.tile([P, PACK, N], F32, name="weight0"), sb.tile([P, PACK, DIRECT], F32, name="weight1")]
-        for j in range(PACK):
-            nc.scalar.activation(weight[0][:, j, :].rearrange("p (c i) -> p c i", i=LINE), rw_bank[:].rearrange("p (i c) -> p c i", i=LINE),
-                                 ACT.Copy, scale=cw_sb[:, 0, j:j + 1])
-        for j in range(PACK):
-            nc.scalar.activation(weight[1][:, j, :], minus_rw[:, 0:DIRECT], ACT.Copy, scale=cw_sb[:, 1, j:j + 1])
+        rw_spread = rw_bank[:].rearrange("p (i c) -> p c i", i=LINE)
+        rw_late = sb.tile([P, HALF], F32, name="rw_late")
+        nc.scalar.copy(rw_late[:].rearrange("p (c i) -> p c i", i=LINE), rw_spread[:, HALF // LINE:N // LINE, :])
         column_bank = bank("column_bank")
-        for q in TURNED:
-            nc.tensor.transpose(column_bank[:, q * P:(q + 1) * P], minus_rw[:, q * P:(q + 1) * P], ident[:])
-        minus_rw_column = sb.tile([P, len(TURNED)], F32, name="minus_rw_column")
-        nc.scalar.copy(minus_rw_column[:], column_bank[:, DIRECT:N:P])
+        for q in range(BLOCKS):
+            nc.tensor.transpose(column_bank[:, q * P:(q + 1) * P], rw_late[:, q * P:(q + 1) * P], ident[:])
+        turned = (TURN0, True)
+        direct = [HALF if turned[h] else N for h in range(V_PASSES)]
+        flipped = [FULL[h] and turned[h] for h in range(V_PASSES)]
+        weight = [sb.tile([P, PACK, direct[h]], F32, name="weight%d" % h) for h in range(V_PASSES)]
+        minus_rw_column = sb.tile([P, BLOCKS], F32, name="minus_rw_column")
+        minus_cw = sb.tile([P, V_PASSES, PACK], F32, name="minus_cw")
+        if any(flipped):
+            nc.scalar.activation(minus_cw[:], cw_sb[:], ACT.Copy, scale=-1.0)
+        for h in range(V_PASSES):
+            for j in range(PACK):
+                nc.scalar.activation(weight[h][:, j, :].rearrange("p (c i) -> p c i", i=LINE), rw_spread[:, 0:direct[h] // LINE, :],
+                                     ACT.Copy, scale=(minus_cw if flipped[h] else cw_sb)[:, h, j:j + 1])
+            if h == 0:
+                nc.scalar.activation(minus_rw_column[:], column_bank[:, 0:HALF:P], ACT.Copy, scale=-1.0)
 
         def place(t):
             return slice((t % 2 * 2 + t // 2) * P, (t % 2 * 2 + t // 2 + 1) * P)
@@ -127,13 +146,16 @@ def tile_attend_gml_nce_kernel(tc, xT, wd, wv, y, cw, rw, offs, out):
         def by_words(full_bank):
             return full_bank[:].rearrange("p (e k) -> p k e", e=2)
 
-        cw_bank = bank("cw_bank")
-        for t in range(PACK):
-            nc.tensor.transpose(cw_bank[:, place(t)], cw_sb[:, 1, t:t + 1].to_broadcast([P, P]), ident[:])
         weight_turned = {}
-        for q in TURNED:
-            weight_turned[q] = sb.tile([P, 2 * P, 2], F32, name="weight_turned%d" % q)
-            nc.scalar.activation(weight_turned[q][:], by_words(cw_bank), ACT.Copy, scale=minus_rw_column[:, q - TURNED[0]:q - TURNED[0] + 1])
+        for h in range(V_PASSES):
+            if not turned[h]:
+                continue
+            cw_bank = bank("cw_bank")
+            for t in range(PACK):
+                nc.tensor.transpose(cw_bank[:, place(t)], cw_sb[:, h, t:t + 1].to_broadcast([P, P]), ident[:])
+            for q in range(BLOCKS):
+                weight_turned[h, q] = scalar_tile([P, 2 * P, 2], F32, "weight_turned%d_%d" % (h, q))
+                nc.scalar.activation(weight_turned[h, q][:], by_words(cw_bank), ACT.Copy, scale=minus_rw_column[:, q:q + 1])
 
         windows = [sb.tile([P, T], F32, name="window%d" % b) for b in range(D_TILES)]
         nc.vector.memset(windows[0][:], 0.0)
@@ -144,9 +166,7 @@ def tile_attend_gml_nce_kernel(tc, xT, wd, wv, y, cw, rw, offs, out):
         x_bf = sb.tile([P, N, PACK], BF16, name="x_bf", align_bytes=64)
         x_codes = sb.tile([P, N], U32, name="x_codes", align_bytes=64)
         x_scales = sb.tile([P, N], U8, name="x_scales", align_bytes=64)
-        half = N // 2
-        halves = [slice(0, half), slice(half, N)]
-        offset_halves = [offsets[:, 0:half // 16], offsets[:, half // 16:N // 16]]
+        offset_halves = [offsets[:, 0:HALF // 16], offsets[:, HALF // 16:N // 16]]
         for j in range(PACK - 1):
             nc.vector.tensor_copy(x_bf[:, :, j], x_planes[j][:].indirect(offsets[:]))
         for u in range(2):
@@ -157,122 +177,108 @@ def tile_attend_gml_nce_kernel(tc, xT, wd, wv, y, cw, rw, offs, out):
 
         g_codes = sb.tile([P, V_PASSES, N], U32, name="g_codes", align_bytes=64)
         g_scales = sb.tile([P, V_PASSES, N], U8, name="g_scales", align_bytes=64)
-        nc.gpsimd.memset(g_codes[:, 1, DIRECT:N], 0)
-        nc.gpsimd.memset(g_scales[:, 1, DIRECT:N], 0)
-        wd_codes = {}
-        wd_bf = {0: sb.tile([P, PACK, P, PACK], BF16, name="wd_bf0", align_bytes=64)}
-        for t in range(PACK):
-            wd_codes[0, t] = line.tile([P, P], U32, name="wd_codes0_%d" % t, tag="wd_line", align_bytes=64)
-        wd_bf[1] = line.tile([P, PACK, P, PACK], BF16, name="wd_bf1", tag="wd_line", align_bytes=64)
-        sig = [sb.tile([P, PACK, N], F32, name="sig0")]
-        sig1 = {}
-        codes1 = {}
-        scales1 = [sb.tile([P, 2, P], U8, name="wd_scales1_%d" % k, align_bytes=64) for k in range(2)]
-        diff = [sb.tile([P, PACK, (N, DIRECT)[h]], F32, name="diff%d" % h) for h in range(V_PASSES)]
+        nc.gpsimd.memset(g_codes[:, 1, halves[1]], 0)
+        nc.gpsimd.memset(g_scales[:, 1, halves[1]], 0)
+        wd_bf, wd_codes, sig, g_bf, g_turned, g_words, wv_bf, wv_codes = {}, {}, {}, {}, {}, {}, {}, {}
+        wd_scales = {(h, k): sb.tile([P, 2, P], U8, name="wd_scales%d_%d" % (h, k), align_bytes=64) for h in range(V_PASSES) for k in range(2)}
+        diff = [sb.tile([P, PACK, direct[h]], F32, name="diff%d" % h) for h in range(V_PASSES)]
 
-        def cast_wd(copy, h, t0, ms, m0=0):
+        def cast_wd(copy, new_tile, h, k, ms, m0=0):
+            if (h, k) not in wd_bf:
+                wd_bf[h, k] = new_tile([P, 2, P, PACK], BF16, "wd_bf%d_%d" % (h, k))
             src = wd_raw[h, m0][:].rearrange("p j (m t) -> p m j t", t=PACK)
-            dst = wd_bf[h][:].rearrange("p t m j -> p m j t")
-            copy(dst[:, ms, :, t0:t0 + 2], src[:, ms.start - m0:ms.stop - m0, :, t0:t0 + 2])
+            dst = wd_bf[h, k][:].rearrange("p e m j -> p m j e")
+            copy(dst[:, ms], src[:, ms.start - m0:ms.stop - m0, :, 2 * k:2 * k + 2])
 
-        def logits(h):
-            wd_scales = sb.tile([P, PACK, P], U8, name="wd_scales%d" % h, align_bytes=64)
-            for t in range(PACK):
-                nc.vector.quantize_mx(out=wd_codes[h, t][:].bitcast(E4M3), scales=wd_scales[:, t, :],
-                                      in_=wd_bf[h][:, t].rearrange("p m j -> p (m j)"))
-                a_bank = bank("a_bank")
-                nc.tensor.matmul_mx(out=a_bank[:], lhsT=wd_codes[h, t][:].bitcast(E4M3), lhsT_scale=wd_scales[:, t, :],
-                                    rhs=x_codes[:].bitcast(E4M3), rhs_scale=x_scales[:], start=True, stop=True)
-                nc.scalar.activation(sig[h][:, t, :], a_bank[:], ACT.Sigmoid, scale=(1.0, -1.0)[h])
+        def quantise_wd(h, k):
+            wd_codes[h, k] = vector_tile([P, 2, P], U32, "wd_codes%d_%d" % (h, k))
+            for es in ([slice(0, 1), slice(1, 2)] if (h, k) == (0, 0) else [slice(0, 2)]):
+                nc.vector.quantize_mx(out=wd_codes[h, k][:, es].rearrange("p e m -> p (e m)").bitcast(E4M3),
+                                      scales=wd_scales[h, k][:, es].rearrange("p e m -> p (e m)"),
+                                      in_=wd_bf[h, k][:, es].rearrange("p e m j -> p (e m j)"))
 
-        def quantise_wd1(k):
-            codes1[k] = vline.tile([P, 2, P], U32, name="wd_codes1_%d" % k, tag="vline", align_bytes=64)
-            nc.vector.quantize_mx(out=codes1[k][:].rearrange("p t m -> p (t m)").bitcast(E4M3),
-                                  scales=scales1[k][:].rearrange("p t m -> p (t m)"),
-                                  in_=wd_bf[1][:, 2 * k:2 * k + 2].rearrange("p t m j -> p (t m j)"))
-
-        def logits_second(u, k):
+        def logits(h, u, k):
+            if FULL[h]:
+                for e in range(2 if u == 0 else 0):
+                    a_bank = bank("a_bank")
+                    nc.tensor.matmul_mx(out=a_bank[:], lhsT=wd_codes[h, k][:, e, :].bitcast(E4M3), lhsT_scale=wd_scales[h, k][:, e, :],
+                                        rhs=x_codes[:].bitcast(E4M3), rhs_scale=x_scales[:], start=True, stop=True)
+                    whole = scalar_tile([P, N], F32, "sig%d_%d" % (h, 2 * k + e))
+                    nc.scalar.activation(whole[:], a_bank[:], ACT.Sigmoid, scale=-1.0 if flipped[h] else 1.0)
+                    sig[h, 2 * k + e] = whole[:]
+                    sig[h, 1, 2 * k + e] = whole[:, halves[1]]
+                return
             a_bank = bank("a_bank")
             for e in range(2):
-                nc.tensor.matmul_mx(out=a_bank[:, halves[e]], lhsT=codes1[k][:, e, :].bitcast(E4M3), lhsT_scale=scales1[k][:, e, :],
+                nc.tensor.matmul_mx(out=a_bank[:, halves[e]], lhsT=wd_codes[h, k][:, e, :].bitcast(E4M3), lhsT_scale=wd_scales[h, k][:, e, :],
                                     rhs=x_codes[:, halves[u]].bitcast(E4M3), rhs_scale=x_scales[:, halves[u]], start=True, stop=True)
-            sig1[u, k] = late.tile([P, 2, half], F32, name="sig1_%d_%d" % (u, k), tag="late", align_bytes=64)
-            nc.scalar.activation(sig1[u, k][:].rearrange("p t n -> p (t n)"), a_bank[:], ACT.Sigmoid, scale=-1.0)
+            pair = scalar_tile([P, 2, HALF], F32, "sig%d_%d_%d" % (h, u, k))
+            nc.scalar.activation(pair[:].rearrange("p e n -> p (e n)"), a_bank[:], ACT.Sigmoid, scale=-1.0 if u == 1 and turned[h] else 1.0)
+            sig[h, u, "pair", k] = pair[:]
+            for e in range(2):
+                sig[h, u, 2 * k + e] = pair[:, e, :]
 
-        def subtract_labels(h, ts):
-            for t in ts:
-                for ns in ([slice(0, P), slice(P, N)] if t == PACK - 1 else [slice(0, N)]):
-                    nc.vector.tensor_tensor(diff[h][:, t, ns], sig[h][:, t, ns], y_sb[h][:, t, ns], ALU.subtract)
-
-        g_bf = {}
-
-        def add_labels(k):
+        def subtract_labels(h, k, u=0):
             ts = slice(2 * k, 2 * k + 2)
-            nc.vector.scalar_tensor_tensor(diff[1][:, ts, :], y1[0][:, ts, :], -1.0, sig1[0, k][:], ALU.add, ALU.add)
+            if not FULL[h]:
+                nc.vector.tensor_tensor(diff[h][:, ts, halves[u]], sig[h, u, "pair", k], y_sb[h, u][:, ts, :], ALU.subtract)
+                return
+            for t in range(2 * k, 2 * k + 2):
+                if flipped[h]:
+                    nc.vector.scalar_tensor_tensor(diff[h][:, t, :], y_sb[h, 0][:, t, :], -1.0, sig[h, t][:, halves[0]], ALU.add, ALU.add)
+                else:
+                    for ns in ([slice(0, P), slice(P, N)] if t == PACK - 1 else [slice(0, N)]):
+                        nc.vector.tensor_tensor(diff[h][:, t, ns], sig[h, t][:, ns], y_whole[h][:, t, ns], ALU.subtract)
 
-        def turn_and_add():
-            sums = {q: bank("sum_bank") for q in TURNED}
-            blocks = {q: slice(q * P - DIRECT, (q + 1) * P - DIRECT) for q in TURNED}
-            labels = [(q, t, y1[1][:, t, blocks[q]]) for q in TURNED for t in range(PACK)]
-            sigmoids = [(q, t, sig1[1, t // 2][:, t % 2, blocks[q]]) for t in range(PACK) for q in TURNED]
-            first, second = (labels, sigmoids) if Y_FIRST else (sigmoids, labels)
+        def turn_and_add(h):
+            sums = [bank("sum_bank") for q in range(BLOCKS)]
+            labels = [(q, t, y_sb[h, 1][:, t, q * P:(q + 1) * P]) for q in range(BLOCKS) for t in range(PACK)]
+            sigmoids = [(q, t, sig[h, 1, t][:, q * P:(q + 1) * P]) for t in range(PACK) for q in range(BLOCKS)]
+            first, second = (labels, sigmoids) if Y_FIRST[h] else (sigmoids, labels)
             for q, t, part in first:
                 nc.tensor.matmul(sums[q][:, place(t)], lhsT=part, rhs=ident[:], is_transpose=True, start=t == 0, stop=False)
             for q, t, part in second:
                 nc.tensor.matmul(sums[q][:, place(t)], lhsT=part, rhs=ident[:], is_transpose=True, start=False, stop=t == PACK - 1)
             return sums
 
-        g_turned = {}
+        def weigh_turned(sums, h, q):
+            g_turned[h, q] = vector_tile([P, 2 * P, 2], BF16, "g_turned%d_%d" % (h, q))
+            nc.vector.scalar_tensor_tensor(g_turned[h, q][:], by_words(sums[q]), -1.0, weight_turned[h, q][:], ALU.add, ALU.mult)
 
-        def weigh_turned(sums, q):
-            g_turned[q] = ahead.tile([P, 2 * P, 2], BF16, name="g_turned%d" % q, tag="ahead", align_bytes=64)
-            nc.vector.scalar_tensor_tensor(g_turned[q][:], by_words(sums[q]), -1.0, weight_turned[q][:], ALU.add, ALU.mult)
-
-        def turn_back():
+        def turn_back(h):
             word_bank = bank("word_bank")
-            for a, q in enumerate(TURNED):
-                words = g_turned[q][:].rearrange("p k e -> p (k e)").bitcast(F32)
+            for q in range(BLOCKS):
+                words = g_turned[h, q][:].rearrange("p k e -> p (k e)").bitcast(F32)
                 for u in range(2):
-                    nc.tensor.transpose(word_bank[:, (2 * a + u) * P:(2 * a + u + 1) * P], words[:, u * P:(u + 1) * P], ident[:])
-            g_words = late.tile([P, len(TURNED), P, 2], F32, name="g_words", tag="late", align_bytes=64)
-            nc.scalar.copy(g_words[:], word_bank[:].rearrange("p (a u i) -> p a i u", a=len(TURNED), u=2))
-            return g_words
+                    nc.tensor.transpose(word_bank[:, (2 * q + u) * P:(2 * q + u + 1) * P], words[:, u * P:(u + 1) * P], ident[:])
+            g_words[h] = scalar_tile([P, BLOCKS, P, 2], F32, "g_words%d" % h)
+            nc.scalar.copy(g_words[h][:], word_bank[:].rearrange("p (q u i) -> p q i u", q=BLOCKS, u=2))
 
-        def quantise_turned(g_words):
-            nc.vector.quantize_mx(out=g_codes[:, 1, DIRECT:N].bitcast(E5M2), scales=g_scales[:, 1, DIRECT:N],
-                                  in_=g_words[:].rearrange("p a i u -> p (a i u)").bitcast(BF16))
+        def quantise_g(h, u):
+            values = g_bf[h, u][:].rearrange("p n t -> p (n t)") if u == 0 or not turned[h] else g_words[h][:].rearrange("p q i u -> p (q i u)").bitcast(BF16)
+            nc.vector.quantize_mx(out=g_codes[:, h, halves[u]].bitcast(E5M2), scales=g_scales[:, h, halves[u]], in_=values)
 
         def weigh(h, q):
-            if h == 0:
-                g_bf[h, q] = vline.tile([P, P, PACK], BF16, name="g_bf%d_%d" % (h, q), tag="vline", align_bytes=64)[:]
-            else:
-                if q == 0:
-                    g_bf[h] = sb.tile([P, DIRECT, PACK], BF16, name="g_bf1", align_bytes=64)
-                g_bf[h, q] = g_bf[h][:, q * P:(q + 1) * P]
+            if q % 2 == 0:
+                g_bf[h, q // 2] = vector_tile([P, HALF, PACK], BF16, "g_bf%d_%d" % (h, q // 2))
             cs = slice(q * P // 2, (q + 1) * P // 2)
-            g_dst = g_bf[h, q].rearrange("p (c i) t -> p c t i", i=2)
+            g_dst = g_bf[h, q // 2][:, q % 2 * P:(q % 2 + 1) * P].rearrange("p (c i) t -> p c t i", i=2)
             g_src = diff[h][:].rearrange("p t (c i) -> p c t i", i=2)
             g_weight = weight[h][:].rearrange("p t (c i) -> p c t i", i=2)
             nc.vector.tensor_tensor(g_dst, g_src[:, cs], g_weight[:, cs], ALU.mult)
 
-        def quantise_g(h, n0, n1, values):
-            nc.vector.quantize_mx(out=g_codes[:, h, n0:n1].bitcast(E5M2), scales=g_scales[:, h, n0:n1],
-                                  in_=values.rearrange("p n t -> p (n t)"))
-
-        wv_codes = {}
         wv_scales = sb.tile([P, D_TILES, V_PASSES, P], U8, name="wv_scales", align_bytes=64)
-        wv_bf = {}
 
         def cast_wv(b, hs=range(V_PASSES)):
             for h in hs:
                 if h == 0:
-                    wv_bf[b] = late.tile([P, V_PASSES, P, PACK], BF16, name="wv_bf%d" % b, tag="late", align_bytes=64)
+                    wv_bf[b] = scalar_tile([P, V_PASSES, P, PACK], BF16, "wv_bf%d" % b)
                 nc.scalar.copy(wv_bf[b][:, h].rearrange("p (c i) j -> p c j i", i=LINE),
                                wv_raw[h][b // 2][:, :, b % 2 * P:(b % 2 + 1) * P].rearrange("p j (c i) -> p c j i", i=LINE))
 
         def quantise_wv(b, h0=0, h1=V_PASSES):
-            if b == 0:
-                wv_tile = ahead.tile([P, h1 - h0, P], U32, name="wv_codes%d_%d" % (b, h0), tag="ahead", align_bytes=64)
+            if b < EARLY_TILES:
+                wv_tile = vector_tile([P, h1 - h0, P], U32, "wv_codes%d_%d" % (b, h0))
             else:
                 wv_tile = sb.tile([P, h1 - h0, P], U32, name="wv_codes%d" % b, align_bytes=64)
             for h in range(h0, h1):
@@ -292,7 +298,7 @@ def tile_attend_gml_nce_kernel(tc, xT, wd, wv, y, cw, rw, offs, out):
             return dx_bank
 
         def copy_dx(dx_bank, b, ns):
-            dx = late.tile([P, ns.stop - ns.start], F32, name="dx%d_%d" % (b, ns.start), tag="late", align_bytes=64)
+            dx = scalar_tile([P, ns.stop - ns.start], F32, "dx%d_%d" % (b, ns.start))
             nc.scalar.copy(dx[:], dx_bank[:, ns])
             return dx
 
@@ -301,75 +307,81 @@ def tile_attend_gml_nce_kernel(tc, xT, wd, wv, y, cw, rw, offs, out):
             if ns.stop == N:
                 nc.sync.dma_start(out[b * P:(b + 1) * P, :], windows[b][:])
 
-        for t0 in (0, 2):
-            cast_wd(nc.vector.tensor_copy, 0, t0, slice(0, WD0_VECTOR))
-            cast_wd(nc.scalar.copy, 0, t0, slice(WD0_VECTOR, P))
-        logits(0)
-        if WD1_EARLY:
-            for t0 in (0, 2):
-                cast_wd(nc.vector.tensor_copy, 1, t0, slice(0, WD1_EARLY))
-        late_cut = max(WD1_EARLY, WD1_VECTOR)
-        subtract_labels(0, range(PACK - 1))
-        if WD1_VECTOR > WD1_EARLY:
-            for t0 in (0, 2):
-                cast_wd(nc.vector.tensor_copy, 1, t0, slice(WD1_EARLY, WD1_VECTOR), WD1_EARLY)
-        subtract_labels(0, [PACK - 1])
-        if late_cut < P:
-            for t0 in (0, 2):
-                cast_wd(nc.scalar.copy, 1, t0, slice(late_cut, P), WD1_EARLY)
-        for step in V_ORDER:
-            if step == "q":
-                quantise_wd1(len(codes1))
-                logits_second(0, len(codes1) - 1)
-            else:
-                weigh(0, "abcd".index(step))
-        if S_ORDER == "BW":
-            logits_second(1, 0)
-            logits_second(1, 1)
-            cast_wv(0)
-        elif S_ORDER == "WB":
-            cast_wv(0)
-            logits_second(1, 0)
-            logits_second(1, 1)
-        elif S_ORDER == "wBw":
-            cast_wv(0, [0])
-            logits_second(1, 0)
-            logits_second(1, 1)
-            cast_wv(0, [1])
-        for q in range(2):
-            quantise_g(0, q * P, (q + 1) * P, g_bf[0, q])
-        add_labels(0)
-        quantise_g(0, 2 * P, 3 * P, g_bf[0, 2])
-        add_labels(1)
-        quantise_g(0, 3 * P, 4 * P, g_bf[0, 3])
-        sums = turn_and_add()
-        weigh(1, 0)
-        if SPLIT_WV0:
-            quantise_wv(0, 0, 1)
-            early0 = dx_product(0, None, [0])
-            weigh(1, 1)
-            quantise_wv(0, 1, 2)
-            quantise_g(1, 0, DIRECT, g_bf[1][:])
-            dx_product(0, early0, [1])
+        if WD0_VECTOR == P:
+            cast_wd(nc.vector.tensor_copy, vector_tile, 0, 0, slice(0, P))
+            cast_wd(nc.scalar.copy, scalar_tile, 0, 1, slice(0, P))
         else:
-            weigh(1, 1)
-            quantise_wv(0)
-            quantise_g(1, 0, DIRECT, g_bf[1][:])
-            early0 = dx_product(0)
-        for q in TURNED:
-            weigh_turned(sums, q)
-        cast_wv(1)
-        quantise_wv(1)
-        dx_early0 = copy_dx(early0, 0, halves[0])
-        g_words = turn_back()
-        early1 = dx_product(1)
-        scatter(dx_early0, 0, halves[0])
-        quantise_turned(g_words)
-        scatter(copy_dx(early1, 1, halves[0]), 1, halves[0])
-        final = [dx_product(b) for b in range(EARLY_TILES)]
-        for b in range(EARLY_TILES):
-            cast_wv(EARLY_TILES + b)
-            quantise_wv(EARLY_TILES + b)
-            scatter(copy_dx(final[b], b, halves[1]), b, halves[1])
+            for k in range(2):
+                cast_wd(nc.scalar.copy, scalar_tile, 0, k, slice(WD0_VECTOR, P))
+                cast_wd(nc.vector.tensor_copy, scalar_tile, 0, k, slice(0, WD0_VECTOR))
+        early = {}
+        turned_sums = {}
+        for step in ORDER.split():
+            what, k = step[0], int(step[-1]) if len(step) > 1 else 0
+            if what == "A":
+                quantise_wd(0, k)
+                logits(0, 0, k)
+            elif what == "B":
+                logits(0, 1, k)
+            elif what in "VS":
+                copy, new_tile = (nc.vector.tensor_copy, vector_tile) if what == "V" else (nc.scalar.copy, scalar_tile)
+                if step[1] == "a":
+                    cast_wd(copy, new_tile, 1, k, slice(0, WD1_EARLY))
+                else:
+                    cast_wd(copy, new_tile, 1, k, slice(WD1_EARLY, P), WD1_EARLY)
+            elif what in "de":
+                subtract_labels("de".index(what), k)
+            elif what == "D":
+                subtract_labels(0, k, 1)
+            elif what in "TU":
+                turned_sums["TU".index(what)] = turn_and_add("TU".index(what))
+            elif what in "am":
+                weigh("am".index(what), k)
+            elif what == "q":
+                quantise_wd(1, k)
+                logits(1, 0, k)
+            elif what == "s":
+                weigh_turned(turned_sums[0], 0, k)
+            elif what == "g":
+                quantise_g(0, 0)
+            elif what == "G":
+                quantise_g(0, 1)
+            elif what == "h":
+                quantise_g(1, 0)
+            elif what == "x":
+                turn_back(0)
+            elif what == "C":
+                logits(1, 1, k)
+            elif what == "w":
+                cast_wv(0, [k])
+            else:
+                quantise_wv(0, k, k + 1)
+                if k == 0:
+                    early[0] = dx_product(0, None, [0])
+        sums = turned_sums[1]
+        dx_product(0, early[0], [1])
+        final, dx_early = {}, {}
+        for step in TAIL.split():
+            what, k = step[0], int(step[-1]) if len(step) > 1 else 0
+            if what == "s":
+                weigh_turned(sums, 1, k)
+            elif what == "w":
+                cast_wv(k)
+            elif what == "v":
+                quantise_wv(k)
+            elif what == "x":
+                dx_early[k] = copy_dx(early[k], k, halves[0])
+            elif what == "b":
+                turn_back(1)
+            elif what == "p":
+                early[k] = dx_product(k)
+            elif what == "A":
+                scatter(dx_early[k], k, halves[0])
+            elif what == "g":
+                quantise_g(1, 1)
+            elif what == "f":
+                final[k] = dx_product(k)
+            else:
+                scatter(copy_dx(final[k], k, halves[1]), k, halves[1])
         for b in range(EARLY_TILES, D_TILES):
             scatter(copy_dx(dx_product(b), b, slice(0, N)), b, slice(0, N))

@@ -26,15 +26,15 @@ HALF = N // 2
 BLOCKS = HALF // P
 EARLY_TILES = 2
 WD0_VECTOR = 128
-WD1_EARLY = 64
-S_BUFS = 23
+WD1_EARLY = 0
+S_BUFS = 24
 V_BUFS = 16
-LOADS = ("wd0", "wd1a", "y0_02", "y0_23", "wd1b", "y0_34", "y1", "wv0", "wv1")
+LOADS = ("x1", "x2", "x3", "wd0", "wd1b", "y0_02", "y0_24", "y1", "wv00", "wv10", "wv01", "wv11")
 Y_FIRST = (True, True)
 TURN0 = False
 FULL = (True, True)
 TAIL = "s0 s1 w1 v1 x0 b p1 A0 g x1 A1 f0 f1 w2 v2 B0 w3 v3 B1"
-ORDER = "A0 A1 Va0 Va1 Sb0 Sb1 d0 d1 q0 a0 q1 a1 a2 a3 g C0 C1 U w0 w1 e0 e1 G m0 m1 v0 h v1"
+ORDER = "A0 A1 Vb0 Sb1 q0 d0 d1 q1 a0 a1 a2 a3 g C0 C1 U w0 w1 e0 e1 G m0 m1 v0 h v1"
 
 
 def tile_attend_gml_nce_kernel(tc, xT, wd, wv, y, cw, rw, offs, out):
@@ -59,12 +59,24 @@ def tile_attend_gml_nce_kernel(tc, xT, wd, wv, y, cw, rw, offs, out):
         offsets = sb.tile([P, N // 16], U16, name="offsets")
         x_planes = [sb.tile([P, T], F32, name="x_plane%d" % j) for j in range(PACK)]
         wd_parts = [part for part in ((0, 0, P), (1, 0, WD1_EARLY), (1, WD1_EARLY, P)) if part[1] < part[2]]
-        wd_raw = {(h, m0): sb.tile([P, PACK, (m1 - m0) * PACK], F32, name="wd_raw%d_%d" % (h, m0)) for h, m0, m1 in wd_parts}
+        if "wd" in LOADS:
+            wd_whole = sb.tile([P, PACK, V], F32, name="wd_whole")
+            wd_raw = {(h, 0): wd_whole[:, :, h * PASS:(h + 1) * PASS] for h in range(V_PASSES)}
+        else:
+            wd_raw = {(h, m0): sb.tile([P, PACK, (m1 - m0) * PACK], F32, name="wd_raw%d_%d" % (h, m0))[:] for h, m0, m1 in wd_parts}
 
         def load_wd(h, m0, m1):
-            nc.sync.dma_start(wd_raw[h, m0][:], wd_rows[:, :, h * PASS + m0 * PACK:h * PASS + m1 * PACK])
+            nc.sync.dma_start(wd_raw[h, m0], wd_rows[:, :, h * PASS + m0 * PACK:h * PASS + m1 * PACK])
 
-        wv_raw = [[sb.tile([P, PACK, D // 2], F32, name="wv_raw%d_%d" % (h, u)) for u in range(2)] for h in range(V_PASSES)]
+        wv_raw, wv_whole = {}, {}
+        for h in range(V_PASSES):
+            if "wv%d" % h in LOADS:
+                wv_whole[h] = sb.tile([P, PACK, D], F32, name="wv_whole%d" % h)
+            for u in range(2):
+                if "wv%d" % h in LOADS:
+                    wv_raw[h, u] = wv_whole[h][:, :, u * D // 2:(u + 1) * D // 2]
+                else:
+                    wv_raw[h, u] = sb.tile([P, PACK, D // 2], F32, name="wv_raw%d_%d" % (h, u))[:]
         y_whole = {}
         y_sb = {}
         for h in range(V_PASSES):
@@ -87,19 +99,24 @@ def tile_attend_gml_nce_kernel(tc, xT, wd, wv, y, cw, rw, offs, out):
         nc.sync.dma_start(offsets[:], offs)
         nc.scalar.dma_start(rw_sb[:], rw[0:1, :].rearrange("o (c i) -> (o c) i", i=LINE))
         nc.scalar.dma_start(cw_sb[:], cw.rearrange("(h p j) o -> p h (j o)", p=P, j=PACK))
-        for j in range(1, PACK):
-            nc.sync.dma_start(x_planes[j][:], x_rows[j])
         for what in LOADS:
-            if what == "wd0":
+            if what[0] == "x":
+                nc.sync.dma_start(x_planes[int(what[1])][:], x_rows[int(what[1])])
+            elif what == "wd":
+                nc.sync.dma_start(wd_whole[:], wd_rows)
+            elif what == "wd0":
                 load_wd(0, 0, P)
             elif what == "wd1a":
                 load_wd(1, 0, WD1_EARLY)
             elif what == "wd1b":
                 load_wd(1, WD1_EARLY, P)
             elif what.startswith("wv"):
-                u = int(what[2])
-                for h in range(V_PASSES):
-                    nc.sync.dma_start(wv_raw[h][u][:], wv_rows[h][:, :, u * D // 2:(u + 1) * D // 2])
+                h = int(what[2])
+                if len(what) == 3:
+                    nc.sync.dma_start(wv_whole[h][:], wv_rows[h])
+                else:
+                    u = int(what[3])
+                    nc.sync.dma_start(wv_raw[h, u], wv_rows[h][:, :, u * D // 2:(u + 1) * D // 2])
             elif len(what) == 5:
                 h, ts = int(what[1]), slice(int(what[3]), int(what[4]))
                 nc.sync.dma_start(y_whole[h][:, ts, :], y_rows[h][:, ts, :])
@@ -186,7 +203,7 @@ def tile_attend_gml_nce_kernel(tc, xT, wd, wv, y, cw, rw, offs, out):
         def cast_wd(copy, new_tile, h, k, ms, m0=0):
             if (h, k) not in wd_bf:
                 wd_bf[h, k] = new_tile([P, 2, P, PACK], BF16, "wd_bf%d_%d" % (h, k))
-            src = wd_raw[h, m0][:].rearrange("p j (m t) -> p m j t", t=PACK)
+            src = wd_raw[h, m0].rearrange("p j (m t) -> p m j t", t=PACK)
             dst = wd_bf[h, k][:].rearrange("p e m j -> p m j e")
             copy(dst[:, ms], src[:, ms.start - m0:ms.stop - m0, :, 2 * k:2 * k + 2])
 
@@ -274,7 +291,7 @@ def tile_attend_gml_nce_kernel(tc, xT, wd, wv, y, cw, rw, offs, out):
                 if h == 0:
                     wv_bf[b] = scalar_tile([P, V_PASSES, P, PACK], BF16, "wv_bf%d" % b)
                 nc.scalar.copy(wv_bf[b][:, h].rearrange("p (c i) j -> p c j i", i=LINE),
-                               wv_raw[h][b // 2][:, :, b % 2 * P:(b % 2 + 1) * P].rearrange("p j (c i) -> p c j i", i=LINE))
+                               wv_raw[h, b // 2][:, :, b % 2 * P:(b % 2 + 1) * P].rearrange("p j (c i) -> p c j i", i=LINE))
 
         def quantise_wv(b, h0=0, h1=V_PASSES):
             if b < EARLY_TILES:

@@ -24,17 +24,8 @@ D_TILES = D // P
 LINE = 4
 HALF = N // 2
 BLOCKS = HALF // P
-EARLY_TILES = 2
-WD0_VECTOR = 128
-WD1_EARLY = 0
-S_BUFS = 24
-V_BUFS = 16
-LOADS = ("x1", "x2", "x3", "wd0", "wd1b", "y0_02", "y0_24", "y1", "wv00", "wv10", "wv01", "wv11")
-Y_FIRST = (True, True)
-TURN0 = False
-FULL = (True, True)
-TAIL = "s0 s1 w1 v1 x0 b p1 A0 g x1 A1 f0 f1 w2 v2 B0 w3 v3 B1"
-ORDER = "A0 A1 Vb0 Sb1 q0 d0 d1 q1 a0 a1 a2 a3 g C0 C1 U w0 w1 e0 e1 G m0 m1 v0 h v1"
+S_BUFS = 16
+V_BUFS = 20
 
 
 def tile_attend_gml_nce_kernel(tc, xT, wd, wv, y, cw, rw, offs, out):
@@ -54,39 +45,14 @@ def tile_attend_gml_nce_kernel(tc, xT, wd, wv, y, cw, rw, offs, out):
         def vector_tile(shape, dtype, name):
             return vline.tile(shape, dtype, name=name, tag="vline", align_bytes=64)
 
-        halves = [slice(0, HALF), slice(HALF, N)]
+        early, late = slice(0, HALF), slice(HALF, N)
+        pairs = [slice(0, 2), slice(2, 4)]
 
         offsets = sb.tile([P, N // 16], U16, name="offsets")
         x_planes = [sb.tile([P, T], F32, name="x_plane%d" % j) for j in range(PACK)]
-        wd_parts = [part for part in ((0, 0, P), (1, 0, WD1_EARLY), (1, WD1_EARLY, P)) if part[1] < part[2]]
-        if "wd" in LOADS:
-            wd_whole = sb.tile([P, PACK, V], F32, name="wd_whole")
-            wd_raw = {(h, 0): wd_whole[:, :, h * PASS:(h + 1) * PASS] for h in range(V_PASSES)}
-        else:
-            wd_raw = {(h, m0): sb.tile([P, PACK, (m1 - m0) * PACK], F32, name="wd_raw%d_%d" % (h, m0))[:] for h, m0, m1 in wd_parts}
-
-        def load_wd(h, m0, m1):
-            nc.sync.dma_start(wd_raw[h, m0], wd_rows[:, :, h * PASS + m0 * PACK:h * PASS + m1 * PACK])
-
-        wv_raw, wv_whole = {}, {}
-        for h in range(V_PASSES):
-            if "wv%d" % h in LOADS:
-                wv_whole[h] = sb.tile([P, PACK, D], F32, name="wv_whole%d" % h)
-            for u in range(2):
-                if "wv%d" % h in LOADS:
-                    wv_raw[h, u] = wv_whole[h][:, :, u * D // 2:(u + 1) * D // 2]
-                else:
-                    wv_raw[h, u] = sb.tile([P, PACK, D // 2], F32, name="wv_raw%d_%d" % (h, u))[:]
-        y_whole = {}
-        y_sb = {}
-        for h in range(V_PASSES):
-            if "y%da" % h in LOADS:
-                for u in range(2):
-                    y_sb[h, u] = sb.tile([P, PACK, HALF], F32, name="y%d_%d" % (h, u))[:]
-            else:
-                y_whole[h] = sb.tile([P, PACK, N], F32, name="y_sb%d" % h)
-                for u in range(2):
-                    y_sb[h, u] = y_whole[h][:, :, halves[u]]
+        wd_raw = [sb.tile([P, PACK, PASS], F32, name="wd_raw%d" % h) for h in range(V_PASSES)]
+        wv_raw = {(h, u): sb.tile([P, PACK, D // 2], F32, name="wv_raw%d_%d" % (h, u)) for h in range(V_PASSES) for u in range(2)}
+        y_sb = [sb.tile([P, PACK, N], F32, name="y_sb%d" % h) for h in range(V_PASSES)]
         cw_sb = sb.tile([P, V_PASSES, PACK], F32, name="cw_sb")
         rw_sb = sb.tile([P, LINE], F32, name="rw_sb")
 
@@ -99,32 +65,16 @@ def tile_attend_gml_nce_kernel(tc, xT, wd, wv, y, cw, rw, offs, out):
         nc.sync.dma_start(offsets[:], offs)
         nc.scalar.dma_start(rw_sb[:], rw[0:1, :].rearrange("o (c i) -> (o c) i", i=LINE))
         nc.scalar.dma_start(cw_sb[:], cw.rearrange("(h p j) o -> p h (j o)", p=P, j=PACK))
-        for what in LOADS:
-            if what[0] == "x":
-                nc.sync.dma_start(x_planes[int(what[1])][:], x_rows[int(what[1])])
-            elif what == "wd":
-                nc.sync.dma_start(wd_whole[:], wd_rows)
-            elif what == "wd0":
-                load_wd(0, 0, P)
-            elif what == "wd1a":
-                load_wd(1, 0, WD1_EARLY)
-            elif what == "wd1b":
-                load_wd(1, WD1_EARLY, P)
-            elif what.startswith("wv"):
-                h = int(what[2])
-                if len(what) == 3:
-                    nc.sync.dma_start(wv_whole[h][:], wv_rows[h])
-                else:
-                    u = int(what[3])
-                    nc.sync.dma_start(wv_raw[h, u], wv_rows[h][:, :, u * D // 2:(u + 1) * D // 2])
-            elif len(what) == 5:
-                h, ts = int(what[1]), slice(int(what[3]), int(what[4]))
-                nc.sync.dma_start(y_whole[h][:, ts, :], y_rows[h][:, ts, :])
-            elif len(what) == 2:
-                nc.sync.dma_start(y_whole[int(what[1])][:], y_rows[int(what[1])])
-            else:
-                h, u = int(what[1]), "ab".index(what[2])
-                nc.sync.dma_start(y_sb[h, u], y_rows[h][:, :, halves[u]])
+        for j in range(1, PACK):
+            nc.sync.dma_start(x_planes[j][:], x_rows[j])
+        for h in range(V_PASSES):
+            nc.sync.dma_start(wd_raw[h][:], wd_rows[:, :, h * PASS:(h + 1) * PASS])
+        for ts in pairs:
+            nc.sync.dma_start(y_sb[0][:, ts, :], y_rows[0][:, ts, :])
+        nc.sync.dma_start(y_sb[1][:], y_rows[1])
+        for u in range(2):
+            for h in range(V_PASSES):
+                nc.sync.dma_start(wv_raw[h, u][:], wv_rows[h][:, :, u * D // 2:(u + 1) * D // 2])
 
         warm = sb.tile([P, 1], F32, name="warm")
         warm_out = sb.tile([P, 1], F32, name="warm_out")
@@ -142,20 +92,15 @@ def tile_attend_gml_nce_kernel(tc, xT, wd, wv, y, cw, rw, offs, out):
         column_bank = bank("column_bank")
         for q in range(BLOCKS):
             nc.tensor.transpose(column_bank[:, q * P:(q + 1) * P], rw_late[:, q * P:(q + 1) * P], ident[:])
-        turned = (TURN0, True)
-        direct = [HALF if turned[h] else N for h in range(V_PASSES)]
-        flipped = [FULL[h] and turned[h] for h in range(V_PASSES)]
-        weight = [sb.tile([P, PACK, direct[h]], F32, name="weight%d" % h) for h in range(V_PASSES)]
-        minus_rw_column = sb.tile([P, BLOCKS], F32, name="minus_rw_column")
         minus_cw = sb.tile([P, V_PASSES, PACK], F32, name="minus_cw")
-        if any(flipped):
-            nc.scalar.activation(minus_cw[:], cw_sb[:], ACT.Copy, scale=-1.0)
+        nc.scalar.activation(minus_cw[:], cw_sb[:], ACT.Copy, scale=-1.0)
+        minus_rw_column = sb.tile([P, BLOCKS], F32, name="minus_rw_column")
+        nc.scalar.activation(minus_rw_column[:], column_bank[:, 0:HALF:P], ACT.Copy, scale=-1.0)
+        weight = [sb.tile([P, PACK, HALF], F32, name="weight%d" % h) for h in range(V_PASSES)]
         for h in range(V_PASSES):
-            for j in range(PACK):
-                nc.scalar.activation(weight[h][:, j, :].rearrange("p (c i) -> p c i", i=LINE), rw_spread[:, 0:direct[h] // LINE, :],
-                                     ACT.Copy, scale=(minus_cw if flipped[h] else cw_sb)[:, h, j:j + 1])
-            if h == 0:
-                nc.scalar.activation(minus_rw_column[:], column_bank[:, 0:HALF:P], ACT.Copy, scale=-1.0)
+            for t in range(PACK):
+                nc.scalar.activation(weight[h][:, t, :].rearrange("p (c i) -> p c i", i=LINE), rw_spread[:, 0:HALF // LINE, :],
+                                     ACT.Copy, scale=minus_cw[:, h, t:t + 1])
 
         def place(t):
             return slice((t % 2 * 2 + t // 2) * P, (t % 2 * 2 + t // 2 + 1) * P)
@@ -165,8 +110,6 @@ def tile_attend_gml_nce_kernel(tc, xT, wd, wv, y, cw, rw, offs, out):
 
         weight_turned = {}
         for h in range(V_PASSES):
-            if not turned[h]:
-                continue
             cw_bank = bank("cw_bank")
             for t in range(PACK):
                 nc.tensor.transpose(cw_bank[:, place(t)], cw_sb[:, h, t:t + 1].to_broadcast([P, P]), ident[:])
@@ -183,29 +126,34 @@ def tile_attend_gml_nce_kernel(tc, xT, wd, wv, y, cw, rw, offs, out):
         x_bf = sb.tile([P, N, PACK], BF16, name="x_bf", align_bytes=64)
         x_codes = sb.tile([P, N], U32, name="x_codes", align_bytes=64)
         x_scales = sb.tile([P, N], U8, name="x_scales", align_bytes=64)
-        offset_halves = [offsets[:, 0:HALF // 16], offsets[:, HALF // 16:N // 16]]
+
+        def listed(ns):
+            return offsets[:, ns.start // 16:ns.stop // 16]
+
         for j in range(PACK - 1):
             nc.vector.tensor_copy(x_bf[:, :, j], x_planes[j][:].indirect(offsets[:]))
-        for u in range(2):
-            nc.vector.tensor_copy(x_bf[:, halves[u], PACK - 1], x_planes[PACK - 1][:].indirect(offset_halves[u]))
-        for u in range(2):
-            nc.vector.quantize_mx(out=x_codes[:, halves[u]].bitcast(E4M3), scales=x_scales[:, halves[u]],
-                                  in_=x_bf[:, halves[u]].rearrange("p n j -> p (n j)"))
+        for ns in (early, late):
+            nc.vector.tensor_copy(x_bf[:, ns, PACK - 1], x_planes[PACK - 1][:].indirect(listed(ns)))
+        for ns in (early, late):
+            nc.vector.quantize_mx(out=x_codes[:, ns].bitcast(E4M3), scales=x_scales[:, ns],
+                                  in_=x_bf[:, ns].rearrange("p n j -> p (n j)"))
 
-        g_codes = sb.tile([P, V_PASSES, N], U32, name="g_codes", align_bytes=64)
-        g_scales = sb.tile([P, V_PASSES, N], U8, name="g_scales", align_bytes=64)
-        nc.gpsimd.memset(g_codes[:, 1, halves[1]], 0)
-        nc.gpsimd.memset(g_scales[:, 1, halves[1]], 0)
-        wd_bf, wd_codes, sig, g_bf, g_turned, g_words, wv_bf, wv_codes = {}, {}, {}, {}, {}, {}, {}, {}
+        g_codes = [sb.tile([P, HALF + N], U32, name="g_codes%d" % h, align_bytes=64) for h in range(V_PASSES)]
+        g_scales = [sb.tile([P, HALF + N], U8, name="g_scales%d" % h, align_bytes=64) for h in range(V_PASSES)]
+        for h in range(V_PASSES):
+            nc.gpsimd.memset(g_codes[h][:, 0:HALF], 0)
+            nc.gpsimd.memset(g_scales[h][:, 0:HALF], 0)
+
+        wd_bf, wd_codes, g_bf, sums, g_turned, g_words, wv_bf, wv_codes = {}, {}, {}, {}, {}, {}, {}, {}
         wd_scales = {(h, k): sb.tile([P, 2, P], U8, name="wd_scales%d_%d" % (h, k), align_bytes=64) for h in range(V_PASSES) for k in range(2)}
-        diff = [sb.tile([P, PACK, direct[h]], F32, name="diff%d" % h) for h in range(V_PASSES)]
+        wv_scales = sb.tile([P, D_TILES, V_PASSES, P], U8, name="wv_scales", align_bytes=64)
+        sig = {(h, k): sb.tile([P, 2, N], F32, name="sig%d_%d" % (h, k)) for h in range(V_PASSES) for k in range(2)}
+        diff = [sb.tile([P, PACK, HALF], F32, name="diff%d" % h) for h in range(V_PASSES)]
 
-        def cast_wd(copy, new_tile, h, k, ms, m0=0):
-            if (h, k) not in wd_bf:
-                wd_bf[h, k] = new_tile([P, 2, P, PACK], BF16, "wd_bf%d_%d" % (h, k))
-            src = wd_raw[h, m0].rearrange("p j (m t) -> p m j t", t=PACK)
-            dst = wd_bf[h, k][:].rearrange("p e m j -> p m j e")
-            copy(dst[:, ms], src[:, ms.start - m0:ms.stop - m0, :, 2 * k:2 * k + 2])
+        def cast_wd(copy, new_tile, h, k):
+            wd_bf[h, k] = new_tile([P, 2, P, PACK], BF16, "wd_bf%d_%d" % (h, k))
+            src = wd_raw[h][:].rearrange("p j (m t) -> p m j t", t=PACK)
+            copy(wd_bf[h, k][:].rearrange("p e m j -> p m j e"), src[:, :, :, pairs[k]])
 
         def quantise_wd(h, k):
             wd_codes[h, k] = vector_tile([P, 2, P], U32, "wd_codes%d_%d" % (h, k))
@@ -214,53 +162,46 @@ def tile_attend_gml_nce_kernel(tc, xT, wd, wv, y, cw, rw, offs, out):
                                       scales=wd_scales[h, k][:, es].rearrange("p e m -> p (e m)"),
                                       in_=wd_bf[h, k][:, es].rearrange("p e m j -> p (e m j)"))
 
-        def logits(h, u, k):
-            if FULL[h]:
-                for e in range(2 if u == 0 else 0):
-                    a_bank = bank("a_bank")
-                    nc.tensor.matmul_mx(out=a_bank[:], lhsT=wd_codes[h, k][:, e, :].bitcast(E4M3), lhsT_scale=wd_scales[h, k][:, e, :],
-                                        rhs=x_codes[:].bitcast(E4M3), rhs_scale=x_scales[:], start=True, stop=True)
-                    whole = scalar_tile([P, N], F32, "sig%d_%d" % (h, 2 * k + e))
-                    nc.scalar.activation(whole[:], a_bank[:], ACT.Sigmoid, scale=-1.0 if flipped[h] else 1.0)
-                    sig[h, 2 * k + e] = whole[:]
-                    sig[h, 1, 2 * k + e] = whole[:, halves[1]]
-                return
-            a_bank = bank("a_bank")
+        def logits(h, k):
             for e in range(2):
-                nc.tensor.matmul_mx(out=a_bank[:, halves[e]], lhsT=wd_codes[h, k][:, e, :].bitcast(E4M3), lhsT_scale=wd_scales[h, k][:, e, :],
-                                    rhs=x_codes[:, halves[u]].bitcast(E4M3), rhs_scale=x_scales[:, halves[u]], start=True, stop=True)
-            pair = scalar_tile([P, 2, HALF], F32, "sig%d_%d_%d" % (h, u, k))
-            nc.scalar.activation(pair[:].rearrange("p e n -> p (e n)"), a_bank[:], ACT.Sigmoid, scale=-1.0 if u == 1 and turned[h] else 1.0)
-            sig[h, u, "pair", k] = pair[:]
-            for e in range(2):
-                sig[h, u, 2 * k + e] = pair[:, e, :]
+                a_bank = bank("a_bank")
+                nc.tensor.matmul_mx(out=a_bank[:], lhsT=wd_codes[h, k][:, e, :].bitcast(E4M3), lhsT_scale=wd_scales[h, k][:, e, :],
+                                    rhs=x_codes[:].bitcast(E4M3), rhs_scale=x_scales[:], start=True, stop=True)
+                nc.scalar.activation(sig[h, k][:, e, :], a_bank[:], ACT.Sigmoid, scale=-1.0)
 
-        def subtract_labels(h, k, u=0):
-            ts = slice(2 * k, 2 * k + 2)
-            if not FULL[h]:
-                nc.vector.tensor_tensor(diff[h][:, ts, halves[u]], sig[h, u, "pair", k], y_sb[h, u][:, ts, :], ALU.subtract)
-                return
-            for t in range(2 * k, 2 * k + 2):
-                if flipped[h]:
-                    nc.vector.scalar_tensor_tensor(diff[h][:, t, :], y_sb[h, 0][:, t, :], -1.0, sig[h, t][:, halves[0]], ALU.add, ALU.add)
-                else:
-                    for ns in ([slice(0, P), slice(P, N)] if t == PACK - 1 else [slice(0, N)]):
-                        nc.vector.tensor_tensor(diff[h][:, t, ns], sig[h, t][:, ns], y_whole[h][:, t, ns], ALU.subtract)
+        def subtract(h, k):
+            for ns in ([early] if k == 0 else [slice(0, P), slice(P, HALF)]):
+                nc.vector.scalar_tensor_tensor(diff[h][:, pairs[k], ns], y_sb[h][:, pairs[k], ns], -1.0, sig[h, k][:, :, ns], ALU.add, ALU.add)
 
-        def turn_and_add(h):
-            sums = [bank("sum_bank") for q in range(BLOCKS)]
-            labels = [(q, t, y_sb[h, 1][:, t, q * P:(q + 1) * P]) for q in range(BLOCKS) for t in range(PACK)]
-            sigmoids = [(q, t, sig[h, 1, t][:, q * P:(q + 1) * P]) for t in range(PACK) for q in range(BLOCKS)]
-            first, second = (labels, sigmoids) if Y_FIRST[h] else (sigmoids, labels)
-            for q, t, part in first:
-                nc.tensor.matmul(sums[q][:, place(t)], lhsT=part, rhs=ident[:], is_transpose=True, start=t == 0, stop=False)
-            for q, t, part in second:
-                nc.tensor.matmul(sums[q][:, place(t)], lhsT=part, rhs=ident[:], is_transpose=True, start=False, stop=t == PACK - 1)
-            return sums
+        def weigh(h, q):
+            if q == 0:
+                g_bf[h] = vector_tile([P, HALF, PACK], BF16, "g_bf%d" % h)
+            cs = slice(q * P // 2, (q + 1) * P // 2)
+            g_dst = g_bf[h][:, q * P:(q + 1) * P].rearrange("p (c i) t -> p c t i", i=2)
+            g_src = diff[h][:].rearrange("p t (c i) -> p c t i", i=2)
+            g_weight = weight[h][:].rearrange("p t (c i) -> p c t i", i=2)
+            nc.vector.tensor_tensor(g_dst, g_src[:, cs], g_weight[:, cs], ALU.mult)
 
-        def weigh_turned(sums, h, q):
+        def block(q):
+            return slice(HALF + q * P, HALF + (q + 1) * P)
+
+        def turn_sigmoids(h):
+            for q in range(BLOCKS):
+                sums[h, q] = bank("sum_bank")
+            for t in range(PACK):
+                for q in range(BLOCKS):
+                    nc.tensor.matmul(sums[h, q][:, place(t)], lhsT=sig[h, t // 2][:, t % 2, block(q)], rhs=ident[:],
+                                     is_transpose=True, start=t == 0, stop=False)
+
+        def turn_labels(h, ts):
+            for q in range(BLOCKS):
+                for t in ts:
+                    nc.tensor.matmul(sums[h, q][:, place(t)], lhsT=y_sb[h][:, t, block(q)], rhs=ident[:],
+                                     is_transpose=True, start=False, stop=t == PACK - 1)
+
+        def weigh_turned(h, q):
             g_turned[h, q] = vector_tile([P, 2 * P, 2], BF16, "g_turned%d_%d" % (h, q))
-            nc.vector.scalar_tensor_tensor(g_turned[h, q][:], by_words(sums[q]), -1.0, weight_turned[h, q][:], ALU.add, ALU.mult)
+            nc.vector.scalar_tensor_tensor(g_turned[h, q][:], by_words(sums[h, q]), -1.0, weight_turned[h, q][:], ALU.add, ALU.mult)
 
         def turn_back(h):
             word_bank = bank("word_bank")
@@ -271,134 +212,97 @@ def tile_attend_gml_nce_kernel(tc, xT, wd, wv, y, cw, rw, offs, out):
             g_words[h] = scalar_tile([P, BLOCKS, P, 2], F32, "g_words%d" % h)
             nc.scalar.copy(g_words[h][:], word_bank[:].rearrange("p (q u i) -> p q i u", q=BLOCKS, u=2))
 
-        def quantise_g(h, u):
-            values = g_bf[h, u][:].rearrange("p n t -> p (n t)") if u == 0 or not turned[h] else g_words[h][:].rearrange("p q i u -> p (q i u)").bitcast(BF16)
-            nc.vector.quantize_mx(out=g_codes[:, h, halves[u]].bitcast(E5M2), scales=g_scales[:, h, halves[u]], in_=values)
+        def quantise_g(h, ns):
+            values = g_bf[h][:].rearrange("p n t -> p (n t)") if ns == early else g_words[h][:].rearrange("p q i u -> p (q i u)").bitcast(BF16)
+            cs = slice(HALF + ns.start, HALF + ns.stop)
+            nc.vector.quantize_mx(out=g_codes[h][:, cs].bitcast(E5M2), scales=g_scales[h][:, cs], in_=values)
 
-        def weigh(h, q):
-            if q % 2 == 0:
-                g_bf[h, q // 2] = vector_tile([P, HALF, PACK], BF16, "g_bf%d_%d" % (h, q // 2))
-            cs = slice(q * P // 2, (q + 1) * P // 2)
-            g_dst = g_bf[h, q // 2][:, q % 2 * P:(q % 2 + 1) * P].rearrange("p (c i) t -> p c t i", i=2)
-            g_src = diff[h][:].rearrange("p t (c i) -> p c t i", i=2)
-            g_weight = weight[h][:].rearrange("p t (c i) -> p c t i", i=2)
-            nc.vector.tensor_tensor(g_dst, g_src[:, cs], g_weight[:, cs], ALU.mult)
-
-        wv_scales = sb.tile([P, D_TILES, V_PASSES, P], U8, name="wv_scales", align_bytes=64)
-
-        def cast_wv(b, hs=range(V_PASSES)):
-            for h in hs:
-                if h == 0:
-                    wv_bf[b] = scalar_tile([P, V_PASSES, P, PACK], BF16, "wv_bf%d" % b)
-                nc.scalar.copy(wv_bf[b][:, h].rearrange("p (c i) j -> p c j i", i=LINE),
-                               wv_raw[h, b // 2][:, :, b % 2 * P:(b % 2 + 1) * P].rearrange("p j (c i) -> p c j i", i=LINE))
+        def cast_wv(b, h):
+            if h == 0:
+                wv_bf[b] = scalar_tile([P, V_PASSES, P, PACK], BF16, "wv_bf%d" % b)
+            nc.scalar.copy(wv_bf[b][:, h].rearrange("p (c i) j -> p c j i", i=LINE),
+                           wv_raw[h, b // 2][:, :, b % 2 * P:(b % 2 + 1) * P].rearrange("p j (c i) -> p c j i", i=LINE))
 
         def quantise_wv(b, h0=0, h1=V_PASSES):
-            if b < EARLY_TILES:
-                wv_tile = vector_tile([P, h1 - h0, P], U32, "wv_codes%d_%d" % (b, h0))
-            else:
-                wv_tile = sb.tile([P, h1 - h0, P], U32, name="wv_codes%d" % b, align_bytes=64)
+            wv_tile = vector_tile([P, h1 - h0, P], U32, "wv_codes%d_%d" % (b, h0))
             for h in range(h0, h1):
                 wv_codes[b, h] = wv_tile[:, h - h0, :]
             nc.vector.quantize_mx(out=wv_tile[:].rearrange("p h m -> p (h m)").bitcast(E4M3),
                                   scales=wv_scales[:, b, h0:h1].rearrange("p h m -> p (h m)"),
                                   in_=wv_bf[b][:, h0:h1].rearrange("p h m j -> p (h m j)"))
 
-        def dx_product(b, dx_bank=None, hs=range(V_PASSES)):
-            if dx_bank is None:
-                dx_bank = bank("dx_bank")
-            for h in hs:
-                nc.tensor.matmul_mx(out=dx_bank[:], lhsT=wv_codes[b, h].bitcast(E4M3),
-                                    lhsT_scale=wv_scales[:, b, h, :],
-                                    rhs=g_codes[:, h, :].bitcast(E5M2), rhs_scale=g_scales[:, h, :],
-                                    start=h == 0, stop=h == V_PASSES - 1)
+        def dx_pass(dx_bank, b, h, first):
+            cs = slice(first, first + N)
+            nc.tensor.matmul_mx(out=dx_bank[:], lhsT=wv_codes[b, h].bitcast(E4M3), lhsT_scale=wv_scales[:, b, h, :],
+                                rhs=g_codes[h][:, cs].bitcast(E5M2), rhs_scale=g_scales[h][:, cs],
+                                start=h == 0, stop=h == V_PASSES - 1)
+
+        def dx_product(b, first):
+            dx_bank = bank("dx_bank")
+            for h in range(V_PASSES):
+                dx_pass(dx_bank, b, h, first)
             return dx_bank
 
-        def copy_dx(dx_bank, b, ns):
-            dx = scalar_tile([P, ns.stop - ns.start], F32, "dx%d_%d" % (b, ns.start))
-            nc.scalar.copy(dx[:], dx_bank[:, ns])
+        def copy_dx(dx_bank, cs, name):
+            dx = scalar_tile([P, cs.stop - cs.start], F32, name)
+            nc.scalar.copy(dx[:], dx_bank[:, cs])
             return dx
 
         def scatter(dx, b, ns):
-            nc.vector.tensor_copy(windows[b][:].indirect(offsets[:, ns.start // 16:ns.stop // 16]), dx[:])
+            nc.vector.tensor_copy(windows[b][:].indirect(listed(ns)), dx[:])
             if ns.stop == N:
                 nc.sync.dma_start(out[b * P:(b + 1) * P, :], windows[b][:])
 
-        if WD0_VECTOR == P:
-            cast_wd(nc.vector.tensor_copy, vector_tile, 0, 0, slice(0, P))
-            cast_wd(nc.scalar.copy, scalar_tile, 0, 1, slice(0, P))
-        else:
-            for k in range(2):
-                cast_wd(nc.scalar.copy, scalar_tile, 0, k, slice(WD0_VECTOR, P))
-                cast_wd(nc.vector.tensor_copy, scalar_tile, 0, k, slice(0, WD0_VECTOR))
-        early = {}
-        turned_sums = {}
-        for step in ORDER.split():
-            what, k = step[0], int(step[-1]) if len(step) > 1 else 0
-            if what == "A":
-                quantise_wd(0, k)
-                logits(0, 0, k)
-            elif what == "B":
-                logits(0, 1, k)
-            elif what in "VS":
-                copy, new_tile = (nc.vector.tensor_copy, vector_tile) if what == "V" else (nc.scalar.copy, scalar_tile)
-                if step[1] == "a":
-                    cast_wd(copy, new_tile, 1, k, slice(0, WD1_EARLY))
-                else:
-                    cast_wd(copy, new_tile, 1, k, slice(WD1_EARLY, P), WD1_EARLY)
-            elif what in "de":
-                subtract_labels("de".index(what), k)
-            elif what == "D":
-                subtract_labels(0, k, 1)
-            elif what in "TU":
-                turned_sums["TU".index(what)] = turn_and_add("TU".index(what))
-            elif what in "am":
-                weigh("am".index(what), k)
-            elif what == "q":
-                quantise_wd(1, k)
-                logits(1, 0, k)
-            elif what == "s":
-                weigh_turned(turned_sums[0], 0, k)
-            elif what == "g":
-                quantise_g(0, 0)
-            elif what == "G":
-                quantise_g(0, 1)
-            elif what == "h":
-                quantise_g(1, 0)
-            elif what == "x":
-                turn_back(0)
-            elif what == "C":
-                logits(1, 1, k)
-            elif what == "w":
-                cast_wv(0, [k])
-            else:
-                quantise_wv(0, k, k + 1)
-                if k == 0:
-                    early[0] = dx_product(0, None, [0])
-        sums = turned_sums[1]
-        dx_product(0, early[0], [1])
-        final, dx_early = {}, {}
-        for step in TAIL.split():
-            what, k = step[0], int(step[-1]) if len(step) > 1 else 0
-            if what == "s":
-                weigh_turned(sums, 1, k)
-            elif what == "w":
-                cast_wv(k)
-            elif what == "v":
-                quantise_wv(k)
-            elif what == "x":
-                dx_early[k] = copy_dx(early[k], k, halves[0])
-            elif what == "b":
-                turn_back(1)
-            elif what == "p":
-                early[k] = dx_product(k)
-            elif what == "A":
-                scatter(dx_early[k], k, halves[0])
-            elif what == "g":
-                quantise_g(1, 1)
-            elif what == "f":
-                final[k] = dx_product(k)
-            else:
-                scatter(copy_dx(final[k], k, halves[1]), k, halves[1])
-        for b in range(EARLY_TILES, D_TILES):
-            scatter(copy_dx(dx_product(b), b, slice(0, N)), b, slice(0, N))
+        cast_wd(nc.vector.tensor_copy, vector_tile, 0, 0)
+        cast_wd(nc.scalar.copy, scalar_tile, 0, 1)
+        for k in range(2):
+            quantise_wd(0, k)
+            logits(0, k)
+        for k in range(2):
+            cast_wd(nc.vector.tensor_copy, vector_tile, 1, k)
+        for k in range(2):
+            quantise_wd(1, k)
+            logits(1, k)
+            subtract(0, k)
+        for h in range(V_PASSES):
+            turn_sigmoids(h)
+            turn_labels(h, range(PACK))
+        weigh(0, 0)
+        weigh(0, 1)
+        subtract(1, 0)
+        quantise_g(0, early)
+        subtract(1, 1)
+        weigh(1, 0)
+        weigh(1, 1)
+        cast_wv(0, 0)
+        cast_wv(0, 1)
+        quantise_wv(0, 0, 1)
+        first_bank = bank("dx_bank")
+        dx_pass(first_bank, 0, 0, 0)
+        quantise_g(1, early)
+        weigh_turned(0, 0)
+        quantise_wv(0, 1, 2)
+        dx_pass(first_bank, 0, 1, 0)
+        weigh_turned(0, 1)
+        weigh_turned(1, 0)
+        weigh_turned(1, 1)
+        cast_wv(1, 0)
+        cast_wv(1, 1)
+        quantise_wv(1)
+        dx0 = copy_dx(first_bank, late, "dx_early0")
+        turn_back(0)
+        turn_back(1)
+        second_bank = dx_product(1, 0)
+        scatter(dx0, 0, early)
+        quantise_g(0, late)
+        quantise_g(1, late)
+        dx1 = copy_dx(second_bank, late, "dx_early1")
+        scatter(dx1, 1, early)
+        final = [dx_product(b, HALF) for b in range(2)]
+        for b in range(2):
+            cast_wv(2 + b, 0)
+            cast_wv(2 + b, 1)
+            quantise_wv(2 + b)
+            scatter(copy_dx(final[b], late, "dx_late%d" % b), b, late)
+        for b in range(2, D_TILES):
+            scatter(copy_dx(dx_product(b, HALF), slice(0, N), "dx%d" % b), b, slice(0, N))

@@ -117,11 +117,10 @@ def tile_attend_gml_nce_kernel(tc, xT, wd, wv, y, cw, rw, offs, out):
                 weight_turned[h, q] = scalar_tile([P, 2 * P, 2], F32, "weight_turned%d_%d" % (h, q))
                 nc.scalar.activation(weight_turned[h, q][:], by_words(cw_bank), ACT.Copy, scale=minus_rw_column[:, q:q + 1])
 
-        windows = [sb.tile([P, T], F32, name="window%d" % b) for b in range(D_TILES)]
-        nc.vector.memset(windows[0][:], 0.0)
-        nc.vector.memset(windows[1][:], 0.0)
-        nc.vector.memset(windows[2][:], 0.0)
-        nc.gpsimd.memset(windows[3][:], 0.0)
+        windows = [sb.tile([P, T], F32, name="window%d" % b) for b in range(D_TILES - 1)]
+        for window in windows:
+            nc.vector.memset(window[:], 0.0)
+        windows.append(windows[0])
 
         x_bf = sb.tile([P, N, PACK], BF16, name="x_bf", align_bytes=64)
         x_codes = sb.tile([P, N], U32, name="x_codes", align_bytes=64)
@@ -141,8 +140,8 @@ def tile_attend_gml_nce_kernel(tc, xT, wd, wv, y, cw, rw, offs, out):
         g_codes = [sb.tile([P, HALF + N], U32, name="g_codes%d" % h, align_bytes=64) for h in range(V_PASSES)]
         g_scales = [sb.tile([P, HALF + N], U8, name="g_scales%d" % h, align_bytes=64) for h in range(V_PASSES)]
         for h in range(V_PASSES):
-            nc.gpsimd.memset(g_codes[h][:, 0:HALF], 0)
-            nc.gpsimd.memset(g_scales[h][:, 0:HALF], 0)
+            nc.vector.memset(g_codes[h][:, 0:HALF], 0)
+            nc.vector.memset(g_scales[h][:, 0:HALF].bitcast(U32), 0)
 
         wd_bf, wd_codes, g_bf, sums, g_turned, g_words, wv_bf, wv_codes = {}, {}, {}, {}, {}, {}, {}, {}
         wd_scales = {(h, k): sb.tile([P, 2, P], U8, name="wd_scales%d_%d" % (h, k), align_bytes=64) for h in range(V_PASSES) for k in range(2)}

@@ -24,6 +24,7 @@ D_TILES = D // P
 LINE = 4
 HALF = N // 2
 BLOCKS = HALF // P
+WV_LOADS = ((0, 0, 1), (1, 0, 1), (0, 1, 2), (1, 1, 2), (0, 2, 4), (1, 2, 4))
 S_BUFS = 16
 V_BUFS = 20
 
@@ -51,7 +52,6 @@ def tile_attend_gml_nce_kernel(tc, xT, wd, wv, y, cw, rw, offs, out):
         offsets = sb.tile([P, N // 16], U16, name="offsets")
         x_planes = [sb.tile([P, T], F32, name="x_plane%d" % j) for j in range(PACK)]
         wd_raw = [sb.tile([P, PACK, PASS], F32, name="wd_raw%d" % h) for h in range(V_PASSES)]
-        wv_raw = {(h, u): sb.tile([P, PACK, D // 2], F32, name="wv_raw%d_%d" % (h, u)) for h in range(V_PASSES) for u in range(2)}
         y_sb = [sb.tile([P, PACK, N], F32, name="y_sb%d" % h) for h in range(V_PASSES)]
         cw_sb = sb.tile([P, V_PASSES, PACK], F32, name="cw_sb")
         rw_sb = sb.tile([P, LINE], F32, name="rw_sb")
@@ -72,9 +72,12 @@ def tile_attend_gml_nce_kernel(tc, xT, wd, wv, y, cw, rw, offs, out):
         for ts in pairs:
             nc.sync.dma_start(y_sb[0][:, ts, :], y_rows[0][:, ts, :])
         nc.sync.dma_start(y_sb[1][:], y_rows[1])
-        for u in range(2):
-            for h in range(V_PASSES):
-                nc.sync.dma_start(wv_raw[h, u][:], wv_rows[h][:, :, u * D // 2:(u + 1) * D // 2])
+        wv_raw = {}
+        for h, b0, b1 in WV_LOADS:
+            part = sb.tile([P, PACK, (b1 - b0) * P], F32, name="wv_raw%d_%d" % (h, b0))
+            nc.sync.dma_start(part[:], wv_rows[h][:, :, b0 * P:b1 * P])
+            for b in range(b0, b1):
+                wv_raw[h, b] = part[:, :, (b - b0) * P:(b - b0 + 1) * P]
 
         warm = sb.tile([P, 1], F32, name="warm")
         warm_out = sb.tile([P, 1], F32, name="warm_out")
@@ -220,7 +223,7 @@ def tile_attend_gml_nce_kernel(tc, xT, wd, wv, y, cw, rw, offs, out):
             if h == 0:
                 wv_bf[b] = scalar_tile([P, V_PASSES, P, PACK], BF16, "wv_bf%d" % b)
             nc.scalar.copy(wv_bf[b][:, h].rearrange("p (c i) j -> p c j i", i=LINE),
-                           wv_raw[h, b // 2][:, :, b % 2 * P:(b % 2 + 1) * P].rearrange("p j (c i) -> p c j i", i=LINE))
+                           wv_raw[h, b].rearrange("p j (c i) -> p c j i", i=LINE))
 
         def quantise_wv(b, h0=0, h1=V_PASSES):
             wv_tile = vector_tile([P, h1 - h0, P], U32, "wv_codes%d_%d" % (b, h0))
@@ -298,10 +301,13 @@ def tile_attend_gml_nce_kernel(tc, xT, wd, wv, y, cw, rw, offs, out):
         dx1 = copy_dx(second_bank, late, "dx_early1")
         scatter(dx1, 1, early)
         final = [dx_product(b, HALF) for b in range(2)]
+        cast_wv(2, 0)
+        cast_wv(2, 1)
+        quantise_wv(2)
         for b in range(2):
-            cast_wv(2 + b, 0)
-            cast_wv(2 + b, 1)
-            quantise_wv(2 + b)
             scatter(copy_dx(final[b], late, "dx_late%d" % b), b, late)
+        cast_wv(3, 0)
+        cast_wv(3, 1)
+        quantise_wv(3)
         for b in range(2, D_TILES):
             scatter(copy_dx(dx_product(b, HALF), slice(0, N), "dx%d" % b), b, slice(0, N))

@@ -69,9 +69,9 @@ def tile_attend_gml_nce_kernel(tc, xT, wd, wv, y, cw, rw, offs, out):
             nc.sync.dma_start(x_planes[j][:], x_rows[j])
         for h in range(V_PASSES):
             nc.sync.dma_start(wd_raw[h][:], wd_rows[:, :, h * PASS:(h + 1) * PASS])
-        for ts in pairs:
-            nc.sync.dma_start(y_sb[0][:, ts, :], y_rows[0][:, ts, :])
-        nc.sync.dma_start(y_sb[1][:], y_rows[1])
+        for h in range(V_PASSES):
+            for ts in pairs:
+                nc.sync.dma_start(y_sb[h][:, ts, :], y_rows[h][:, ts, :])
         wv_raw = {}
         for h, b0, b1 in WV_LOADS:
             part = sb.tile([P, PACK, (b1 - b0) * P], F32, name="wv_raw%d_%d" % (h, b0))

@@ -24,8 +24,9 @@ D_TILES = D // P
 LINE = 4
 HALF = N // 2
 BLOCKS = HALF // P
+EARLY_TILES = 2
 WV_LOADS = ((0, 0, 1), (1, 0, 1), (0, 1, 2), (1, 1, 2), (0, 2, 4), (1, 2, 4))
-S_BUFS = 16
+S_BUFS = 20
 V_BUFS = 20
 
 
@@ -47,12 +48,13 @@ def tile_attend_gml_nce_kernel(tc, xT, wd, wv, y, cw, rw, offs, out):
             return vline.tile(shape, dtype, name=name, tag="vline", align_bytes=64)
 
         early, late = slice(0, HALF), slice(HALF, N)
+        halves = [early, late]
         pairs = [slice(0, 2), slice(2, 4)]
 
         offsets = sb.tile([P, N // 16], U16, name="offsets")
         x_planes = [sb.tile([P, T], F32, name="x_plane%d" % j) for j in range(PACK)]
         wd_raw = [sb.tile([P, PACK, PASS], F32, name="wd_raw%d" % h) for h in range(V_PASSES)]
-        y_sb = [sb.tile([P, PACK, N], F32, name="y_sb%d" % h) for h in range(V_PASSES)]
+        y_sb = {(h, k): sb.tile([P, 2, N], F32, name="y_sb%d_%d" % (h, k)) for h in range(V_PASSES) for k in range(2)}
         cw_sb = sb.tile([P, V_PASSES, PACK], F32, name="cw_sb")
         rw_sb = sb.tile([P, LINE], F32, name="rw_sb")
 
@@ -70,8 +72,8 @@ def tile_attend_gml_nce_kernel(tc, xT, wd, wv, y, cw, rw, offs, out):
         for h in range(V_PASSES):
             nc.sync.dma_start(wd_raw[h][:], wd_rows[:, :, h * PASS:(h + 1) * PASS])
         for h in range(V_PASSES):
-            for ts in pairs:
-                nc.sync.dma_start(y_sb[h][:, ts, :], y_rows[h][:, ts, :])
+            for k in range(2):
+                nc.sync.dma_start(y_sb[h, k][:], y_rows[h][:, pairs[k], :])
         wv_raw = {}
         for h, b0, b1 in WV_LOADS:
             part = sb.tile([P, PACK, (b1 - b0) * P], F32, name="wv_raw%d_%d" % (h, b0))
@@ -125,32 +127,28 @@ def tile_attend_gml_nce_kernel(tc, xT, wd, wv, y, cw, rw, offs, out):
             nc.vector.memset(window[:], 0.0)
         windows.append(windows[0])
 
-        x_bf = sb.tile([P, N, PACK], BF16, name="x_bf", align_bytes=64)
-        x_codes = sb.tile([P, N], U32, name="x_codes", align_bytes=64)
-        x_scales = sb.tile([P, N], U8, name="x_scales", align_bytes=64)
-
-        def listed(ns):
-            return offsets[:, ns.start // 16:ns.stop // 16]
-
-        for j in range(PACK - 1):
-            nc.vector.tensor_copy(x_bf[:, :, j], x_planes[j][:].indirect(offsets[:]))
-        for ns in (early, late):
-            nc.vector.tensor_copy(x_bf[:, ns, PACK - 1], x_planes[PACK - 1][:].indirect(listed(ns)))
-        for ns in (early, late):
-            nc.vector.quantize_mx(out=x_codes[:, ns].bitcast(E4M3), scales=x_scales[:, ns],
-                                  in_=x_bf[:, ns].rearrange("p n j -> p (n j)"))
-
         g_codes = [sb.tile([P, HALF + N], U32, name="g_codes%d" % h, align_bytes=64) for h in range(V_PASSES)]
         g_scales = [sb.tile([P, HALF + N], U8, name="g_scales%d" % h, align_bytes=64) for h in range(V_PASSES)]
         for h in range(V_PASSES):
             nc.vector.memset(g_codes[h][:, 0:HALF], 0)
             nc.vector.memset(g_scales[h][:, 0:HALF].bitcast(U32), 0)
 
-        wd_bf, wd_codes, g_bf, sums, g_turned, g_words, wv_bf, wv_codes = {}, {}, {}, {}, {}, {}, {}, {}
+        x_bf = sb.tile([P, N, PACK], BF16, name="x_bf", align_bytes=64)
+        x_scales = [sb.tile([P, HALF], U8, name="x_scales%d" % s, align_bytes=64) for s in range(2)]
         wd_scales = {(h, k): sb.tile([P, 2, P], U8, name="wd_scales%d_%d" % (h, k), align_bytes=64) for h in range(V_PASSES) for k in range(2)}
         wv_scales = sb.tile([P, D_TILES, V_PASSES, P], U8, name="wv_scales", align_bytes=64)
-        sig = {(h, k): sb.tile([P, 2, N], F32, name="sig%d_%d" % (h, k)) for h in range(V_PASSES) for k in range(2)}
-        diff = [sb.tile([P, PACK, HALF], F32, name="diff%d" % h) for h in range(V_PASSES)]
+        x_codes, wd_bf, wd_codes, sig, diff, g_bf, sums, g_turned, g_words, wv_bf, wv_codes = {}, {}, {}, {}, {}, {}, {}, {}, {}, {}, {}
+
+        def listed(ns):
+            return offsets[:, ns.start // 16:ns.stop // 16]
+
+        def gather(j, ns):
+            nc.vector.tensor_copy(x_bf[:, ns, j], x_planes[j][:].indirect(listed(ns)))
+
+        def quantise_x(s):
+            x_codes[s] = vector_tile([P, HALF], U32, "x_codes%d" % s)
+            nc.vector.quantize_mx(out=x_codes[s][:].bitcast(E4M3), scales=x_scales[s][:],
+                                  in_=x_bf[:, halves[s]].rearrange("p n j -> p (n j)"))
 
         def cast_wd(copy, new_tile, h, k):
             wd_bf[h, k] = new_tile([P, 2, P, PACK], BF16, "wd_bf%d_%d" % (h, k))
@@ -159,46 +157,44 @@ def tile_attend_gml_nce_kernel(tc, xT, wd, wv, y, cw, rw, offs, out):
 
         def quantise_wd(h, k):
             wd_codes[h, k] = vector_tile([P, 2, P], U32, "wd_codes%d_%d" % (h, k))
-            for es in ([slice(0, 1), slice(1, 2)] if (h, k) == (0, 0) else [slice(0, 2)]):
-                nc.vector.quantize_mx(out=wd_codes[h, k][:, es].rearrange("p e m -> p (e m)").bitcast(E4M3),
-                                      scales=wd_scales[h, k][:, es].rearrange("p e m -> p (e m)"),
-                                      in_=wd_bf[h, k][:, es].rearrange("p e m j -> p (e m j)"))
+            nc.vector.quantize_mx(out=wd_codes[h, k][:].rearrange("p e m -> p (e m)").bitcast(E4M3),
+                                  scales=wd_scales[h, k][:].rearrange("p e m -> p (e m)"),
+                                  in_=wd_bf[h, k][:].rearrange("p e m j -> p (e m j)"))
 
-        def logits(h, k):
+        def sigmoids(h, k, s):
+            a_bank = bank("a_bank")
             for e in range(2):
-                a_bank = bank("a_bank")
-                nc.tensor.matmul_mx(out=a_bank[:], lhsT=wd_codes[h, k][:, e, :].bitcast(E4M3), lhsT_scale=wd_scales[h, k][:, e, :],
-                                    rhs=x_codes[:].bitcast(E4M3), rhs_scale=x_scales[:], start=True, stop=True)
-                nc.scalar.activation(sig[h, k][:, e, :], a_bank[:], ACT.Sigmoid, scale=-1.0)
+                nc.tensor.matmul_mx(out=a_bank[:, e * HALF:(e + 1) * HALF], lhsT=wd_codes[h, k][:, e, :].bitcast(E4M3),
+                                    lhsT_scale=wd_scales[h, k][:, e, :], rhs=x_codes[s][:].bitcast(E4M3), rhs_scale=x_scales[s][:],
+                                    start=True, stop=True)
+            sig[h, k, s] = scalar_tile([P, 2, HALF], F32, "sig%d_%d_%d" % (h, k, s))
+            nc.scalar.activation(sig[h, k, s][:].rearrange("p e n -> p (e n)"), a_bank[:], ACT.Sigmoid, scale=-1.0)
 
         def subtract(h, k):
-            for ns in ([early] if k == 0 else [slice(0, P), slice(P, HALF)]):
-                nc.vector.scalar_tensor_tensor(diff[h][:, pairs[k], ns], y_sb[h][:, pairs[k], ns], -1.0, sig[h, k][:, :, ns], ALU.add, ALU.add)
+            for q in range(BLOCKS):
+                if k == 0:
+                    diff[h, q] = vector_tile([P, PACK, P], F32, "diff%d_%d" % (h, q))
+                ns = slice(q * P, (q + 1) * P)
+                nc.vector.scalar_tensor_tensor(diff[h, q][:, pairs[k], :], y_sb[h, k][:, :, ns], -1.0, sig[h, k, 0][:, :, ns], ALU.add, ALU.add)
 
-        def weigh(h, q):
-            if q == 0:
-                g_bf[h] = vector_tile([P, HALF, PACK], BF16, "g_bf%d" % h)
-            cs = slice(q * P // 2, (q + 1) * P // 2)
-            g_dst = g_bf[h][:, q * P:(q + 1) * P].rearrange("p (c i) t -> p c t i", i=2)
-            g_src = diff[h][:].rearrange("p t (c i) -> p c t i", i=2)
-            g_weight = weight[h][:].rearrange("p t (c i) -> p c t i", i=2)
-            nc.vector.tensor_tensor(g_dst, g_src[:, cs], g_weight[:, cs], ALU.mult)
+        def weigh(h):
+            g_bf[h] = vector_tile([P, HALF, PACK], BF16, "g_bf%d" % h)
+            for q in range(BLOCKS):
+                ns = slice(q * P, (q + 1) * P)
+                nc.vector.tensor_tensor(g_bf[h][:, ns].rearrange("p (c i) t -> p c t i", i=2),
+                                        diff[h, q][:].rearrange("p t (c i) -> p c t i", i=2),
+                                        weight[h][:, :, ns].rearrange("p t (c i) -> p c t i", i=2), ALU.mult)
 
-        def block(q):
-            return slice(HALF + q * P, HALF + (q + 1) * P)
-
-        def turn_sigmoids(h):
+        def turn(h):
             for q in range(BLOCKS):
                 sums[h, q] = bank("sum_bank")
             for t in range(PACK):
                 for q in range(BLOCKS):
-                    nc.tensor.matmul(sums[h, q][:, place(t)], lhsT=sig[h, t // 2][:, t % 2, block(q)], rhs=ident[:],
+                    nc.tensor.matmul(sums[h, q][:, place(t)], lhsT=y_sb[h, t // 2][:, t % 2, HALF + q * P:HALF + (q + 1) * P], rhs=ident[:],
                                      is_transpose=True, start=t == 0, stop=False)
-
-        def turn_labels(h, ts):
-            for q in range(BLOCKS):
-                for t in ts:
-                    nc.tensor.matmul(sums[h, q][:, place(t)], lhsT=y_sb[h][:, t, block(q)], rhs=ident[:],
+            for t in range(PACK):
+                for q in range(BLOCKS):
+                    nc.tensor.matmul(sums[h, q][:, place(t)], lhsT=sig[h, t // 2, 1][:, t % 2, q * P:(q + 1) * P], rhs=ident[:],
                                      is_transpose=True, start=False, stop=t == PACK - 1)
 
         def weigh_turned(h, q):
@@ -219,19 +215,19 @@ def tile_attend_gml_nce_kernel(tc, xT, wd, wv, y, cw, rw, offs, out):
             cs = slice(HALF + ns.start, HALF + ns.stop)
             nc.vector.quantize_mx(out=g_codes[h][:, cs].bitcast(E5M2), scales=g_scales[h][:, cs], in_=values)
 
-        def cast_wv(b, h):
-            if h == 0:
-                wv_bf[b] = scalar_tile([P, V_PASSES, P, PACK], BF16, "wv_bf%d" % b)
-            nc.scalar.copy(wv_bf[b][:, h].rearrange("p (c i) j -> p c j i", i=LINE),
-                           wv_raw[h, b].rearrange("p j (c i) -> p c j i", i=LINE))
+        def cast_wv(b, h0, h1):
+            wv_bf[b, h0] = scalar_tile([P, h1 - h0, P, PACK], BF16, "wv_bf%d_%d" % (b, h0))
+            for h in range(h0, h1):
+                nc.scalar.copy(wv_bf[b, h0][:, h - h0].rearrange("p (c i) j -> p c j i", i=LINE),
+                               wv_raw[h, b].rearrange("p j (c i) -> p c j i", i=LINE))
 
-        def quantise_wv(b, h0=0, h1=V_PASSES):
+        def quantise_wv(b, h0, h1):
             wv_tile = vector_tile([P, h1 - h0, P], U32, "wv_codes%d_%d" % (b, h0))
             for h in range(h0, h1):
                 wv_codes[b, h] = wv_tile[:, h - h0, :]
             nc.vector.quantize_mx(out=wv_tile[:].rearrange("p h m -> p (h m)").bitcast(E4M3),
                                   scales=wv_scales[:, b, h0:h1].rearrange("p h m -> p (h m)"),
-                                  in_=wv_bf[b][:, h0:h1].rearrange("p h m j -> p (h m j)"))
+                                  in_=wv_bf[b, h0][:].rearrange("p h m j -> p (h m j)"))
 
         def dx_pass(dx_bank, b, h, first):
             cs = slice(first, first + N)
@@ -239,10 +235,10 @@ def tile_attend_gml_nce_kernel(tc, xT, wd, wv, y, cw, rw, offs, out):
                                 rhs=g_codes[h][:, cs].bitcast(E5M2), rhs_scale=g_scales[h][:, cs],
                                 start=h == 0, stop=h == V_PASSES - 1)
 
-        def dx_product(b, first):
+        def dx_product(b):
             dx_bank = bank("dx_bank")
             for h in range(V_PASSES):
-                dx_pass(dx_bank, b, h, first)
+                dx_pass(dx_bank, b, h, HALF)
             return dx_bank
 
         def copy_dx(dx_bank, cs, name):
@@ -255,59 +251,64 @@ def tile_attend_gml_nce_kernel(tc, xT, wd, wv, y, cw, rw, offs, out):
             if ns.stop == N:
                 nc.sync.dma_start(out[b * P:(b + 1) * P, :], windows[b][:])
 
+        for j in range(PACK - 1):
+            gather(j, slice(0, N))
+        for ns in halves:
+            gather(PACK - 1, ns)
+        quantise_x(0)
         cast_wd(nc.vector.tensor_copy, vector_tile, 0, 0)
         cast_wd(nc.scalar.copy, scalar_tile, 0, 1)
+        quantise_x(1)
         for k in range(2):
             quantise_wd(0, k)
-            logits(0, k)
+            sigmoids(0, k, 0)
+        for k in range(2):
+            sigmoids(0, k, 1)
         for k in range(2):
             cast_wd(nc.vector.tensor_copy, vector_tile, 1, k)
         for k in range(2):
             quantise_wd(1, k)
-            logits(1, k)
+            sigmoids(1, k, 0)
             subtract(0, k)
+        for k in range(2):
+            sigmoids(1, k, 1)
         for h in range(V_PASSES):
-            turn_sigmoids(h)
-            turn_labels(h, range(PACK))
-        weigh(0, 0)
-        weigh(0, 1)
+            turn(h)
+        weigh(0)
         subtract(1, 0)
         quantise_g(0, early)
         subtract(1, 1)
-        weigh(1, 0)
-        weigh(1, 1)
-        cast_wv(0, 0)
-        cast_wv(0, 1)
+        weigh(1)
+        for b in range(EARLY_TILES):
+            for h in range(V_PASSES):
+                cast_wv(b, h, h + 1)
         quantise_wv(0, 0, 1)
-        first_bank = bank("dx_bank")
-        dx_pass(first_bank, 0, 0, 0)
-        quantise_g(1, early)
+        early_banks = [bank("dx_bank") for b in range(EARLY_TILES)]
+        dx_pass(early_banks[0], 0, 0, 0)
         weigh_turned(0, 0)
+        quantise_g(1, early)
         quantise_wv(0, 1, 2)
-        dx_pass(first_bank, 0, 1, 0)
+        dx_pass(early_banks[0], 0, 1, 0)
         weigh_turned(0, 1)
+        quantise_wv(1, 0, 1)
+        dx_pass(early_banks[1], 1, 0, 0)
+        dx0 = copy_dx(early_banks[0], late, "dx_early0")
+        turn_back(0)
         weigh_turned(1, 0)
         weigh_turned(1, 1)
-        cast_wv(1, 0)
-        cast_wv(1, 1)
-        quantise_wv(1)
-        dx0 = copy_dx(first_bank, late, "dx_early0")
-        turn_back(0)
+        quantise_wv(1, 1, 2)
         turn_back(1)
-        second_bank = dx_product(1, 0)
+        dx_pass(early_banks[1], 1, 1, 0)
         scatter(dx0, 0, early)
         quantise_g(0, late)
         quantise_g(1, late)
-        dx1 = copy_dx(second_bank, late, "dx_early1")
-        scatter(dx1, 1, early)
-        final = [dx_product(b, HALF) for b in range(2)]
-        cast_wv(2, 0)
-        cast_wv(2, 1)
-        quantise_wv(2)
-        for b in range(2):
+        scatter(copy_dx(early_banks[1], late, "dx_early1"), 1, early)
+        final = [dx_product(b) for b in range(EARLY_TILES)]
+        cast_wv(2, 0, V_PASSES)
+        quantise_wv(2, 0, V_PASSES)
+        for b in range(EARLY_TILES):
             scatter(copy_dx(final[b], late, "dx_late%d" % b), b, late)
-        cast_wv(3, 0)
-        cast_wv(3, 1)
-        quantise_wv(3)
-        for b in range(2, D_TILES):
-            scatter(copy_dx(dx_product(b, HALF), slice(0, N), "dx%d" % b), b, slice(0, N))
+        cast_wv(3, 0, V_PASSES)
+        quantise_wv(3, 0, V_PASSES)
+        for b in range(EARLY_TILES, D_TILES):
+            scatter(copy_dx(dx_product(b), slice(0, N), "dx%d" % b), b, slice(0, N))

@@ -55,8 +55,8 @@ def tile_attend_gml_nce_kernel(tc, xT, wd, wv, y, cw, rw, offs, out):
         x_planes = [sb.tile([P, T], F32, name="x_plane%d" % j) for j in range(PACK)]
         wd_raw = [sb.tile([P, PACK, PASS], F32, name="wd_raw%d" % h) for h in range(V_PASSES)]
         y_sb = {(h, k): sb.tile([P, 2, N], F32, name="y_sb%d_%d" % (h, k)) for h in range(V_PASSES) for k in range(2)}
-        cw_sb = sb.tile([P, V_PASSES, PACK], F32, name="cw_sb")
-        rw_sb = sb.tile([P, LINE], F32, name="rw_sb")
+        rows = sb.tile([P, PASS], F32, name="rows")
+        nc.vector.memset(rows[:], 0.0)
 
         x_rows = xT.rearrange("(p j) n -> j p n", j=PACK)
         wd_rows = wd.rearrange("(p j) v -> p j v", j=PACK)
@@ -65,8 +65,8 @@ def tile_attend_gml_nce_kernel(tc, xT, wd, wv, y, cw, rw, offs, out):
 
         nc.sync.dma_start(x_planes[0][:], x_rows[0])
         nc.sync.dma_start(offsets[:], offs)
-        nc.scalar.dma_start(rw_sb[:], rw[0:1, :].rearrange("o (c i) -> (o c) i", i=LINE))
-        nc.scalar.dma_start(cw_sb[:], cw.rearrange("(h p j) o -> p h (j o)", p=P, j=PACK))
+        nc.sync.dma_start(rows[0:V_PASSES, :], cw.rearrange("(h v) o -> h (v o)", h=V_PASSES))
+        nc.sync.dma_start(rows[V_PASSES:V_PASSES + 1, :], rw[0:1, :])
         for j in range(1, PACK):
             nc.sync.dma_start(x_planes[j][:], x_rows[j])
         for h in range(V_PASSES):
@@ -88,6 +88,13 @@ def tile_attend_gml_nce_kernel(tc, xT, wd, wv, y, cw, rw, offs, out):
 
         ident = sb.tile([P, P], F32, name="ident")
         make_identity(nc, ident[:])
+        rows_bank = bank("rows_bank")
+        for t in range(PACK):
+            nc.tensor.transpose(rows_bank[:, t * P:(t + 1) * P], rows[:, t:PASS:PACK], ident[:])
+        columns = sb.tile([P, V_PASSES + 1, PACK], F32, name="columns")
+        nc.scalar.copy(columns[:], rows_bank[:].rearrange("p (t r) -> p r t", t=PACK)[:, 0:V_PASSES + 1, :])
+        cw_sb = columns[:, 0:V_PASSES, :]
+        rw_sb = columns[:, V_PASSES, :]
         rw_bank = bank("rw_bank")
         for i in range(LINE):
             nc.tensor.transpose(rw_bank[:, i * P:(i + 1) * P], rw_sb[:, i:i + 1].to_broadcast([P, P]), ident[:])
@@ -98,7 +105,7 @@ def tile_attend_gml_nce_kernel(tc, xT, wd, wv, y, cw, rw, offs, out):
         for q in range(BLOCKS):
             nc.tensor.transpose(column_bank[:, q * P:(q + 1) * P], rw_late[:, q * P:(q + 1) * P], ident[:])
         minus_cw = sb.tile([P, V_PASSES, PACK], F32, name="minus_cw")
-        nc.scalar.activation(minus_cw[:], cw_sb[:], ACT.Copy, scale=-1.0)
+        nc.scalar.activation(minus_cw[:], cw_sb, ACT.Copy, scale=-1.0)
         minus_rw_column = sb.tile([P, BLOCKS], F32, name="minus_rw_column")
         nc.scalar.activation(minus_rw_column[:], column_bank[:, 0:HALF:P], ACT.Copy, scale=-1.0)
         weight = [sb.tile([P, PACK, HALF], F32, name="weight%d" % h) for h in range(V_PASSES)]

@@ -25,7 +25,7 @@ LINE = 4
 HALF = N // 2
 BLOCKS = HALF // P
 EARLY_TILES = 2
-WV_LOADS = ((0, 0, 1), (1, 0, 1), (0, 1, 2), (1, 1, 2), (0, 2, 4), (1, 2, 4))
+WV_LOADS = ((0, 0, 2), (1, 0, 1), (1, 1, 2), (0, 2, 4), (1, 2, 4))
 S_BUFS = 20
 V_BUFS = 20
 
@@ -289,10 +289,10 @@ def tile_attend_gml_nce_kernel(tc, xT, wd, wv, y, cw, rw, offs, out):
         for b in range(EARLY_TILES):
             for h in range(V_PASSES):
                 cast_wv(b, h, h + 1)
+        weigh_turned(0, 0)
         quantise_wv(0, 0, 1)
         early_banks = [bank("dx_bank") for b in range(EARLY_TILES)]
         dx_pass(early_banks[0], 0, 0, 0)
-        weigh_turned(0, 0)
         quantise_g(1, early)
         quantise_wv(0, 1, 2)
         dx_pass(early_banks[0], 0, 1, 0)

@@ -26,6 +26,7 @@ HALF = N // 2
 BLOCKS = HALF // P
 EARLY_TILES = 2
 WV_LOADS = ((0, 0, 2), (1, 0, 1), (1, 1, 2), (0, 2, 4), (1, 2, 4))
+WD_SHARE = 48
 S_BUFS = 20
 V_BUFS = 20
 
@@ -162,6 +163,12 @@ def tile_attend_gml_nce_kernel(tc, xT, wd, wv, y, cw, rw, offs, out):
             src = wd_raw[h][:].rearrange("p j (m t) -> p m j t", t=PACK)
             copy(wd_bf[h, k][:].rearrange("p e m j -> p m j e"), src[:, :, :, pairs[k]])
 
+        def cast_wd_shared(h, k):
+            wd_bf[h, k] = scalar_tile([P, 2, P, PACK], BF16, "wd_bf%d_%d" % (h, k))
+            src = wd_raw[h][:].rearrange("p j (m t) -> p m j t", t=PACK)
+            for copy, ms in ((nc.scalar.copy, slice(WD_SHARE, P)), (nc.vector.tensor_copy, slice(0, WD_SHARE))):
+                copy(wd_bf[h, k][:].rearrange("p e m j -> p m j e")[:, ms], src[:, ms, :, pairs[k]])
+
         def quantise_wd(h, k):
             wd_codes[h, k] = vector_tile([P, 2, P], U32, "wd_codes%d_%d" % (h, k))
             nc.vector.quantize_mx(out=wd_codes[h, k][:].rearrange("p e m -> p (e m)").bitcast(E4M3),
@@ -264,11 +271,12 @@ def tile_attend_gml_nce_kernel(tc, xT, wd, wv, y, cw, rw, offs, out):
             gather(PACK - 1, ns)
         quantise_x(0)
         cast_wd(nc.vector.tensor_copy, vector_tile, 0, 0)
-        cast_wd(nc.scalar.copy, scalar_tile, 0, 1)
+        cast_wd_shared(0, 1)
+        quantise_wd(0, 0)
+        sigmoids(0, 0, 0)
         quantise_x(1)
-        for k in range(2):
-            quantise_wd(0, k)
-            sigmoids(0, k, 0)
+        quantise_wd(0, 1)
+        sigmoids(0, 1, 0)
         for k in range(2):
             sigmoids(0, k, 1)
         for k in range(2):

@@ -24,11 +24,12 @@ D_TILES = D // P
 LINE = 4
 HALF = N // 2
 BLOCKS = HALF // P
-EARLY_TILES = 2
-WV_LOADS = ((0, 0, 2), (1, 0, 1), (1, 1, 2), (0, 2, 4), (1, 2, 4))
 WD_SHARE = 48
-S_BUFS = 20
+S_BUFS = 22
 V_BUFS = 20
+EARLY, LATE = 0, 1
+DIRECT_BLOCKS = ((0, EARLY, (0, 1)), (1, EARLY, (0, 1)), (1, LATE, (1,)))
+TURNED_BLOCKS = ((0, LATE, (0, 1)), (1, LATE, (0,)))
 
 
 def tile_attend_gml_nce_kernel(tc, xT, wd, wv, y, cw, rw, offs, out):
@@ -48,12 +49,11 @@ def tile_attend_gml_nce_kernel(tc, xT, wd, wv, y, cw, rw, offs, out):
         def vector_tile(shape, dtype, name):
             return vline.tile(shape, dtype, name=name, tag="vline", align_bytes=64)
 
-        early, late = slice(0, HALF), slice(HALF, N)
-        halves = [early, late]
+        halves = [slice(0, HALF), slice(HALF, N)]
         pairs = [slice(0, 2), slice(2, 4)]
 
         offsets = sb.tile([P, N // 16], U16, name="offsets")
-        x_planes = [sb.tile([P, T], F32, name="x_plane%d" % j) for j in range(PACK)]
+        x_planes = [sb.tile([P, T], F32, name="x_plane%d" % j, tag="wide%d" % j) for j in range(PACK)]
         wd_raw = [sb.tile([P, PACK, PASS], F32, name="wd_raw%d" % h) for h in range(V_PASSES)]
         y_sb = {(h, k): sb.tile([P, 2, N], F32, name="y_sb%d_%d" % (h, k)) for h in range(V_PASSES) for k in range(2)}
         rows = sb.tile([P, PASS], F32, name="rows")
@@ -76,11 +76,12 @@ def tile_attend_gml_nce_kernel(tc, xT, wd, wv, y, cw, rw, offs, out):
             for k in range(2):
                 nc.sync.dma_start(y_sb[h, k][:], y_rows[h][:, pairs[k], :])
         wv_raw = {}
-        for h, b0, b1 in WV_LOADS:
-            part = sb.tile([P, PACK, (b1 - b0) * P], F32, name="wv_raw%d_%d" % (h, b0))
-            nc.sync.dma_start(part[:], wv_rows[h][:, :, b0 * P:b1 * P])
-            for b in range(b0, b1):
-                wv_raw[h, b] = part[:, :, (b - b0) * P:(b - b0 + 1) * P]
+        for b0 in range(0, D_TILES, 2):
+            for h in range(V_PASSES):
+                part = sb.tile([P, PACK, 2 * P], F32, name="wv_raw%d_%d" % (h, b0))
+                nc.sync.dma_start(part[:], wv_rows[h][:, :, b0 * P:(b0 + 2) * P])
+                for b in range(b0, b0 + 2):
+                    wv_raw[h, b] = part[:, :, (b - b0) * P:(b - b0 + 1) * P]
 
         warm = sb.tile([P, 1], F32, name="warm")
         warm_out = sb.tile([P, 1], F32, name="warm_out")
@@ -89,31 +90,26 @@ def tile_attend_gml_nce_kernel(tc, xT, wd, wv, y, cw, rw, offs, out):
 
         ident = sb.tile([P, P], F32, name="ident")
         make_identity(nc, ident[:])
-        rows_bank = bank("rows_bank")
+        cw_bank = bank("cw_bank")
         for t in range(PACK):
-            nc.tensor.transpose(rows_bank[:, t * P:(t + 1) * P], rows[:, t:PASS:PACK], ident[:])
-        columns = sb.tile([P, V_PASSES + 1, PACK], F32, name="columns")
-        nc.scalar.copy(columns[:], rows_bank[:].rearrange("p (t r) -> p r t", t=PACK)[:, 0:V_PASSES + 1, :])
-        cw_sb = columns[:, 0:V_PASSES, :]
-        rw_sb = columns[:, V_PASSES, :]
+            nc.tensor.transpose(cw_bank[:, t * P:(t + 1) * P], rows[:, t:PASS:PACK], ident[:])
+        cw_sb = sb.tile([P, V_PASSES, PACK], F32, name="cw_sb")
+        nc.scalar.copy(cw_sb[:], cw_bank[:].rearrange("p (t r) -> p r t", t=PACK)[:, 0:V_PASSES, :])
         rw_bank = bank("rw_bank")
-        for i in range(LINE):
-            nc.tensor.transpose(rw_bank[:, i * P:(i + 1) * P], rw_sb[:, i:i + 1].to_broadcast([P, P]), ident[:])
-        rw_spread = rw_bank[:].rearrange("p (i c) -> p c i", i=LINE)
-        rw_late = sb.tile([P, HALF], F32, name="rw_late")
-        nc.scalar.copy(rw_late[:].rearrange("p (c i) -> p c i", i=LINE), rw_spread[:, HALF // LINE:N // LINE, :])
-        column_bank = bank("column_bank")
-        for q in range(BLOCKS):
-            nc.tensor.transpose(column_bank[:, q * P:(q + 1) * P], rw_late[:, q * P:(q + 1) * P], ident[:])
-        minus_cw = sb.tile([P, V_PASSES, PACK], F32, name="minus_cw")
-        nc.scalar.activation(minus_cw[:], cw_sb, ACT.Copy, scale=-1.0)
-        minus_rw_column = sb.tile([P, BLOCKS], F32, name="minus_rw_column")
-        nc.scalar.activation(minus_rw_column[:], column_bank[:, 0:HALF:P], ACT.Copy, scale=-1.0)
-        weight = [sb.tile([P, PACK, HALF], F32, name="weight%d" % h) for h in range(V_PASSES)]
-        for h in range(V_PASSES):
+        for q in range(N // P):
+            nc.tensor.transpose(rw_bank[:, q * P:(q + 1) * P], rows[:, q * P:(q + 1) * P], ident[:])
+        minus_rw = sb.tile([P, N // P], F32, name="minus_rw")
+        nc.scalar.activation(minus_rw[:], rw_bank[:, V_PASSES:N:P], ACT.Copy, scale=-1.0)
+        spread_bank = bank("spread_bank")
+        for q in range(N // P):
+            nc.tensor.transpose(spread_bank[:, q * P:(q + 1) * P], minus_rw[:, q:q + 1].to_broadcast([P, P]), ident[:])
+        weight = {}
+        for h, s, qs in DIRECT_BLOCKS:
+            both = sb.tile([P, PACK, len(qs) * P], F32, name="weight%d_%d" % (h, s))
             for t in range(PACK):
-                nc.scalar.activation(weight[h][:, t, :].rearrange("p (c i) -> p c i", i=LINE), rw_spread[:, 0:HALF // LINE, :],
-                                     ACT.Copy, scale=minus_cw[:, h, t:t + 1])
+                nc.scalar.activation(both[:, t, :], spread_bank[:, s * HALF + qs[0] * P:s * HALF + (qs[-1] + 1) * P], ACT.Copy, scale=cw_sb[:, h, t:t + 1])
+            for n, q in enumerate(qs):
+                weight[h, s, q] = both[:, :, n * P:(n + 1) * P]
 
         def place(t):
             return slice((t % 2 * 2 + t // 2) * P, (t % 2 * 2 + t // 2 + 1) * P)
@@ -122,30 +118,25 @@ def tile_attend_gml_nce_kernel(tc, xT, wd, wv, y, cw, rw, offs, out):
             return full_bank[:].rearrange("p (e k) -> p k e", e=2)
 
         weight_turned = {}
-        for h in range(V_PASSES):
-            cw_bank = bank("cw_bank")
+        for h in sorted(set(h for h, s, qs in TURNED_BLOCKS)):
+            along_bank = bank("along_bank")
             for t in range(PACK):
-                nc.tensor.transpose(cw_bank[:, place(t)], cw_sb[:, h, t:t + 1].to_broadcast([P, P]), ident[:])
-            for q in range(BLOCKS):
-                weight_turned[h, q] = scalar_tile([P, 2 * P, 2], F32, "weight_turned%d_%d" % (h, q))
-                nc.scalar.activation(weight_turned[h, q][:], by_words(cw_bank), ACT.Copy, scale=minus_rw_column[:, q:q + 1])
+                nc.tensor.transpose(along_bank[:, place(t)], cw_sb[:, h, t:t + 1].to_broadcast([P, P]), ident[:])
+            for s, q in [(s, q) for g, s, qs in TURNED_BLOCKS if g == h for q in qs]:
+                weight_turned[h, s, q] = scalar_tile([P, 2 * P, 2], F32, "weight_turned%d_%d_%d" % (h, s, q))
+                nc.scalar.activation(weight_turned[h, s, q][:], by_words(along_bank), ACT.Copy, scale=minus_rw[:, BLOCKS * s + q:BLOCKS * s + q + 1])
 
         windows = [sb.tile([P, T], F32, name="window%d" % b) for b in range(D_TILES - 1)]
         for window in windows:
             nc.vector.memset(window[:], 0.0)
-        windows.append(windows[0])
-
-        g_codes = [sb.tile([P, HALF + N], U32, name="g_codes%d" % h, align_bytes=64) for h in range(V_PASSES)]
-        g_scales = [sb.tile([P, HALF + N], U8, name="g_scales%d" % h, align_bytes=64) for h in range(V_PASSES)]
-        for h in range(V_PASSES):
-            nc.vector.memset(g_codes[h][:, 0:HALF], 0)
-            nc.vector.memset(g_scales[h][:, 0:HALF].bitcast(U32), 0)
 
         x_bf = sb.tile([P, N, PACK], BF16, name="x_bf", align_bytes=64)
         x_scales = [sb.tile([P, HALF], U8, name="x_scales%d" % s, align_bytes=64) for s in range(2)]
         wd_scales = {(h, k): sb.tile([P, 2, P], U8, name="wd_scales%d_%d" % (h, k), align_bytes=64) for h in range(V_PASSES) for k in range(2)}
-        wv_scales = sb.tile([P, D_TILES, V_PASSES, P], U8, name="wv_scales", align_bytes=64)
-        x_codes, wd_bf, wd_codes, sig, diff, g_bf, sums, g_turned, g_words, wv_bf, wv_codes = {}, {}, {}, {}, {}, {}, {}, {}, {}, {}, {}
+        wv_scales = {(b, h): sb.tile([P, V_PASSES, P], U8, name="wv_scales%d_%d" % (b, h), align_bytes=64) for b in range(D_TILES) for h in range(V_PASSES)}
+        g_scales = {(h, s): sb.tile([P, HALF], U8, name="g_scales%d_%d" % (h, s), align_bytes=64) for h in range(V_PASSES) for s in range(2)}
+        x_codes, wd_bf, wd_codes, sig, unused, g_bf, sums, g_turned, g_words, g_codes = {}, {}, {}, {}, {}, {}, {}, {}, {}, {}
+        wv_bf, wv_codes, wv_scale, dx_bank, dx, turned = {}, {}, {}, {}, {}, {}
 
         def listed(ns):
             return offsets[:, ns.start // 16:ns.stop // 16]
@@ -163,10 +154,10 @@ def tile_attend_gml_nce_kernel(tc, xT, wd, wv, y, cw, rw, offs, out):
             src = wd_raw[h][:].rearrange("p j (m t) -> p m j t", t=PACK)
             copy(wd_bf[h, k][:].rearrange("p e m j -> p m j e"), src[:, :, :, pairs[k]])
 
-        def cast_wd_shared(h, k):
+        def cast_wd_shared(h, k, share):
             wd_bf[h, k] = scalar_tile([P, 2, P, PACK], BF16, "wd_bf%d_%d" % (h, k))
             src = wd_raw[h][:].rearrange("p j (m t) -> p m j t", t=PACK)
-            for copy, ms in ((nc.scalar.copy, slice(WD_SHARE, P)), (nc.vector.tensor_copy, slice(0, WD_SHARE))):
+            for copy, ms in ((nc.scalar.copy, slice(share, P)), (nc.vector.tensor_copy, slice(0, share))):
                 copy(wd_bf[h, k][:].rearrange("p e m j -> p m j e")[:, ms], src[:, ms, :, pairs[k]])
 
         def quantise_wd(h, k):
@@ -184,146 +175,182 @@ def tile_attend_gml_nce_kernel(tc, xT, wd, wv, y, cw, rw, offs, out):
             sig[h, k, s] = scalar_tile([P, 2, HALF], F32, "sig%d_%d_%d" % (h, k, s))
             nc.scalar.activation(sig[h, k, s][:].rearrange("p e n -> p (e n)"), a_bank[:], ACT.Sigmoid, scale=-1.0)
 
-        def subtract(h, k):
-            for q in range(BLOCKS):
-                if k == 0:
-                    diff[h, q] = vector_tile([P, PACK, P], F32, "diff%d_%d" % (h, q))
-                ns = slice(q * P, (q + 1) * P)
-                nc.vector.scalar_tensor_tensor(diff[h, q][:, pairs[k], :], y_sb[h, k][:, :, ns], -1.0, sig[h, k, 0][:, :, ns], ALU.add, ALU.add)
+        diff = {(h, s): sb.tile([P, PACK, HALF], F32, name="diff%d_%d" % (h, s)) for h, s, qs in DIRECT_BLOCKS}
 
-        def weigh(h):
-            g_bf[h] = vector_tile([P, HALF, PACK], BF16, "g_bf%d" % h)
-            for q in range(BLOCKS):
-                ns = slice(q * P, (q + 1) * P)
-                nc.vector.tensor_tensor(g_bf[h][:, ns].rearrange("p (c i) t -> p c t i", i=2),
-                                        diff[h, q][:].rearrange("p t (c i) -> p c t i", i=2),
-                                        weight[h][:, :, ns].rearrange("p t (c i) -> p c t i", i=2), ALU.mult)
+        def subtract(h, s, k, qs):
+            ns = slice(qs[0] * P, (qs[-1] + 1) * P)
+            nc.vector.scalar_tensor_tensor(diff[h, s][:, pairs[k], ns], y_sb[h, k][:, :, s * HALF + ns.start:s * HALF + ns.stop], -1.0,
+                                           sig[h, k, s][:, :, ns], ALU.add, ALU.add)
 
-        def turn(h):
-            for q in range(BLOCKS):
-                sums[h, q] = bank("sum_bank")
-            for t in range(PACK):
-                for q in range(BLOCKS):
-                    nc.tensor.matmul(sums[h, q][:, place(t)], lhsT=y_sb[h, t // 2][:, t % 2, HALF + q * P:HALF + (q + 1) * P], rhs=ident[:],
-                                     is_transpose=True, start=t == 0, stop=False)
-            for t in range(PACK):
-                for q in range(BLOCKS):
-                    nc.tensor.matmul(sums[h, q][:, place(t)], lhsT=sig[h, t // 2, 1][:, t % 2, q * P:(q + 1) * P], rhs=ident[:],
-                                     is_transpose=True, start=False, stop=t == PACK - 1)
+        def values_tile(new_tile, h, s):
+            if (h, s) not in g_bf:
+                g_bf[h, s] = new_tile([P, HALF, PACK], BF16, "g_bf%d_%d" % (h, s))
+            return g_bf[h, s]
 
-        def weigh_turned(h, q):
-            g_turned[h, q] = vector_tile([P, 2 * P, 2], BF16, "g_turned%d_%d" % (h, q))
-            nc.vector.scalar_tensor_tensor(g_turned[h, q][:], by_words(sums[h, q]), -1.0, weight_turned[h, q][:], ALU.add, ALU.mult)
+        def weigh(h, s, q):
+            ns = slice(q * P, (q + 1) * P)
+            nc.vector.tensor_tensor(values_tile(vector_tile, h, s)[:, ns].rearrange("p (c i) t -> p c t i", i=2),
+                                    diff[h, s][:, :, ns].rearrange("p t (c i) -> p c t i", i=2),
+                                    weight[h, s, q].rearrange("p t (c i) -> p c t i", i=2), ALU.mult)
 
-        def turn_back(h):
-            word_bank = bank("word_bank")
-            for q in range(BLOCKS):
-                words = g_turned[h, q][:].rearrange("p k e -> p (k e)").bitcast(F32)
-                for u in range(2):
-                    nc.tensor.transpose(word_bank[:, (2 * q + u) * P:(2 * q + u + 1) * P], words[:, u * P:(u + 1) * P], ident[:])
-            g_words[h] = scalar_tile([P, BLOCKS, P, 2], F32, "g_words%d" % h)
-            nc.scalar.copy(g_words[h][:], word_bank[:].rearrange("p (q u i) -> p q i u", q=BLOCKS, u=2))
+        def cast_tile(copy, new_tile, b, h):
+            if h == 0:
+                wv_bf[b] = new_tile([P, V_PASSES, P, PACK], BF16, "wv_bf%d" % b)
+            copy(wv_bf[b][:, h].rearrange("p (c i) j -> p c j i", i=LINE), wv_raw[h, b].rearrange("p j (c i) -> p c j i", i=LINE))
 
-        def quantise_g(h, ns):
-            values = g_bf[h][:].rearrange("p n t -> p (n t)") if ns == early else g_words[h][:].rearrange("p q i u -> p (q i u)").bitcast(BF16)
-            cs = slice(HALF + ns.start, HALF + ns.stop)
-            nc.vector.quantize_mx(out=g_codes[h][:, cs].bitcast(E5M2), scales=g_scales[h][:, cs], in_=values)
-
-        def cast_wv(b, h0, h1):
-            wv_bf[b, h0] = scalar_tile([P, h1 - h0, P, PACK], BF16, "wv_bf%d_%d" % (b, h0))
-            for h in range(h0, h1):
-                nc.scalar.copy(wv_bf[b, h0][:, h - h0].rearrange("p (c i) j -> p c j i", i=LINE),
-                               wv_raw[h, b].rearrange("p j (c i) -> p c j i", i=LINE))
-
-        def quantise_wv(b, h0, h1):
-            wv_tile = vector_tile([P, h1 - h0, P], U32, "wv_codes%d_%d" % (b, h0))
-            for h in range(h0, h1):
-                wv_codes[b, h] = wv_tile[:, h - h0, :]
-            nc.vector.quantize_mx(out=wv_tile[:].rearrange("p h m -> p (h m)").bitcast(E4M3),
-                                  scales=wv_scales[:, b, h0:h1].rearrange("p h m -> p (h m)"),
-                                  in_=wv_bf[b, h0][:].rearrange("p h m j -> p (h m j)"))
-
-        def dx_pass(dx_bank, b, h, first):
-            cs = slice(first, first + N)
-            nc.tensor.matmul_mx(out=dx_bank[:], lhsT=wv_codes[b, h].bitcast(E4M3), lhsT_scale=wv_scales[:, b, h, :],
-                                rhs=g_codes[h][:, cs].bitcast(E5M2), rhs_scale=g_scales[h][:, cs],
-                                start=h == 0, stop=h == V_PASSES - 1)
-
-        def dx_product(b):
-            dx_bank = bank("dx_bank")
+        def quantise_tile(b):
+            codes = vector_tile([P, V_PASSES, P], U32, "wv_codes%d" % b)
+            scales = wv_scales[b, 0]
             for h in range(V_PASSES):
-                dx_pass(dx_bank, b, h, HALF)
-            return dx_bank
+                wv_codes[b, h] = codes[:, h, :]
+                wv_scale[b, h] = scales[:, h, :]
+            nc.vector.quantize_mx(out=codes[:].rearrange("p h m -> p (h m)").bitcast(E4M3), scales=scales[:].rearrange("p h m -> p (h m)"),
+                                  in_=wv_bf[b][:].rearrange("p h m j -> p (h m j)"))
 
-        def copy_dx(dx_bank, cs, name):
-            dx = scalar_tile([P, cs.stop - cs.start], F32, name)
-            nc.scalar.copy(dx[:], dx_bank[:, cs])
-            return dx
+        def turn(h, s, what, ks, qs):
+            for k in ks:
+                for t in range(2 * k, 2 * k + 2):
+                    for q in qs:
+                        if (h, s, q) not in sums:
+                            sums[h, s, q] = bank("sum_bank")
+                        turned[h, s, q] = turned.get((h, s, q), 0) + 1
+                        src = y_sb[h, k][:, t % 2, s * HALF + q * P:s * HALF + (q + 1) * P] if what == "y" else sig[h, k, s][:, t % 2, q * P:(q + 1) * P]
+                        nc.tensor.matmul(sums[h, s, q][:, place(t)], lhsT=src, rhs=ident[:], is_transpose=True,
+                                         start=turned[h, s, q] == 1, stop=turned[h, s, q] == 2 * PACK)
 
-        def scatter(dx, b, ns):
-            nc.vector.tensor_copy(windows[b][:].indirect(listed(ns)), dx[:])
-            if ns.stop == N:
-                nc.sync.dma_start(out[b * P:(b + 1) * P, :], windows[b][:])
+        def weigh_turned(h, s, q):
+            g_turned[h, s, q] = vector_tile([P, 2 * P, 2], BF16, "g_turned%d_%d_%d" % (h, s, q))
+            nc.vector.scalar_tensor_tensor(g_turned[h, s, q][:], by_words(sums[h, s, q]), -1.0, weight_turned[h, s, q][:], ALU.add, ALU.mult)
 
-        for j in range(PACK - 1):
+        def turn_back(h, s, qs):
+            word_bank = bank("word_bank")
+            for n, q in enumerate(qs):
+                words = g_turned[h, s, q][:].rearrange("p k e -> p (k e)").bitcast(F32)
+                for u in range(2):
+                    nc.tensor.transpose(word_bank[:, (2 * n + u) * P:(2 * n + u + 1) * P], words[:, u * P:(u + 1) * P], ident[:])
+            dst = values_tile(scalar_tile, h, s)[:, qs[0] * P:(qs[-1] + 1) * P].rearrange("p n t -> p (n t)").bitcast(F32)
+            nc.scalar.copy(dst.rearrange("p (q i u) -> p q i u", q=len(qs), u=2),
+                           word_bank[:, 0:len(qs) * 2 * P].rearrange("p (q u i) -> p q i u", q=len(qs), u=2))
+
+        def quantise_g(h, s):
+            g_codes[h, s] = vector_tile([P, HALF], U32, "g_codes%d_%d" % (h, s))
+            nc.vector.quantize_mx(out=g_codes[h, s][:].bitcast(E5M2), scales=g_scales[h, s][:], in_=g_bf[h, s][:].rearrange("p n t -> p (n t)"))
+
+        def dx_pass(b, s, h):
+            if h == 0:
+                dx_bank[b, s] = bank("dx_bank")
+            nc.tensor.matmul_mx(out=dx_bank[b, s][:, 0:HALF], lhsT=wv_codes[b, h].bitcast(E4M3), lhsT_scale=wv_scale[b, h],
+                                rhs=g_codes[h, s][:].bitcast(E5M2), rhs_scale=g_scales[h, s][:], start=h == 0, stop=h == V_PASSES - 1)
+
+        def dx_product(b, s):
+            for h in range(V_PASSES):
+                dx_pass(b, s, h)
+
+        def copy_dx(copy, new_tile, b, s):
+            dx[b, s] = new_tile([P, HALF], F32, "dx%d_%d" % (b, s))
+            copy(dx[b, s][:], dx_bank[b, s][:, 0:HALF])
+
+        def scalar_scatter(window, values):
+            nc.scalar.activation(window, values, ACT.Copy)
+
+        def scatter(copy, b, s):
+            copy(windows[b][:].indirect(listed(halves[s])), dx[b, s][:])
+
+        def store(b):
+            queue = nc.sync
+            queue.dma_start(out[b * P:(b + 1) * P, :], windows[b][:])
+
+        on_vector = (nc.vector.tensor_copy, vector_tile)
+        on_scalar = (nc.scalar.copy, scalar_tile)
+
+        gather(0, slice(0, N))
+        windows.append(sb.tile([P, T], F32, name="window3", tag="wide0"))
+        nc.gpsimd.memset(windows[D_TILES - 1][:], 0.0)
+        for j in range(1, PACK - 1):
             gather(j, slice(0, N))
         for ns in halves:
             gather(PACK - 1, ns)
-        quantise_x(0)
-        cast_wd(nc.vector.tensor_copy, vector_tile, 0, 0)
-        cast_wd_shared(0, 1)
+        quantise_x(EARLY)
+        cast_wd(*on_vector, 0, 0)
+        cast_wd_shared(0, 1, WD_SHARE)
         quantise_wd(0, 0)
-        sigmoids(0, 0, 0)
-        quantise_x(1)
+        quantise_x(LATE)
         quantise_wd(0, 1)
-        sigmoids(0, 1, 0)
-        for k in range(2):
-            sigmoids(0, k, 1)
-        for k in range(2):
-            cast_wd(nc.vector.tensor_copy, vector_tile, 1, k)
+        cast_wd(*on_vector, 1, 0)
+        cast_wd_shared(1, 1, 64)
+        for s in range(2):
+            for k in range(2):
+                sigmoids(0, k, s)
         for k in range(2):
             quantise_wd(1, k)
-            sigmoids(1, k, 0)
-            subtract(0, k)
         for k in range(2):
-            sigmoids(1, k, 1)
+            sigmoids(1, k, EARLY)
+        turn(0, LATE, "y", (0, 1), (0, 1))
+        for k in range(2):
+            sigmoids(1, k, LATE)
+        turn(0, LATE, "sig", (0, 1), (0, 1))
+        turn(1, LATE, "y", (0, 1), (0,))
+        turn(1, LATE, "sig", (0, 1), (0,))
+        subtract(0, EARLY, 0, (0, 1))
+        for q in range(BLOCKS):
+            subtract(0, EARLY, 1, (q,))
+        for q in range(BLOCKS):
+            weigh(0, EARLY, q)
+        subtract(1, EARLY, 0, (0, 1))
+        quantise_g(0, EARLY)
+        subtract(1, EARLY, 1, (0, 1))
+        for q in range(BLOCKS):
+            weigh_turned(0, LATE, q)
+        weigh_turned(1, LATE, 0)
+        cast_tile(*on_scalar, 0, 0)
+        cast_tile(*on_scalar, 1, 0)
+        cast_tile(*on_scalar, 0, 1)
+        turn_back(0, LATE, (0, 1))
+        turn_back(1, LATE, (0,))
+        for q in range(BLOCKS):
+            weigh(1, EARLY, q)
+        quantise_tile(0)
+        dx_pass(0, EARLY, 0)
+        quantise_g(1, EARLY)
+        dx_pass(0, EARLY, 1)
+        cast_tile(*on_scalar, 1, 1)
+        cast_tile(*on_scalar, 2, 0)
+        for k in range(2):
+            subtract(1, LATE, k, (1,))
+        quantise_g(0, LATE)
+        dx_pass(0, LATE, 0)
+        weigh(1, LATE, 1)
+        copy_dx(*on_scalar, 0, EARLY)
+        scatter(scalar_scatter, 0, EARLY)
+        quantise_tile(1)
+        quantise_g(1, LATE)
+        dx_pass(0, LATE, 1)
+        dx_product(1, EARLY)
+        dx_product(1, LATE)
+        cast_tile(*on_vector, 2, 1)
         for h in range(V_PASSES):
-            turn(h)
-        weigh(0)
-        subtract(1, 0)
-        quantise_g(0, early)
-        subtract(1, 1)
-        weigh(1)
-        for b in range(EARLY_TILES):
-            for h in range(V_PASSES):
-                cast_wv(b, h, h + 1)
-        weigh_turned(0, 0)
-        quantise_wv(0, 0, 1)
-        early_banks = [bank("dx_bank") for b in range(EARLY_TILES)]
-        dx_pass(early_banks[0], 0, 0, 0)
-        quantise_g(1, early)
-        quantise_wv(0, 1, 2)
-        dx_pass(early_banks[0], 0, 1, 0)
-        weigh_turned(0, 1)
-        quantise_wv(1, 0, 1)
-        dx_pass(early_banks[1], 1, 0, 0)
-        dx0 = copy_dx(early_banks[0], late, "dx_early0")
-        turn_back(0)
-        weigh_turned(1, 0)
-        weigh_turned(1, 1)
-        quantise_wv(1, 1, 2)
-        turn_back(1)
-        dx_pass(early_banks[1], 1, 1, 0)
-        scatter(dx0, 0, early)
-        quantise_g(0, late)
-        quantise_g(1, late)
-        scatter(copy_dx(early_banks[1], late, "dx_early1"), 1, early)
-        final = [dx_product(b) for b in range(EARLY_TILES)]
-        cast_wv(2, 0, V_PASSES)
-        quantise_wv(2, 0, V_PASSES)
-        for b in range(EARLY_TILES):
-            scatter(copy_dx(final[b], late, "dx_late%d" % b), b, late)
-        cast_wv(3, 0, V_PASSES)
-        quantise_wv(3, 0, V_PASSES)
-        for b in range(EARLY_TILES, D_TILES):
-            scatter(copy_dx(dx_product(b), slice(0, N), "dx%d" % b), b, slice(0, N))
+            cast_tile(*on_vector, 3, h)
+        copy_dx(*on_vector, 0, LATE)
+        quantise_tile(2)
+        scatter(nc.vector.tensor_copy, 0, LATE)
+        store(0)
+        copy_dx(*on_scalar, 1, EARLY)
+        dx_product(2, EARLY)
+        dx_product(2, LATE)
+        scatter(scalar_scatter, 1, EARLY)
+        copy_dx(*on_scalar, 2, EARLY)
+        quantise_tile(3)
+        copy_dx(*on_vector, 1, LATE)
+        copy_dx(*on_vector, 2, LATE)
+        scatter(nc.vector.tensor_copy, 1, LATE)
+        store(1)
+        dx_product(3, EARLY)
+        dx_product(3, LATE)
+        scatter(scalar_scatter, 2, EARLY)
+        copy_dx(*on_scalar, 3, EARLY)
+        copy_dx(*on_scalar, 3, LATE)
+        scatter(nc.vector.tensor_copy, 2, LATE)
+        store(2)
+        scatter(scalar_scatter, 3, EARLY)
+        scatter(scalar_scatter, 3, LATE)
+        store(3)

@@ -126,7 +126,7 @@ def tile_attend_gml_nce_kernel(tc, xT, wd, wv, y, cw, rw, offs, out):
                 weight_turned[h, s, q] = scalar_tile([P, 2 * P, 2], F32, "weight_turned%d_%d_%d" % (h, s, q))
                 nc.scalar.activation(weight_turned[h, s, q][:], by_words(along_bank), ACT.Copy, scale=minus_rw[:, BLOCKS * s + q:BLOCKS * s + q + 1])
 
-        windows = [sb.tile([P, T], F32, name="window%d" % b) for b in range(D_TILES - 1)]
+        windows = [sb.tile([P, T], F32, name="window%d" % b) for b in range(D_TILES)]
         for window in windows:
             nc.vector.memset(window[:], 0.0)
 
@@ -263,10 +263,7 @@ def tile_attend_gml_nce_kernel(tc, xT, wd, wv, y, cw, rw, offs, out):
         on_vector = (nc.vector.tensor_copy, vector_tile)
         on_scalar = (nc.scalar.copy, scalar_tile)
 
-        gather(0, slice(0, N))
-        windows.append(sb.tile([P, T], F32, name="window3", tag="wide0"))
-        nc.gpsimd.memset(windows[D_TILES - 1][:], 0.0)
-        for j in range(1, PACK - 1):
+        for j in range(PACK - 1):
             gather(j, slice(0, N))
         for ns in halves:
             gather(PACK - 1, ns)

@@ -325,29 +325,29 @@ def tile_attend_gml_nce_kernel(tc, xT, wd, wv, y, cw, rw, offs, out):
         dx_product(1, EARLY)
         dx_product(1, LATE)
         cast_tile(*on_vector, 2, 1)
-        for h in range(V_PASSES):
-            cast_tile(*on_vector, 3, h)
+        cast_tile(*on_vector, 3, 0)
+        cast_tile(*on_vector, 3, 1)
         copy_dx(*on_vector, 0, LATE)
         quantise_tile(2)
+        quantise_tile(3)
         scatter(nc.vector.tensor_copy, 0, LATE)
         store(0)
         copy_dx(*on_scalar, 1, EARLY)
+        copy_dx(*on_scalar, 1, LATE)
         dx_product(2, EARLY)
         dx_product(2, LATE)
         scatter(scalar_scatter, 1, EARLY)
-        copy_dx(*on_scalar, 2, EARLY)
-        quantise_tile(3)
-        copy_dx(*on_vector, 1, LATE)
-        copy_dx(*on_vector, 2, LATE)
         scatter(nc.vector.tensor_copy, 1, LATE)
         store(1)
+        copy_dx(*on_scalar, 2, EARLY)
+        copy_dx(*on_scalar, 2, LATE)
         dx_product(3, EARLY)
         dx_product(3, LATE)
         scatter(scalar_scatter, 2, EARLY)
-        copy_dx(*on_scalar, 3, EARLY)
-        copy_dx(*on_scalar, 3, LATE)
         scatter(nc.vector.tensor_copy, 2, LATE)
         store(2)
+        copy_dx(*on_scalar, 3, EARLY)
+        copy_dx(*on_scalar, 3, LATE)
         scatter(scalar_scatter, 3, EARLY)
         scatter(scalar_scatter, 3, LATE)
         store(3)

@@ -26,7 +26,7 @@ HALF = N // 2
 BLOCKS = HALF // P
 WD_SHARE = 48
 S_BUFS = 22
-V_BUFS = 20
+V_BUFS = 22
 EARLY, LATE = 0, 1
 DIRECT_BLOCKS = ((0, EARLY, (0, 1)), (1, EARLY, (0, 1)), (1, LATE, (1,)))
 TURNED_BLOCKS = ((0, LATE, (0, 1)), (1, LATE, (0,)))
@@ -72,22 +72,49 @@ def tile_attend_gml_nce_kernel(tc, xT, wd, wv, y, cw, rw, offs, out):
             nc.sync.dma_start(x_planes[j][:], x_rows[j])
         for h in range(V_PASSES):
             nc.sync.dma_start(wd_raw[h][:], wd_rows[:, :, h * PASS:(h + 1) * PASS])
-        for h in range(V_PASSES):
-            for k in range(2):
-                nc.sync.dma_start(y_sb[h, k][:], y_rows[h][:, pairs[k], :])
         wv_raw = {}
-        for b0 in range(0, D_TILES, 2):
-            for h in range(V_PASSES):
-                part = sb.tile([P, PACK, 2 * P], F32, name="wv_raw%d_%d" % (h, b0))
-                nc.sync.dma_start(part[:], wv_rows[h][:, :, b0 * P:(b0 + 2) * P])
-                for b in range(b0, b0 + 2):
-                    wv_raw[h, b] = part[:, :, (b - b0) * P:(b - b0 + 1) * P]
+
+        def load_y(h, k):
+            nc.sync.dma_start(y_sb[h, k][:], y_rows[h][:, pairs[k], :])
+
+        def load_wv(h, b0, b1):
+            part = sb.tile([P, PACK, (b1 - b0) * P], F32, name="wv_raw%d_%d" % (h, b0))
+            nc.sync.dma_start(part[:], wv_rows[h][:, :, b0 * P:b1 * P])
+            for b in range(b0, b1):
+                wv_raw[h, b] = part[:, :, (b - b0) * P:(b - b0 + 1) * P]
+
+        load_y(0, 0)
+        load_y(0, 1)
+        load_y(1, 0)
+        load_y(1, 1)
+        load_wv(0, 0, 1)
+        load_wv(1, 0, 1)
+        load_wv(0, 1, 2)
+        load_wv(1, 1, 2)
+        load_wv(0, 2, 4)
+        load_wv(1, 2, 4)
 
         warm = sb.tile([P, 1], F32, name="warm")
         warm_out = sb.tile([P, 1], F32, name="warm_out")
         nc.vector.memset(warm[:], 0.0)
         nc.scalar.activation(warm_out[:], warm[:], ACT.Sigmoid)
 
+        windows = [sb.tile([P, T], F32, name="window%d" % b) for b in range(D_TILES)]
+        for window in windows:
+            nc.vector.memset(window[:], 0.0)
+
+        x_bf = sb.tile([P, N, PACK], BF16, name="x_bf", align_bytes=64)
+
+        def listed(ns):
+            return offsets[:, ns.start // 16:ns.stop // 16]
+
+        def scalar_copy(dst, src):
+            nc.scalar.activation(dst, src, ACT.Copy)
+
+        def gather(copy, j, ns):
+            copy(x_bf[:, ns, j], x_planes[j][:].indirect(listed(ns)))
+
+        gather(scalar_copy, 0, slice(0, N))
         ident = sb.tile([P, P], F32, name="ident")
         make_identity(nc, ident[:])
         cw_bank = bank("cw_bank")
@@ -104,6 +131,7 @@ def tile_attend_gml_nce_kernel(tc, xT, wd, wv, y, cw, rw, offs, out):
         for q in range(N // P):
             nc.tensor.transpose(spread_bank[:, q * P:(q + 1) * P], minus_rw[:, q:q + 1].to_broadcast([P, P]), ident[:])
         weight = {}
+        gather(scalar_copy, 1, slice(0, N))
         for h, s, qs in DIRECT_BLOCKS:
             both = sb.tile([P, PACK, len(qs) * P], F32, name="weight%d_%d" % (h, s))
             for t in range(PACK):
@@ -117,32 +145,24 @@ def tile_attend_gml_nce_kernel(tc, xT, wd, wv, y, cw, rw, offs, out):
         def by_words(full_bank):
             return full_bank[:].rearrange("p (e k) -> p k e", e=2)
 
-        weight_turned = {}
-        for h in sorted(set(h for h, s, qs in TURNED_BLOCKS)):
-            along_bank = bank("along_bank")
+        along_bank = [bank("along_bank") for h in range(V_PASSES)]
+        for h in range(V_PASSES):
             for t in range(PACK):
-                nc.tensor.transpose(along_bank[:, place(t)], cw_sb[:, h, t:t + 1].to_broadcast([P, P]), ident[:])
-            for s, q in [(s, q) for g, s, qs in TURNED_BLOCKS if g == h for q in qs]:
-                weight_turned[h, s, q] = scalar_tile([P, 2 * P, 2], F32, "weight_turned%d_%d_%d" % (h, s, q))
-                nc.scalar.activation(weight_turned[h, s, q][:], by_words(along_bank), ACT.Copy, scale=minus_rw[:, BLOCKS * s + q:BLOCKS * s + q + 1])
+                nc.tensor.transpose(along_bank[h][:, place(t)], cw_sb[:, h, t:t + 1].to_broadcast([P, P]), ident[:])
+        weight_turned = {}
 
-        windows = [sb.tile([P, T], F32, name="window%d" % b) for b in range(D_TILES)]
-        for window in windows:
-            nc.vector.memset(window[:], 0.0)
+        def build_turned(h, s, q):
+            weight_turned[h, s, q] = scalar_tile([P, 2 * P, 2], F32, "weight_turned%d_%d_%d" % (h, s, q))
+            nc.scalar.activation(weight_turned[h, s, q][:], by_words(along_bank[h]), ACT.Copy, scale=minus_rw[:, BLOCKS * s + q:BLOCKS * s + q + 1])
 
-        x_bf = sb.tile([P, N, PACK], BF16, name="x_bf", align_bytes=64)
+        build_turned(1, LATE, 0)
+
         x_scales = [sb.tile([P, HALF], U8, name="x_scales%d" % s, align_bytes=64) for s in range(2)]
         wd_scales = {(h, k): sb.tile([P, 2, P], U8, name="wd_scales%d_%d" % (h, k), align_bytes=64) for h in range(V_PASSES) for k in range(2)}
         wv_scales = {(b, h): sb.tile([P, V_PASSES, P], U8, name="wv_scales%d_%d" % (b, h), align_bytes=64) for b in range(D_TILES) for h in range(V_PASSES)}
         g_scales = {(h, s): sb.tile([P, HALF], U8, name="g_scales%d_%d" % (h, s), align_bytes=64) for h in range(V_PASSES) for s in range(2)}
         x_codes, wd_bf, wd_codes, sig, unused, g_bf, sums, g_turned, g_words, g_codes = {}, {}, {}, {}, {}, {}, {}, {}, {}, {}
         wv_bf, wv_codes, wv_scale, dx_bank, dx, turned = {}, {}, {}, {}, {}, {}
-
-        def listed(ns):
-            return offsets[:, ns.start // 16:ns.stop // 16]
-
-        def gather(j, ns):
-            nc.vector.tensor_copy(x_bf[:, ns, j], x_planes[j][:].indirect(listed(ns)))
 
         def quantise_x(s):
             x_codes[s] = vector_tile([P, HALF], U32, "x_codes%d" % s)
@@ -172,15 +192,24 @@ def tile_attend_gml_nce_kernel(tc, xT, wd, wv, y, cw, rw, offs, out):
                 nc.tensor.matmul_mx(out=a_bank[:, e * HALF:(e + 1) * HALF], lhsT=wd_codes[h, k][:, e, :].bitcast(E4M3),
                                     lhsT_scale=wd_scales[h, k][:, e, :], rhs=x_codes[s][:].bitcast(E4M3), rhs_scale=x_scales[s][:],
                                     start=True, stop=True)
-            sig[h, k, s] = scalar_tile([P, 2, HALF], F32, "sig%d_%d_%d" % (h, k, s))
-            nc.scalar.activation(sig[h, k, s][:].rearrange("p e n -> p (e n)"), a_bank[:], ACT.Sigmoid, scale=-1.0)
+            if (h, k, s) == (1, 0, EARLY):
+                sig[h, k, s] = diff[h, s][:, pairs[1], :]
+            else:
+                sig[h, k, s] = scalar_tile([P, 2, HALF], F32, "sig%d_%d_%d" % (h, k, s))
+            nc.scalar.activation(sig[h, k, s][:].rearrange("p e n -> p (e n)"), a_bank[:], ACT.Sigmoid, scale=1.0 if (h, k, s) == (1, 1, EARLY) else -1.0)
 
-        diff = {(h, s): sb.tile([P, PACK, HALF], F32, name="diff%d_%d" % (h, s)) for h, s, qs in DIRECT_BLOCKS}
+        diff = {(h, EARLY): sb.tile([P, PACK, HALF], F32, name="diff%d" % h) for h in range(V_PASSES)}
 
         def subtract(h, s, k, qs):
             ns = slice(qs[0] * P, (qs[-1] + 1) * P)
-            nc.vector.scalar_tensor_tensor(diff[h, s][:, pairs[k], ns], y_sb[h, k][:, :, s * HALF + ns.start:s * HALF + ns.stop], -1.0,
+            if (h, s) not in diff:
+                diff[h, s] = vector_tile([P, PACK, P], F32, "diff_last")
+            dst = diff[h, s][:, pairs[k], ns] if s == EARLY else diff[h, s][:, pairs[k], :]
+            nc.vector.scalar_tensor_tensor(dst, y_sb[h, k][:, :, s * HALF + ns.start:s * HALF + ns.stop], -1.0,
                                            sig[h, k, s][:, :, ns], ALU.add, ALU.add)
+
+        def side_subtract(h, s, k):
+            nc.gpsimd.tensor_tensor(diff[h, s][:, pairs[k], :], y_sb[h, k][:, :, halves[s]], sig[h, k, s][:], ALU.subtract)
 
         def values_tile(new_tile, h, s):
             if (h, s) not in g_bf:
@@ -190,7 +219,7 @@ def tile_attend_gml_nce_kernel(tc, xT, wd, wv, y, cw, rw, offs, out):
         def weigh(h, s, q):
             ns = slice(q * P, (q + 1) * P)
             nc.vector.tensor_tensor(values_tile(vector_tile, h, s)[:, ns].rearrange("p (c i) t -> p c t i", i=2),
-                                    diff[h, s][:, :, ns].rearrange("p t (c i) -> p c t i", i=2),
+                                    (diff[h, s][:, :, ns] if s == EARLY else diff[h, s][:]).rearrange("p t (c i) -> p c t i", i=2),
                                     weight[h, s, q].rearrange("p t (c i) -> p c t i", i=2), ALU.mult)
 
         def cast_tile(copy, new_tile, b, h):
@@ -263,13 +292,15 @@ def tile_attend_gml_nce_kernel(tc, xT, wd, wv, y, cw, rw, offs, out):
         on_vector = (nc.vector.tensor_copy, vector_tile)
         on_scalar = (nc.scalar.copy, scalar_tile)
 
-        for j in range(PACK - 1):
-            gather(j, slice(0, N))
+
+        gather(nc.vector.tensor_copy, 2, slice(0, N))
         for ns in halves:
-            gather(PACK - 1, ns)
+            gather(nc.vector.tensor_copy, 3, ns)
         quantise_x(EARLY)
         cast_wd(*on_vector, 0, 0)
         cast_wd_shared(0, 1, WD_SHARE)
+        for q in range(BLOCKS):
+            build_turned(0, LATE, q)
         quantise_wd(0, 0)
         quantise_x(LATE)
         quantise_wd(0, 1)
@@ -280,12 +311,14 @@ def tile_attend_gml_nce_kernel(tc, xT, wd, wv, y, cw, rw, offs, out):
                 sigmoids(0, k, s)
         for k in range(2):
             quantise_wd(1, k)
+        turn(0, LATE, "y", (0,), (0, 1))
         for k in range(2):
             sigmoids(1, k, EARLY)
-        turn(0, LATE, "y", (0, 1), (0, 1))
+        turn(0, LATE, "y", (1,), (0, 1))
+        turn(0, LATE, "sig", (0, 1), (0,))
         for k in range(2):
             sigmoids(1, k, LATE)
-        turn(0, LATE, "sig", (0, 1), (0, 1))
+        turn(0, LATE, "sig", (0, 1), (1,))
         turn(1, LATE, "y", (0, 1), (0,))
         turn(1, LATE, "sig", (0, 1), (0,))
         subtract(0, EARLY, 0, (0, 1))
@@ -295,13 +328,13 @@ def tile_attend_gml_nce_kernel(tc, xT, wd, wv, y, cw, rw, offs, out):
             weigh(0, EARLY, q)
         subtract(1, EARLY, 0, (0, 1))
         quantise_g(0, EARLY)
-        subtract(1, EARLY, 1, (0, 1))
+        side_subtract(1, EARLY, 1)
         for q in range(BLOCKS):
             weigh_turned(0, LATE, q)
         weigh_turned(1, LATE, 0)
         cast_tile(*on_scalar, 0, 0)
-        cast_tile(*on_scalar, 1, 0)
         cast_tile(*on_scalar, 0, 1)
+        cast_tile(*on_scalar, 1, 0)
         turn_back(0, LATE, (0, 1))
         turn_back(1, LATE, (0,))
         for q in range(BLOCKS):
@@ -324,8 +357,8 @@ def tile_attend_gml_nce_kernel(tc, xT, wd, wv, y, cw, rw, offs, out):
         dx_pass(0, LATE, 1)
         dx_product(1, EARLY)
         dx_product(1, LATE)
-        cast_tile(*on_vector, 2, 1)
         cast_tile(*on_vector, 3, 0)
+        cast_tile(*on_vector, 2, 1)
         cast_tile(*on_vector, 3, 1)
         copy_dx(*on_vector, 0, LATE)
         quantise_tile(2)

@@ -38,6 +38,7 @@ def tile_attend_gml_nce_kernel(tc, xT, wd, wv, y, cw, rw, offs, out):
         sb = ctx.enter_context(tc.tile_pool(name="sb", bufs=1))
         sline = ctx.enter_context(tc.tile_pool(name="sline", bufs=S_BUFS))
         vline = ctx.enter_context(tc.tile_pool(name="vline", bufs=V_BUFS))
+        far = ctx.enter_context(tc.tile_pool(name="far", bufs=1))
         psum = ctx.enter_context(tc.psum_pool(name="psum", bufs=8))
 
         def bank(name):
@@ -53,8 +54,10 @@ def tile_attend_gml_nce_kernel(tc, xT, wd, wv, y, cw, rw, offs, out):
         pairs = [slice(0, 2), slice(2, 4)]
 
         offsets = sb.tile([P, N // 16], U16, name="offsets")
+        windows = [sb.tile([P, T], F32, name="window0")]
         x_planes = [sb.tile([P, T], F32, name="x_plane%d" % j, tag="wide%d" % j) for j in range(PACK)]
         wd_raw = [sb.tile([P, PACK, PASS], F32, name="wd_raw%d" % h) for h in range(V_PASSES)]
+        windows.append(sb.tile([P, T], F32, name="window1"))
         y_sb = {(h, k): sb.tile([P, 2, N], F32, name="y_sb%d_%d" % (h, k)) for h in range(V_PASSES) for k in range(2)}
         rows = sb.tile([P, PASS], F32, name="rows")
         nc.vector.memset(rows[:], 0.0)
@@ -87,10 +90,8 @@ def tile_attend_gml_nce_kernel(tc, xT, wd, wv, y, cw, rw, offs, out):
         load_y(0, 1)
         load_y(1, 0)
         load_y(1, 1)
-        load_wv(0, 0, 1)
-        load_wv(1, 0, 1)
-        load_wv(0, 1, 2)
-        load_wv(1, 1, 2)
+        load_wv(0, 0, 2)
+        load_wv(1, 0, 2)
         load_wv(0, 2, 4)
         load_wv(1, 2, 4)
 
@@ -99,7 +100,8 @@ def tile_attend_gml_nce_kernel(tc, xT, wd, wv, y, cw, rw, offs, out):
         nc.vector.memset(warm[:], 0.0)
         nc.scalar.activation(warm_out[:], warm[:], ACT.Sigmoid)
 
-        windows = [sb.tile([P, T], F32, name="window%d" % b) for b in range(D_TILES)]
+        windows.append(sb.tile([P, T], F32, name="window2"))
+        windows.append(far.tile([P, T], F32, name="window3"))
         for window in windows:
             nc.vector.memset(window[:], 0.0)
 
@@ -333,20 +335,20 @@ def tile_attend_gml_nce_kernel(tc, xT, wd, wv, y, cw, rw, offs, out):
             weigh_turned(0, LATE, q)
         weigh_turned(1, LATE, 0)
         cast_tile(*on_scalar, 0, 0)
-        cast_tile(*on_scalar, 0, 1)
         cast_tile(*on_scalar, 1, 0)
+        cast_tile(*on_scalar, 0, 1)
         turn_back(0, LATE, (0, 1))
         turn_back(1, LATE, (0,))
         for q in range(BLOCKS):
             weigh(1, EARLY, q)
+        for k in range(2):
+            subtract(1, LATE, k, (1,))
         quantise_tile(0)
         dx_pass(0, EARLY, 0)
         quantise_g(1, EARLY)
         dx_pass(0, EARLY, 1)
         cast_tile(*on_scalar, 1, 1)
         cast_tile(*on_scalar, 2, 0)
-        for k in range(2):
-            subtract(1, LATE, k, (1,))
         quantise_g(0, LATE)
         dx_pass(0, LATE, 0)
         weigh(1, LATE, 1)
@@ -357,8 +359,8 @@ def tile_attend_gml_nce_kernel(tc, xT, wd, wv, y, cw, rw, offs, out):
         dx_pass(0, LATE, 1)
         dx_product(1, EARLY)
         dx_product(1, LATE)
-        cast_tile(*on_vector, 3, 0)
         cast_tile(*on_vector, 2, 1)
+        cast_tile(*on_vector, 3, 0)
         cast_tile(*on_vector, 3, 1)
         copy_dx(*on_vector, 0, LATE)
         quantise_tile(2)

@@ -359,11 +359,11 @@ def tile_attend_gml_nce_kernel(tc, xT, wd, wv, y, cw, rw, offs, out):
         dx_pass(0, LATE, 1)
         dx_product(1, EARLY)
         dx_product(1, LATE)
-        cast_tile(*on_vector, 2, 1)
         cast_tile(*on_vector, 3, 0)
+        cast_tile(*on_vector, 2, 1)
         cast_tile(*on_vector, 3, 1)
-        copy_dx(*on_vector, 0, LATE)
         quantise_tile(2)
+        copy_dx(*on_vector, 0, LATE)
         quantise_tile(3)
         scatter(nc.vector.tensor_copy, 0, LATE)
         store(0)

from contextlib import ExitStack

import concourse.mybir as mybir
from concourse.masks import make_identity

N, T, D, V = 512, 2048, 512, 1024
FLOPS = 2 * 2 * N * D * V

F32 = mybir.dt.float32
BF16 = mybir.dt.bfloat16
U32 = mybir.dt.uint32
U16 = mybir.dt.uint16
U8 = mybir.dt.uint8
E4M3 = mybir.dt.float8_e4m3fn_x4
E5M2 = mybir.dt.float8_e5m2_x4
ACT = mybir.ActivationFunctionType
ALU = mybir.AluOpType

P = 128
PACK = 4
PASS = P * PACK
V_PASSES = V // PASS
D_TILES = D // P
LINE = 4
HALF = N // 2
BLOCKS = HALF // P
WD_SHARE = 48
S_BUFS = 22
V_BUFS = 22
EARLY, LATE = 0, 1
DIRECT_BLOCKS = ((0, EARLY, (0, 1)), (1, EARLY, (0, 1)), (1, LATE, (1,)))
TURNED_BLOCKS = ((0, LATE, (0, 1)), (1, LATE, (0,)))


def tile_attend_gml_nce_kernel(tc, xT, wd, wv, y, cw, rw, offs, out):
    nc = tc.nc
    with ExitStack() as ctx:
        sb = ctx.enter_context(tc.tile_pool(name="sb", bufs=1))
        sline = ctx.enter_context(tc.tile_pool(name="sline", bufs=S_BUFS))
        vline = ctx.enter_context(tc.tile_pool(name="vline", bufs=V_BUFS))
        far = ctx.enter_context(tc.tile_pool(name="far", bufs=1))
        psum = ctx.enter_context(tc.psum_pool(name="psum", bufs=8))

        def bank(name):
            return psum.tile([P, N], F32, name=name, tag="bank")

        def scalar_tile(shape, dtype, name):
            return sline.tile(shape, dtype, name=name, tag="sline", align_bytes=64)

        def vector_tile(shape, dtype, name):
            return vline.tile(shape, dtype, name=name, tag="vline", align_bytes=64)

        halves = [slice(0, HALF), slice(HALF, N)]
        pairs = [slice(0, 2), slice(2, 4)]

        offsets = sb.tile([P, N // 16], U16, name="offsets")
        windows = [sb.tile([P, T], F32, name="window0")]
        x_planes = [sb.tile([P, T], F32, name="x_plane%d" % j, tag="wide%d" % j) for j in range(PACK)]
        wd_raw = [sb.tile([P, PACK, PASS], F32, name="wd_raw%d" % h) for h in range(V_PASSES)]
        windows.append(sb.tile([P, T], F32, name="window1"))
        y_sb = {(h, k): sb.tile([P, 2, N], F32, name="y_sb%d_%d" % (h, k)) for h in range(V_PASSES) for k in range(2)}
        rows = sb.tile([P, PASS], F32, name="rows")
        nc.vector.memset(rows[:], 0.0)

        x_rows = xT.rearrange("(p j) n -> j p n", j=PACK)
        wd_rows = wd.rearrange("(p j) v -> p j v", j=PACK)
        wv_rows = wv.rearrange("(h p j) d -> h p j d", p=P, j=PACK)
        y_rows = y.rearrange("(h p j) n -> h p j n", p=P, j=PACK)

        nc.sync.dma_start(x_planes[0][:], x_rows[0])
        nc.sync.dma_start(offsets[:], offs)
        nc.sync.dma_start(rows[0:V_PASSES, :], cw.rearrange("(h v) o -> h (v o)", h=V_PASSES))
        nc.sync.dma_start(rows[V_PASSES:V_PASSES + 1, :], rw[0:1, :])
        for j in range(1, PACK):
            nc.sync.dma_start(x_planes[j][:], x_rows[j])
        for h in range(V_PASSES):
            nc.sync.dma_start(wd_raw[h][:], wd_rows[:, :, h * PASS:(h + 1) * PASS])
        wv_raw = {}

        def load_y(h, k):
            nc.sync.dma_start(y_sb[h, k][:], y_rows[h][:, pairs[k], :])

        def load_wv(h, b0, b1):
            part = sb.tile([P, PACK, (b1 - b0) * P], F32, name="wv_raw%d_%d" % (h, b0))
            nc.sync.dma_start(part[:], wv_rows[h][:, :, b0 * P:b1 * P])
            for b in range(b0, b1):
                wv_raw[h, b] = part[:, :, (b - b0) * P:(b - b0 + 1) * P]

        load_y(0, 0)
        load_y(0, 1)
        load_y(1, 0)
        load_y(1, 1)
        load_wv(0, 0, 2)
        load_wv(1, 0, 2)
        load_wv(0, 2, 4)
        load_wv(1, 2, 4)

        warm = sb.tile([P, 1], F32, name="warm")
        warm_out = sb.tile([P, 1], F32, name="warm_out")
        nc.vector.memset(warm[:], 0.0)
        nc.scalar.activation(warm_out[:], warm[:], ACT.Sigmoid)

        windows.append(sb.tile([P, T], F32, name="window2"))
        windows.append(far.tile([P, T], F32, name="window3"))
        for window in windows:
            nc.vector.memset(window[:], 0.0)

        x_bf = sb.tile([P, N, PACK], BF16, name="x_bf", align_bytes=64)

        def listed(ns):
            return offsets[:, ns.start // 16:ns.stop // 16]

        def scalar_copy(dst, src):
            nc.scalar.activation(dst, src, ACT.Copy)

        def gather(copy, j, ns):
            copy(x_bf[:, ns, j], x_planes[j][:].indirect(listed(ns)))

        gather(scalar_copy, 0, slice(0, N))
        ident = sb.tile([P, P], F32, name="ident")
        make_identity(nc, ident[:])
        cw_bank = bank("cw_bank")
        for t in range(PACK):
            nc.tensor.transpose(cw_bank[:, t * P:(t + 1) * P], rows[:, t:PASS:PACK], ident[:])
        cw_sb = sb.tile([P, V_PASSES, PACK], F32, name="cw_sb")
        nc.scalar.copy(cw_sb[:], cw_bank[:].rearrange("p (t r) -> p r t", t=PACK)[:, 0:V_PASSES, :])
        rw_bank = bank("rw_bank")
        for q in range(N // P):
            nc.tensor.transpose(rw_bank[:, q * P:(q + 1) * P], rows[:, q * P:(q + 1) * P], ident[:])
        minus_rw = sb.tile([P, N // P], F32, name="minus_rw")
        nc.scalar.activation(minus_rw[:], rw_bank[:, V_PASSES:N:P], ACT.Copy, scale=-1.0)
        spread_bank = bank("spread_bank")
        for q in range(N // P):
            nc.tensor.transpose(spread_bank[:, q * P:(q + 1) * P], minus_rw[:, q:q + 1].to_broadcast([P, P]), ident[:])
        weight = {}
        gather(scalar_copy, 1, slice(0, N))
        for h, s, qs in DIRECT_BLOCKS:
            both = sb.tile([P, PACK, len(qs) * P], F32, name="weight%d_%d" % (h, s))
            for t in range(PACK):
                nc.scalar.activation(both[:, t, :], spread_bank[:, s * HALF + qs[0] * P:s * HALF + (qs[-1] + 1) * P], ACT.Copy, scale=cw_sb[:, h, t:t + 1])
            for n, q in enumerate(qs):
                weight[h, s, q] = both[:, :, n * P:(n + 1) * P]

        def place(t):
            return slice((t % 2 * 2 + t // 2) * P, (t % 2 * 2 + t // 2 + 1) * P)

        def by_words(full_bank):
            return full_bank[:].rearrange("p (e k) -> p k e", e=2)

        along_bank = [bank("along_bank") for h in range(V_PASSES)]
        for h in range(V_PASSES):
            for t in range(PACK):
                nc.tensor.transpose(along_bank[h][:, place(t)], cw_sb[:, h, t:t + 1].to_broadcast([P, P]), ident[:])
        weight_turned = {}

        def build_turned(h, s, q):
            weight_turned[h, s, q] = scalar_tile([P, 2 * P, 2], F32, "weight_turned%d_%d_%d" % (h, s, q))
            nc.scalar.activation(weight_turned[h, s, q][:], by_words(along_bank[h]), ACT.Copy, scale=minus_rw[:, BLOCKS * s + q:BLOCKS * s + q + 1])

        build_turned(1, LATE, 0)

        x_scales = [sb.tile([P, HALF], U8, name="x_scales%d" % s, align_bytes=64) for s in range(2)]
        wd_scales = {(h, k): sb.tile([P, 2, P], U8, name="wd_scales%d_%d" % (h, k), align_bytes=64) for h in range(V_PASSES) for k in range(2)}
        wv_scales = {(b, h): sb.tile([P, V_PASSES, P], U8, name="wv_scales%d_%d" % (b, h), align_bytes=64) for b in range(D_TILES) for h in range(V_PASSES)}
        g_scales = {(h, s): sb.tile([P, HALF], U8, name="g_scales%d_%d" % (h, s), align_bytes=64) for h in range(V_PASSES) for s in range(2)}
        x_codes, wd_bf, wd_codes, sig, unused, g_bf, sums, g_turned, g_words, g_codes = {}, {}, {}, {}, {}, {}, {}, {}, {}, {}
        wv_bf, wv_codes, wv_scale, dx_bank, dx, turned = {}, {}, {}, {}, {}, {}

        def quantise_x(s):
            x_codes[s] = vector_tile([P, HALF], U32, "x_codes%d" % s)
            nc.vector.quantize_mx(out=x_codes[s][:].bitcast(E4M3), scales=x_scales[s][:],
                                  in_=x_bf[:, halves[s]].rearrange("p n j -> p (n j)"))

        def cast_wd(copy, new_tile, h, k):
            wd_bf[h, k] = new_tile([P, 2, P, PACK], BF16, "wd_bf%d_%d" % (h, k))
            src = wd_raw[h][:].rearrange("p j (m t) -> p m j t", t=PACK)
            copy(wd_bf[h, k][:].rearrange("p e m j -> p m j e"), src[:, :, :, pairs[k]])

        def cast_wd_shared(h, k, share):
            wd_bf[h, k] = scalar_tile([P, 2, P, PACK], BF16, "wd_bf%d_%d" % (h, k))
            src = wd_raw[h][:].rearrange("p j (m t) -> p m j t", t=PACK)
            for copy, ms in ((nc.scalar.copy, slice(share, P)), (nc.vector.tensor_copy, slice(0, share))):
                copy(wd_bf[h, k][:].rearrange("p e m j -> p m j e")[:, ms], src[:, ms, :, pairs[k]])

        def quantise_wd(h, k):
            wd_codes[h, k] = vector_tile([P, 2, P], U32, "wd_codes%d_%d" % (h, k))
            nc.vector.quantize_mx(out=wd_codes[h, k][:].rearrange("p e m -> p (e m)").bitcast(E4M3),
                                  scales=wd_scales[h, k][:].rearrange("p e m -> p (e m)"),
                                  in_=wd_bf[h, k][:].rearrange("p e m j -> p (e m j)"))

        def sigmoids(h, k, s):
            a_bank = bank("a_bank")
            for e in range(2):
                nc.tensor.matmul_mx(out=a_bank[:, e * HALF:(e + 1) * HALF], lhsT=wd_codes[h, k][:, e, :].bitcast(E4M3),
                                    lhsT_scale=wd_scales[h, k][:, e, :], rhs=x_codes[s][:].bitcast(E4M3), rhs_scale=x_scales[s][:],
                                    start=True, stop=True)
            if (h, k, s) == (1, 0, EARLY):
                sig[h, k, s] = diff[h, s][:, pairs[1], :]
            else:
                sig[h, k, s] = scalar_tile([P, 2, HALF], F32, "sig%d_%d_%d" % (h, k, s))
            nc.scalar.activation(sig[h, k, s][:].rearrange("p e n -> p (e n)"), a_bank[:], ACT.Sigmoid, scale=1.0 if (h, k, s) == (1, 1, EARLY) else -1.0)

        diff = {(h, EARLY): sb.tile([P, PACK, HALF], F32, name="diff%d" % h) for h in range(V_PASSES)}

        def subtract(h, s, k, qs):
            ns = slice(qs[0] * P, (qs[-1] + 1) * P)
            if (h, s) not in diff:
                diff[h, s] = vector_tile([P, PACK, P], F32, "diff_last")
            dst = diff[h, s][:, pairs[k], ns] if s == EARLY else diff[h, s][:, pairs[k], :]
            nc.vector.scalar_tensor_tensor(dst, y_sb[h, k][:, :, s * HALF + ns.start:s * HALF + ns.stop], -1.0,
                                           sig[h, k, s][:, :, ns], ALU.add, ALU.add)

        def side_subtract(h, s, k):
            nc.gpsimd.tensor_tensor(diff[h, s][:, pairs[k], :], y_sb[h, k][:, :, halves[s]], sig[h, k, s][:], ALU.subtract)

        def values_tile(new_tile, h, s):
            if (h, s) not in g_bf:
                g_bf[h, s] = new_tile([P, HALF, PACK], BF16, "g_bf%d_%d" % (h, s))
            return g_bf[h, s]

        def weigh(h, s, q):
            ns = slice(q * P, (q + 1) * P)
            nc.vector.tensor_tensor(values_tile(vector_tile, h, s)[:, ns].rearrange("p (c i) t -> p c t i", i=2),
                                    (diff[h, s][:, :, ns] if s == EARLY else diff[h, s][:]).rearrange("p t (c i) -> p c t i", i=2),
                                    weight[h, s, q].rearrange("p t (c i) -> p c t i", i=2), ALU.mult)

        def cast_tile(copy, new_tile, b, h):
            if h == 0:
                wv_bf[b] = new_tile([P, V_PASSES, P, PACK], BF16, "wv_bf%d" % b)
            copy(wv_bf[b][:, h].rearrange("p (c i) j -> p c j i", i=LINE), wv_raw[h, b].rearrange("p j (c i) -> p c j i", i=LINE))

        def quantise_tile(b):
            codes = vector_tile([P, V_PASSES, P], U32, "wv_codes%d" % b)
            scales = wv_scales[b, 0]
            for h in range(V_PASSES):
                wv_codes[b, h] = codes[:, h, :]
                wv_scale[b, h] = scales[:, h, :]
            nc.vector.quantize_mx(out=codes[:].rearrange("p h m -> p (h m)").bitcast(E4M3), scales=scales[:].rearrange("p h m -> p (h m)"),
                                  in_=wv_bf[b][:].rearrange("p h m j -> p (h m j)"))

        def turn(h, s, what, ks, qs):
            for k in ks:
                for t in range(2 * k, 2 * k + 2):
                    for q in qs:
                        if (h, s, q) not in sums:
                            sums[h, s, q] = bank("sum_bank")
                        turned[h, s, q] = turned.get((h, s, q), 0) + 1
                        src = y_sb[h, k][:, t % 2, s * HALF + q * P:s * HALF + (q + 1) * P] if what == "y" else sig[h, k, s][:, t % 2, q * P:(q + 1) * P]
                        nc.tensor.matmul(sums[h, s, q][:, place(t)], lhsT=src, rhs=ident[:], is_transpose=True,
                                         start=turned[h, s, q] == 1, stop=turned[h, s, q] == 2 * PACK)

        def weigh_turned(h, s, q):
            g_turned[h, s, q] = vector_tile([P, 2 * P, 2], BF16, "g_turned%d_%d_%d" % (h, s, q))
            nc.vector.scalar_tensor_tensor(g_turned[h, s, q][:], by_words(sums[h, s, q]), -1.0, weight_turned[h, s, q][:], ALU.add, ALU.mult)

        def turn_back(h, s, qs):
            word_bank = bank("word_bank")
            for n, q in enumerate(qs):
                words = g_turned[h, s, q][:].rearrange("p k e -> p (k e)").bitcast(F32)
                for u in range(2):
                    nc.tensor.transpose(word_bank[:, (2 * n + u) * P:(2 * n + u + 1) * P], words[:, u * P:(u + 1) * P], ident[:])
            dst = values_tile(scalar_tile, h, s)[:, qs[0] * P:(qs[-1] + 1) * P].rearrange("p n t -> p (n t)").bitcast(F32)
            nc.scalar.copy(dst.rearrange("p (q i u) -> p q i u", q=len(qs), u=2),
                           word_bank[:, 0:len(qs) * 2 * P].rearrange("p (q u i) -> p q i u", q=len(qs), u=2))

        def quantise_g(h, s):
            g_codes[h, s] = vector_tile([P, HALF], U32, "g_codes%d_%d" % (h, s))
            nc.vector.quantize_mx(out=g_codes[h, s][:].bitcast(E5M2), scales=g_scales[h, s][:], in_=g_bf[h, s][:].rearrange("p n t -> p (n t)"))

        def dx_pass(b, s, h):
            if h == 0:
                dx_bank[b, s] = bank("dx_bank")
            nc.tensor.matmul_mx(out=dx_bank[b, s][:, 0:HALF], lhsT=wv_codes[b, h].bitcast(E4M3), lhsT_scale=wv_scale[b, h],
                                rhs=g_codes[h, s][:].bitcast(E5M2), rhs_scale=g_scales[h, s][:], start=h == 0, stop=h == V_PASSES - 1)

        def dx_product(b, s):
            for h in range(V_PASSES):
                dx_pass(b, s, h)

        def copy_dx(copy, new_tile, b, s):
            dx[b, s] = new_tile([P, HALF], F32, "dx%d_%d" % (b, s))
            copy(dx[b, s][:], dx_bank[b, s][:, 0:HALF])

        def scalar_scatter(window, values):
            nc.scalar.activation(window, values, ACT.Copy)

        def scatter(copy, b, s):
            copy(windows[b][:].indirect(listed(halves[s])), dx[b, s][:])

        def store(b):
            queue = nc.sync
            queue.dma_start(out[b * P:(b + 1) * P, :], windows[b][:])

        on_vector = (nc.vector.tensor_copy, vector_tile)
        on_scalar = (nc.scalar.copy, scalar_tile)


        gather(nc.vector.tensor_copy, 2, slice(0, N))
        for ns in halves:
            gather(nc.vector.tensor_copy, 3, ns)
        quantise_x(EARLY)
        cast_wd(*on_vector, 0, 0)
        cast_wd_shared(0, 1, WD_SHARE)
        for q in range(BLOCKS):
            build_turned(0, LATE, q)
        quantise_wd(0, 0)
        quantise_x(LATE)
        quantise_wd(0, 1)
        cast_wd(*on_vector, 1, 0)
        cast_wd_shared(1, 1, 64)
        for s in range(2):
            for k in range(2):
                sigmoids(0, k, s)
        for k in range(2):
            quantise_wd(1, k)
        turn(0, LATE, "y", (0,), (0, 1))
        for k in range(2):
            sigmoids(1, k, EARLY)
        turn(0, LATE, "y", (1,), (0, 1))
        turn(0, LATE, "sig", (0, 1), (0,))
        for k in range(2):
            sigmoids(1, k, LATE)
        turn(0, LATE, "sig", (0, 1), (1,))
        turn(1, LATE, "y", (0, 1), (0,))
        turn(1, LATE, "sig", (0, 1), (0,))
        subtract(0, EARLY, 0, (0, 1))
        for q in range(BLOCKS):
            subtract(0, EARLY, 1, (q,))
        for q in range(BLOCKS):
            weigh(0, EARLY, q)
        subtract(1, EARLY, 0, (0, 1))
        quantise_g(0, EARLY)
        side_subtract(1, EARLY, 1)
        for q in range(BLOCKS):
            weigh_turned(0, LATE, q)
        weigh_turned(1, LATE, 0)
        cast_tile(*on_scalar, 0, 0)
        cast_tile(*on_scalar, 1, 0)
        cast_tile(*on_scalar, 0, 1)
        turn_back(0, LATE, (0, 1))
        turn_back(1, LATE, (0,))
        for q in range(BLOCKS):
            weigh(1, EARLY, q)
        for k in range(2):
            subtract(1, LATE, k, (1,))
        quantise_tile(0)
        dx_pass(0, EARLY, 0)
        quantise_g(1, EARLY)
        dx_pass(0, EARLY, 1)
        cast_tile(*on_scalar, 1, 1)
        cast_tile(*on_scalar, 2, 0)
        quantise_g(0, LATE)
        dx_pass(0, LATE, 0)
        weigh(1, LATE, 1)
        copy_dx(*on_scalar, 0, EARLY)
        scatter(scalar_scatter, 0, EARLY)
        quantise_tile(1)
        quantise_g(1, LATE)
        dx_pass(0, LATE, 1)
        dx_product(1, EARLY)
        dx_product(1, LATE)
        cast_tile(*on_vector, 3, 0)
        cast_tile(*on_vector, 2, 1)
        cast_tile(*on_vector, 3, 1)
        quantise_tile(2)
        copy_dx(*on_vector, 0, LATE)
        quantise_tile(3)
        scatter(nc.vector.tensor_copy, 0, LATE)
        store(0)
        copy_dx(*on_scalar, 1, EARLY)
        copy_dx(*on_scalar, 1, LATE)
        dx_product(2, EARLY)
        dx_product(2, LATE)
        scatter(scalar_scatter, 1, EARLY)
        scatter(nc.vector.tensor_copy, 1, LATE)
        store(1)
        copy_dx(*on_scalar, 2, EARLY)
        copy_dx(*on_scalar, 2, LATE)
        dx_product(3, EARLY)
        dx_product(3, LATE)
        scatter(scalar_scatter, 2, EARLY)
        scatter(nc.vector.tensor_copy, 2, LATE)
        store(2)
        copy_dx(*on_scalar, 3, EARLY)
        copy_dx(*on_scalar, 3, LATE)
        scatter(scalar_scatter, 3, EARLY)
        scatter(scalar_scatter, 3, LATE)
        store(3)
